import numpy as np
import ml_dtypes


def mxq(x, axis, fmt="e4m3"):
    dtype, down = {"e4m3": (ml_dtypes.float8_e4m3fn, 7), "e5m2": (ml_dtypes.float8_e5m2, 14)}[fmt]
    v = np.moveaxis(np.asarray(x, np.float32).astype(ml_dtypes.bfloat16).astype(np.float64), axis, -1)
    blocks = v.reshape(v.shape[:-1] + (-1, 32))
    amax = np.abs(blocks).max(-1, keepdims=True)
    byte = np.maximum(np.where(amax > 0, np.frexp(amax)[1] - 1 + 127, 0) - down, 1)
    scale = np.exp2(byte - 127.0)
    codes = (blocks / scale).astype(np.float32).astype(dtype).astype(np.float64)
    return np.moveaxis((codes * scale).reshape(v.shape), -1, axis)


WIDE = False


def mx_kscale(k):
    if not WIDE:
        return np.ones(k)
    levels = np.array([10, -10, 5, -5, 0])
    if k % 512:
        return np.exp2(np.random.permutation(np.resize(levels, k // 32))).repeat(32)
    a = np.empty((k // 512, 16))
    for p in range(k // 512):
        a[p, :8] = np.random.permutation(np.resize(levels, 8))
        for g in range(8):
            far = levels[np.abs(levels - a[p, g]) >= 10]
            a[p, g + 8] = far[np.random.randint(len(far))]
    return np.exp2(a.ravel()).repeat(32)


def f64(x):
    return np.asarray(x).astype(np.float64)


def striped(idx):
    return np.tile(idx.reshape(-1, 16).T, (8, 1)).astype(np.uint16)


def unstriped(offs):
    return offs[:16].T.reshape(-1).astype(np.int64)


E2M1 = np.array([0.0, 0.5, 1.0, 1.5, 2.0, 3.0, 4.0, 6.0, -0.0, -0.5, -1.0, -1.5, -2.0, -3.0, -4.0, -6.0])


def pack_weight(w, fmt):
    k, n = w.shape
    w = f64(np.asarray(w, np.float32).astype(ml_dtypes.bfloat16)).reshape(k // 32, 32, n)
    amax = np.abs(w).max(1)
    if fmt == "e4m3":
        byte = np.frexp(amax)[1] - 1 + 127 - 7
    else:
        mant, ex = np.frexp(amax / 6.0)
        byte = np.where(mant > 0.5, ex, ex - 1) + 127
    byte = np.clip(np.where(amax > 0, byte, 1), 1, 254)
    scaled = (w * np.exp2(127.0 - byte)[:, None, :]).reshape(k, n).astype(np.float32)
    by_word = np.ascontiguousarray(scaled.reshape(k // 512, 128, 4, n).transpose(0, 1, 3, 2))
    if fmt == "e4m3":
        words = by_word.astype(ml_dtypes.float8_e4m3fn).view(np.uint8)
    else:
        c = by_word.astype(ml_dtypes.float4_e2m1fn).view(np.uint8) & 0xF
        words = (c[..., 0::2] | (c[..., 1::2] << 4)).reshape(k // 512, 128, 2 * n)
    return np.ascontiguousarray(words), np.ascontiguousarray(byte.astype(np.uint8).reshape(k // 512, 16, n))


def unpack_weight(words, scales, fmt):
    g, _, n = scales.shape
    words = np.ascontiguousarray(words).reshape(g, 128, n, -1)
    if fmt == "e4m3":
        vals = words.view(ml_dtypes.float8_e4m3fn).astype(np.float64)
    else:
        nib = np.empty((g, 128, n, 4), np.uint8)
        nib[..., 0::2] = words & 0xF
        nib[..., 1::2] = words >> 4
        vals = E2M1[nib]
    vals = vals * np.repeat(np.exp2(scales.astype(np.float64) - 127.0), 8, axis=1)[..., None]
    return vals.transpose(0, 1, 3, 2).reshape(g * 512, n)


def gelu(v):
    return 0.5 * v * (1.0 + np.tanh(np.sqrt(2.0 / np.pi) * (v + 0.044715 * v**3)))


K, K2, H, N, T, S, T2 = 1024, 512, 512, 384, 4096, 1024, 2048

def setup_inputs():
    n = np.random.standard_normal
    s, s2, u = mx_kscale(K)[:, None], mx_kscale(K2)[:, None], mx_kscale(H)[:, None]
    tab_words, tab_scales = pack_weight(n((K, T)) * s, "e4m3")
    tab2_words, tab2_scales = pack_weight(n((K2, T)) * s2, "e4m3")
    wb_words, wb_scales = pack_weight(n((K, H)) / np.sqrt(K) / s * u.T, "e2m1")
    wi_words, wi_scales = pack_weight(n((K2, H)) / np.sqrt(K2) / s2 * u.T, "e4m3")
    perm = np.random.permutation(T2)
    return {
        "tab_words": tab_words, "tab_scales": tab_scales,
        "tab2_words": tab2_words, "tab2_scales": tab2_scales,
        "offs": striped(np.random.permutation(T)[:S]),
        "offs2": striped(np.random.permutation(T)[:S]),
        "offs3": striped(perm[:S]), "offs4": striped(perm[S:]),
        "wf": (n((K, H)) / np.sqrt(K) / s * u.T).astype(np.float32),
        "wb_words": wb_words, "wb_scales": wb_scales,
        "wm": (1.5 * n((K, H)) / np.sqrt(K) / s).astype(np.float32),
        "wi_words": wi_words, "wi_scales": wi_scales,
        "slope": np.random.uniform(0.1, 0.5, H).astype(np.float32),
        "wg1": np.exp(0.3 * n((128, S))).astype(np.float32),
        "wg2": np.exp(0.3 * n((128, S))).astype(np.float32),
        "wo": (n((H, N)) / np.sqrt(H) / u).astype(np.float32)}

def reference(tab_words, tab_scales, tab2_words, tab2_scales, offs, offs2, offs3, offs4, wf, wb_words, wb_scales,
              wm, wi_words, wi_scales, slope, wg1, wg2, wo):
    v = unpack_weight(tab_words, tab_scales, "e4m3")[:, unstriped(offs)]
    v2 = unpack_weight(tab2_words, tab2_scales, "e4m3")[:, unstriped(offs2)]
    fg = mxq(f64(wf), 0, "e4m3").T @ v
    bg = unpack_weight(wb_words, wb_scales, "e2m1").T @ v
    mt = mxq(f64(wm), 0, "e4m3").T @ v
    h1 = bg + 1.0 / (1.0 + np.exp(-mt)) * (fg - bg)
    d = unpack_weight(wi_words, wi_scales, "e4m3").T @ v2
    h2 = np.maximum(d, f64(slope)[:, None] * d)
    page = np.zeros((H, T2))
    page[:, unstriped(offs3)] = np.tile(f64(wg1), (H // 128, 1)) * h1
    page[:, unstriped(offs4)] = np.tile(f64(wg2), (H // 128, 1)) * h2
    return mxq(f64(wo), 0, "e4m3").T @ mxq(page, 0, "e4m3")

@@ -1,0 +1,280 @@
+from contextlib import ExitStack
+
+import concourse.mybir as mybir
+
+K, K2, H, N, T, S, T2 = 1024, 512, 512, 384, 4096, 1024, 2048
+FLOPS = 2 * (3 * K * H * S + K2 * H * S + H * N * T2)
+
+F32 = mybir.dt.float32
+BF16 = mybir.dt.bfloat16
+I32 = mybir.dt.int32
+U32 = mybir.dt.uint32
+U16 = mybir.dt.uint16
+U8 = mybir.dt.uint8
+FP8X4 = mybir.dt.float8_e4m3fn_x4
+FP4X4 = mybir.dt.float4_e2m1fn_x4
+ALU = mybir.AluOpType
+ACT = mybir.ActivationFunctionType
+
+P = 128
+PACK = 4
+QUAD = 32
+HALF = 512
+CHUNKS = (256, 256, 512, 512, 512)
+
+
+def tile_list_matting_patch_weave_kernel(
+    tc, tab_words, tab_scales, tab2_words, tab2_scales, offs, offs2, offs3, offs4, wf, wb_words, wb_scales,
+    wm, wi_words, wi_scales, slope, wg1, wg2, wo, out,
+):
+    nc = tc.nc
+    halves = S // HALF
+    list_cols = HALF // 16
+
+    with ExitStack() as ctx:
+        lists = ctx.enter_context(tc.tile_pool(name="lists", bufs=1))
+        keep = ctx.enter_context(tc.tile_pool(name="keep", bufs=1))
+        ring = ctx.enter_context(tc.tile_pool(name="ring", bufs=2))
+        psum = ctx.enter_context(tc.psum_pool(name="psum", bufs=2))
+
+        def load_list(src, name):
+            tile = lists.tile([P, S // 16], U16, name=name)
+            nc.sync.dma_start(tile[:], src)
+            return tile
+
+        def load_words(src, name, tag):
+            tile = keep.tile([P, T], U32, name=name, tag=tag)
+            nc.sync.dma_start(tile[:].bitcast(I32), src.rearrange("p t i -> p (t i)").bitcast(I32))
+            return tile
+
+        def zeroed_plane(width, name):
+            tile = keep.tile([P, width], U8, name=name, tag=name, align_bytes=64)
+            nc.vector.memset(tile[:].bitcast(I32), 0)
+            return tile
+
+        def load_gain(src, t, name):
+            tile = ring.tile([P, S], F32, name=name, tag="gain", bufs=5)
+            rows = src.rearrange("(b t) j -> t b j", t=PACK)[t]
+            for q in (0, 2, 1, 3):
+                nc.sync.dma_start(tile[QUAD * q : QUAD * (q + 1), :], rows)
+            return tile
+
+        def load_weight(src, name):
+            width = src.shape[1]
+            tile = ring.tile([P, PACK, width], F32, name=name, tag="raw", bufs=4)
+            nc.sync.dma_start(tile[:], src.rearrange("(p i) c -> p i c", i=PACK))
+            return tile
+
+        def unit(shape, dtype, name, tag):
+            return ring.tile(shape, dtype, name=name, tag=tag, bufs=8, align_bytes=64)
+
+        def bank(name, tag):
+            return psum.tile([P, HALF], F32, name=name, tag=tag, bufs=4 if tag == "fg" else 2)
+
+        wi_plane_raw = zeroed_plane(H, "wi_plane_raw")
+        tab2_plane = zeroed_plane(T, "tab2_plane")
+        tab_plane = zeroed_plane(T, "tab_plane")
+        wb_plane_raw = zeroed_plane(2 * H, "wb_plane_raw")
+        v_plane1 = zeroed_plane(S, "v_plane1")
+        for q in range(4):
+            nc.scalar.dma_start(
+                tab2_plane[QUAD * q : QUAD * q + 4, :].bitcast(I32), tab2_scales[0, 4 * q : 4 * q + 4, :].bitcast(I32)
+            )
+        for q in range(4):
+            nc.gpsimd.dma_start(
+                wi_plane_raw[QUAD * q : QUAD * q + 4, :].bitcast(I32), wi_scales[0, 4 * q : 4 * q + 4, :].bitcast(I32)
+            )
+        for q in range(4):
+            nc.scalar.dma_start(
+                tab_plane[QUAD * q : QUAD * q + 8, :].bitcast(I32), tab_scales[:, 4 * q : 4 * q + 4, :].bitcast(I32)
+            )
+        list2 = load_list(offs2, "list2")
+        wi_raw = keep.tile([P, H], I32, name="wi_raw")
+        nc.sync.dma_start(wi_raw[:], wi_words[0].rearrange("p c i -> p (c i)").bitcast(I32))
+        slopes = keep.tile([P, PACK], F32, name="slopes")
+        nc.sync.dma_start(slopes[:], slope.rearrange("(p t) -> p t", t=PACK))
+        list1 = load_list(offs, "list1")
+        list4 = load_list(offs4, "list4")
+        list3 = load_list(offs3, "list3")
+        wb_raw = keep.tile([P, 2, 2 * H], U8, name="wb_raw")
+        nc.sync.dma_start(wb_raw[:].bitcast(I32), wb_words.bitcast(I32).rearrange("a p c -> p a c"))
+        tab2_window = load_words(tab2_words[0], "tab2_window", "window_a")
+        gains2 = [load_gain(wg2, 0, "gain2_0")]
+        for q in range(4):
+            nc.sync.dma_start(
+                wb_plane_raw[QUAD * q : QUAD * q + 4, :].bitcast(I32).rearrange("p (a c) -> p a c", a=2),
+                wb_scales[:, 4 * q : 4 * q + 4, :].bitcast(I32).rearrange("a r c -> r a c"),
+            )
+
+        v2_plane = keep.tile([P, S], U8, name="v2_plane", align_bytes=64)
+        nc.vector.tensor_copy(v2_plane[:], tab2_plane[:].indirect(list2[:]))
+        wi_codes = keep.tile([P, H], I32, name="wi_codes", align_bytes=64)
+        nc.vector.tensor_copy(
+            wi_codes[:].rearrange("p (t m) -> p m t", t=PACK), wi_raw[:].rearrange("p (m t) -> p m t", t=PACK)
+        )
+        wi_plane = keep.tile([P, H], U8, name="wi_plane", align_bytes=64)
+        nc.vector.tensor_copy(
+            wi_plane[:].rearrange("p (t m) -> p m t", t=PACK), wi_plane_raw[:].rearrange("p (m t) -> p m t", t=PACK)
+        )
+        slope_less_one = keep.tile([P, PACK], F32, name="slope_less_one")
+        nc.scalar.activation(slope_less_one[:], slopes[:], ACT.Identity, bias=-1.0)
+
+        def gather_words(dst, window, lst, h):
+            nc.vector.tensor_copy(dst, window[:].indirect(lst[:, h * list_cols : (h + 1) * list_cols]))
+
+        v2_codes = keep.tile([P, S], U32, name="v2_codes", tag="tab2_plane", align_bytes=64)
+        for h in range(halves):
+            gather_words(v2_codes[:, h * HALF : (h + 1) * HALF], tab2_window, list2, h)
+        v_plane = keep.tile([P, S], U8, name="v_plane", tag="wi_plane_raw", align_bytes=64)
+        nc.vector.tensor_copy(v_plane[:], tab_plane[:].indirect(list1[:]))
+        for q in range(4):
+            nc.sync.dma_start(
+                v_plane1[QUAD * q : QUAD * q + 4, :].bitcast(I32), v_plane[QUAD * q + 4 : QUAD * q + 8, :].bitcast(I32)
+            )
+        wb_codes = keep.tile([P, 2, 2 * H], U8, name="wb_codes", align_bytes=64)
+        nc.vector.tensor_copy(
+            wb_codes[:].bitcast(U16).rearrange("p a (t m) -> p a m t", t=PACK),
+            wb_raw[:].bitcast(U16).rearrange("p a (m t) -> p a m t", t=PACK),
+        )
+        wb_plane = keep.tile([P, 2 * H], U8, name="wb_plane", align_bytes=64)
+        nc.vector.tensor_copy(
+            wb_plane[:].rearrange("p (a t m) -> p a m t", a=2, t=PACK),
+            wb_plane_raw[:].rearrange("p (a m t) -> p a m t", a=2, t=PACK),
+        )
+
+        def quantize_first_weight(src, a, name):
+            raw = load_weight(src[a * 512 : (a + 1) * 512, :], name + "_raw")
+            grouped = ring.tile([P, PACK * H], BF16, name=name + "_grouped", tag="grouped", bufs=4, align_bytes=64)
+            nc.scalar.copy(
+                grouped[:].rearrange("p (t m i) -> p m t i", t=PACK, i=PACK),
+                raw[:].rearrange("p i (m t) -> p m t i", t=PACK),
+            )
+            codes = keep.tile([P, H], U32, name=name + "_codes", align_bytes=64)
+            plane = keep.tile([P, H], U8, name=name + "_plane", align_bytes=64)
+            nc.vector.quantize_mx(codes[:].bitcast(FP8X4), plane[:], grouped[:])
+            return codes, plane
+
+        pages = []
+
+        def interior_slice(t, page):
+            cols_w = slice(t * P, (t + 1) * P)
+            for h in range(halves):
+                cols = slice(h * HALF, (h + 1) * HALF)
+                d = bank(f"d{t}{h}", "fg")
+                nc.tensor.matmul_mx(
+                    d[:], lhsT=wi_codes[:, cols_w].bitcast(FP8X4), lhsT_scale=wi_plane[:, cols_w],
+                    rhs=v2_codes[:, cols].bitcast(FP8X4), rhs_scale=v2_plane[:, cols], start=True, stop=True,
+                )
+                value = unit([P, HALF], F32, f"value2_{t}{h}", "value")
+                nc.scalar.copy(value[:], d[:])
+                lift = unit([P, HALF], F32, f"lift{t}{h}", "second")
+                nc.scalar.activation(lift[:], d[:], ACT.Relu, scale=slope_less_one[:, t : t + 1])
+                nc.gpsimd.tensor_tensor(value[:], value[:], lift[:], ALU.add)
+                nc.gpsimd.tensor_tensor(value[:], value[:], gains2[t][:, cols], ALU.mult)
+                nc.vector.tensor_copy(page[:].indirect(list4[:, h * list_cols : (h + 1) * list_cols]), value[:])
+
+        wq = {}
+        for t, (src, name) in enumerate(((wf, "wf"), (wm, "wm"))):
+            pages.append(keep.tile([P, T2], F32, name=f"page{t}"))
+            interior_slice(t, pages[t])
+            wq[name] = [quantize_first_weight(src, a, f"{name}{a}") for a in range(2)]
+            if t == 0:
+                gains2.append(load_gain(wg2, 1, "gain2_1"))
+
+        windows = [load_words(tab_words[0], "tab_window0", "window_a"), load_words(tab_words[1], "tab_window1", "window_b")]
+        v_codes = [[keep.tile([P, HALF], U32, name=f"v_codes{h}{a}", align_bytes=64) for a in range(2)] for h in range(halves)]
+        for h in range(halves):
+            for a in range(2):
+                gather_words(v_codes[h][a][:], windows[a], list1, h)
+        for t, tag in ((2, "window_b"), (3, "window_a")):
+            gains2.append(load_gain(wg2, t, f"gain2_{t}"))
+            pages.append(keep.tile([P, T2], F32, name=f"page{t}", tag=tag))
+            interior_slice(t, pages[t])
+
+        gains1 = [load_gain(wg1, 0, "gain1_0")]
+        wo_raw = load_weight(wo, "wo_raw")
+        for t in range(1, PACK):
+            gains1.append(load_gain(wg1, t, f"gain1_{t}"))
+
+        wo_grouped = ring.tile([P, PACK * N], BF16, name="wo_grouped", tag="grouped", bufs=4, align_bytes=64)
+        nc.scalar.copy(
+            wo_grouped[:].rearrange("p (c n i) -> p c i n", n=4, i=PACK),
+            wo_raw[:].rearrange("p i (c n) -> p c i n", n=4),
+        )
+        wo_codes = keep.tile([P, N], U32, name="wo_codes", align_bytes=64)
+        wo_plane = keep.tile([P, N], U8, name="wo_plane", align_bytes=64)
+        for c0, c1 in ((0, 256), (256, N)):
+            nc.vector.quantize_mx(wo_codes[:, c0:c1].bitcast(FP8X4), wo_plane[:, c0:c1], wo_grouped[:, PACK * c0 : PACK * c1])
+
+        for t in range(PACK):
+            cols_w = slice(t * P, (t + 1) * P)
+            for h in range(halves):
+                cols = slice(h * HALF, (h + 1) * HALF)
+                moving_planes = (v_plane[:, cols], v_plane[4:P, cols])
+                mt, bg, fg = bank(f"mt{t}{h}", "mt"), bank(f"bg{t}{h}", "bg"), bank(f"fg{t}{h}", "fg")
+                for a in range(2):
+                    codes, plane = wq["wm"][a]
+                    nc.tensor.matmul_mx(
+                        mt[:], lhsT=codes[:, cols_w].bitcast(FP8X4), lhsT_scale=plane[:, cols_w],
+                        rhs=v_codes[h][a][:].bitcast(FP8X4), rhs_scale=moving_planes[a], start=(a == 0), stop=(a == 1),
+                    )
+                for a in range(2):
+                    nc.tensor.matmul_mx(
+                        bg[:], lhsT=wb_codes[:, a, 2 * t * P : 2 * (t + 1) * P].bitcast(FP4X4),
+                        lhsT_scale=wb_plane[:, a * H + t * P : a * H + (t + 1) * P],
+                        rhs=v_codes[h][a][:].bitcast(FP8X4), rhs_scale=(v_plane, v_plane1)[a][:, cols],
+                        start=(a == 0), stop=(a == 1),
+                    )
+                for a in range(2):
+                    codes, plane = wq["wf"][a]
+                    nc.tensor.matmul_mx(
+                        fg[:], lhsT=codes[:, cols_w].bitcast(FP8X4), lhsT_scale=plane[:, cols_w],
+                        rhs=v_codes[h][a][:].bitcast(FP8X4), rhs_scale=moving_planes[a], start=(a == 0), stop=(a == 1),
+                    )
+                bg_sb = unit([P, HALF], F32, f"bg_sb{t}{h}", "first")
+                nc.scalar.copy(bg_sb[:], bg[:])
+                value = unit([P, HALF], F32, f"value1_{t}{h}", "value")
+                if t < 2:
+                    nc.scalar.copy(value[:], fg[:])
+                    nc.gpsimd.tensor_tensor(value[:], value[:], bg_sb[:], ALU.subtract)
+                else:
+                    nc.vector.tensor_tensor(value[:], fg[:], bg_sb[:], ALU.subtract)
+                matte = unit([P, HALF], F32, f"matte{t}{h}", "second")
+                nc.scalar.activation(matte[:], mt[:], ACT.Sigmoid)
+                nc.gpsimd.tensor_tensor(value[:], value[:], matte[:], ALU.mult)
+                nc.gpsimd.tensor_tensor(value[:], value[:], bg_sb[:], ALU.add)
+                nc.gpsimd.tensor_tensor(value[:], value[:], gains1[t][:, cols], ALU.mult)
+                nc.vector.tensor_copy(pages[t][:].indirect(list3[:, h * list_cols : (h + 1) * list_cols]), value[:])
+
+        starts = [sum(CHUNKS[:i]) for i in range(len(CHUNKS))]
+        low = ring.tile([P, 2, T2], BF16, name="low", tag="raw", bufs=4)
+        for t in range(2):
+            nc.scalar.copy(low[:, t, :], pages[t][:])
+        woven, high = [], []
+        for i, width in enumerate(CHUNKS):
+            cols = slice(starts[i], starts[i] + width)
+            tile = keep.tile([P, width, PACK], BF16, name=f"woven{i}", align_bytes=64)
+            nc.scalar.copy(tile[:, :, 0:2], low[:, :, cols].rearrange("p t c -> p c t"))
+            woven.append(tile)
+        for i, width in enumerate(CHUNKS):
+            cols = slice(starts[i], starts[i] + width)
+            tile = unit([P, 2, width], BF16, f"high{i}", "second")
+            nc.scalar.copy(tile[:, 0, :], pages[2][:, cols])
+            high.append(tile)
+        for i, width in enumerate(CHUNKS):
+            cols = slice(starts[i], starts[i] + width)
+            nc.vector.tensor_copy(high[i][:, 1, :], pages[3][:, cols])
+            nc.vector.tensor_copy(woven[i][:, :, 2:4], high[i][:].rearrange("p t c -> p c t"))
+            codes = ring.tile([P, width], U32, name=f"page_codes{i}", tag="page_codes", align_bytes=64)
+            plane = ring.tile([P, width], U8, name=f"page_plane{i}", tag="page_plane", align_bytes=64)
+            nc.vector.quantize_mx(codes[:].bitcast(FP8X4), plane[:], woven[i][:].rearrange("p c t -> p (c t)"))
+            for n in range(N // P):
+                rows = slice(n * P, (n + 1) * P)
+                acc = bank(f"acc{i}{n}", ("mt", "bg", "fg")[n])
+                nc.tensor.matmul_mx(
+                    acc[:, 0:width], lhsT=wo_codes[:, rows].bitcast(FP8X4), lhsT_scale=wo_plane[:, rows],
+                    rhs=codes[:].bitcast(FP8X4), rhs_scale=plane[:], start=True, stop=True,
+                )
+                result = unit([P, width], F32, f"result{i}{n}", "first")
+                nc.scalar.copy(result[:], acc[:, 0:width])
+                nc.sync.dma_start(out[rows, cols], result[:])

@@ -1,3 +1,4 @@
+import itertools
 from contextlib import ExitStack
 
 import concourse.mybir as mybir
@@ -20,6 +21,7 @@ P = 128
 PACK = 4
 QUAD = 32
 HALF = 512
+POOL_DIFFS = 4
 CHUNKS = (256, 256, 512, 512, 512)
 
 
@@ -35,84 +37,97 @@ def tile_list_matting_patch_weave_kernel(
         lists = ctx.enter_context(tc.tile_pool(name="lists", bufs=1))
         keep = ctx.enter_context(tc.tile_pool(name="keep", bufs=1))
         ring = ctx.enter_context(tc.tile_pool(name="ring", bufs=2))
-        psum = ctx.enter_context(tc.psum_pool(name="psum", bufs=2))
+        head = ctx.enter_context(tc.tile_pool(name="head", bufs=1))
+        wide = ctx.enter_context(tc.tile_pool(name="wide", bufs=1))
+        scratch = ctx.enter_context(tc.tile_pool(name="scratch", bufs=1))
+        psum = ctx.enter_context(tc.psum_pool(name="psum", bufs=1))
 
         def load_list(src, name):
             tile = lists.tile([P, S // 16], U16, name=name)
             nc.sync.dma_start(tile[:], src)
             return tile
 
-        def load_words(src, name, tag):
-            tile = keep.tile([P, T], U32, name=name, tag=tag)
-            nc.sync.dma_start(tile[:].bitcast(I32), src.rearrange("p t i -> p (t i)").bitcast(I32))
-            return tile
-
         def zeroed_plane(width, name):
-            tile = keep.tile([P, width], U8, name=name, tag=name, align_bytes=64)
+            tile = keep.tile([P, width], U8, name=name, align_bytes=64)
             nc.vector.memset(tile[:].bitcast(I32), 0)
             return tile
 
-        def load_gain(src, t, name):
-            tile = ring.tile([P, S], F32, name=name, tag="gain", bufs=5)
-            rows = src.rearrange("(b t) j -> t b j", t=PACK)[t]
+        def load_gain(src, pair, name):
+            tile = ring.tile([P, 2, S], F32, name=name, tag="gain")
+            rows = src.rearrange("(b u t) j -> u b t j", u=2, t=2)[pair]
             for q in (0, 2, 1, 3):
-                nc.sync.dma_start(tile[QUAD * q : QUAD * (q + 1), :], rows)
+                nc.sync.dma_start(tile[QUAD * q : QUAD * (q + 1), :, :], rows)
             return tile
 
-        def load_weight(src, name):
-            width = src.shape[1]
-            tile = ring.tile([P, PACK, width], F32, name=name, tag="raw", bufs=4)
-            nc.sync.dma_start(tile[:], src.rearrange("(p i) c -> p i c", i=PACK))
+        def load_weight(src, name, tag):
+            passes, width = src.shape[0] // 512, src.shape[1]
+            tile = keep.tile([P, passes, PACK, width], F32, name=name, tag=tag)
+            nc.sync.dma_start(
+                tile[:].rearrange("p a i c -> p a (i c)"), src.rearrange("(a p i) c -> p a (i c)", p=P, i=PACK)
+            )
             return tile
 
         def unit(shape, dtype, name, tag):
-            return ring.tile(shape, dtype, name=name, tag=tag, bufs=8, align_bytes=64)
+            return ring.tile(shape, dtype, name=name, tag=tag, bufs=9 if tag == "second" else 8, align_bytes=64)
 
-        def bank(name, tag):
-            return psum.tile([P, HALF], F32, name=name, tag=tag, bufs=4 if tag == "fg" else 2)
+        def bank(name, number):
+            return psum.tile([P, HALF], F32, name=name, tag=f"bank{number}")
 
-        wi_plane_raw = zeroed_plane(H, "wi_plane_raw")
-        tab2_plane = zeroed_plane(T, "tab2_plane")
-        tab_plane = zeroed_plane(T, "tab_plane")
+        wi_plane_raw = head.tile([P, H], U8, name="wi_plane_raw", offset=0)
+        nc.vector.memset(wi_plane_raw[:].bitcast(I32), 0)
+        tab2_rows = keep.tile([P, T], U8, name="tab2_rows")
+        nc.vector.memset(tab2_rows[0 : P - 16, :].bitcast(I32), 0)
+        tab_rows = keep.tile([P, T], U8, name="tab_rows")
+        nc.vector.memset(tab_rows[0 : P - 32, :].bitcast(I32), 0)
+        v2_plane = zeroed_plane(S, "v2_plane")
         wb_plane_raw = zeroed_plane(2 * H, "wb_plane_raw")
-        v_plane1 = zeroed_plane(S, "v_plane1")
-        for q in range(4):
-            nc.scalar.dma_start(
-                tab2_plane[QUAD * q : QUAD * q + 4, :].bitcast(I32), tab2_scales[0, 4 * q : 4 * q + 4, :].bitcast(I32)
-            )
+        v_planes = zeroed_plane(2 * S, "v_planes")
         for q in range(4):
             nc.gpsimd.dma_start(
                 wi_plane_raw[QUAD * q : QUAD * q + 4, :].bitcast(I32), wi_scales[0, 4 * q : 4 * q + 4, :].bitcast(I32)
             )
-        for q in range(4):
-            nc.scalar.dma_start(
-                tab_plane[QUAD * q : QUAD * q + 8, :].bitcast(I32), tab_scales[:, 4 * q : 4 * q + 4, :].bitcast(I32)
-            )
         list2 = load_list(offs2, "list2")
-        wi_raw = keep.tile([P, H], I32, name="wi_raw")
-        nc.sync.dma_start(wi_raw[:], wi_words[0].rearrange("p c i -> p (c i)").bitcast(I32))
+        nc.sync.dma_start(tab2_rows[P - 16 : P, :].bitcast(I32), tab2_scales[0].bitcast(I32))
+        v2_rows = keep.tile([P, S], U8, name="v2_rows")
+        nc.vector.tensor_copy(v2_rows[:], tab2_rows[:].indirect(list2[:]))
+        for q in range(4):
+            nc.sync.dma_start(
+                v2_plane[QUAD * q : QUAD * q + 4, :].bitcast(I32),
+                v2_rows[P - 16 + 4 * q : P - 12 + 4 * q, :].bitcast(I32),
+            )
+        list1 = load_list(offs, "list1")
+        nc.sync.dma_start(tab_rows[P - 32 : P, :].bitcast(I32), tab_scales.bitcast(I32).rearrange("a r t -> r a t"))
         slopes = keep.tile([P, PACK], F32, name="slopes")
         nc.sync.dma_start(slopes[:], slope.rearrange("(p t) -> p t", t=PACK))
-        list1 = load_list(offs, "list1")
         list4 = load_list(offs4, "list4")
+        wi_raw = keep.tile([P, H], I32, name="wi_raw")
+        nc.sync.dma_start(wi_raw[:], wi_words[0].rearrange("p c i -> p (c i)").bitcast(I32))
+        tab2_window = wide.tile([P, T], U32, name="tab2_window", offset=0)
+        nc.sync.dma_start(tab2_window[:].bitcast(I32), tab2_words[0].rearrange("p t i -> p (t i)").bitcast(I32))
         list3 = load_list(offs3, "list3")
-        wb_raw = keep.tile([P, 2, 2 * H], U8, name="wb_raw")
+        wb_raw = head.tile([P, 2, 2 * H], U8, name="wb_raw", offset=4 * HALF)
         nc.sync.dma_start(wb_raw[:].bitcast(I32), wb_words.bitcast(I32).rearrange("a p c -> p a c"))
-        tab2_window = load_words(tab2_words[0], "tab2_window", "window_a")
         gains2 = [load_gain(wg2, 0, "gain2_0")]
+        wf_raw = load_weight(wf, "wf_raw", "wf_raw")
         for q in range(4):
             nc.sync.dma_start(
                 wb_plane_raw[QUAD * q : QUAD * q + 4, :].bitcast(I32).rearrange("p (a c) -> p a c", a=2),
                 wb_scales[:, 4 * q : 4 * q + 4, :].bitcast(I32).rearrange("a r c -> r a c"),
             )
+        wm_raw = load_weight(wm, "wm_raw", "wm_raw")
 
-        v2_plane = keep.tile([P, S], U8, name="v2_plane", align_bytes=64)
-        nc.vector.tensor_copy(v2_plane[:], tab2_plane[:].indirect(list2[:]))
+        v_rows = keep.tile([P, S], U8, name="v_rows")
+        nc.vector.tensor_copy(v_rows[:], tab_rows[:].indirect(list1[:]))
         wi_codes = keep.tile([P, H], I32, name="wi_codes", align_bytes=64)
         nc.vector.tensor_copy(
             wi_codes[:].rearrange("p (t m) -> p m t", t=PACK), wi_raw[:].rearrange("p (m t) -> p m t", t=PACK)
         )
-        wi_plane = keep.tile([P, H], U8, name="wi_plane", align_bytes=64)
+        wb_codes = keep.tile([P, 2, 2 * H], U8, name="wb_codes", align_bytes=64)
+        nc.vector.tensor_copy(
+            wb_codes[:].bitcast(U16).rearrange("p a (t m) -> p a m t", t=PACK),
+            wb_raw[:].bitcast(U16).rearrange("p a (m t) -> p a m t", t=PACK),
+        )
+        wi_plane = head.tile([P, H], U8, name="wi_plane", offset=4 * HALF, align_bytes=64)
         nc.vector.tensor_copy(
             wi_plane[:].rearrange("p (t m) -> p m t", t=PACK), wi_plane_raw[:].rearrange("p (m t) -> p m t", t=PACK)
         )
@@ -120,157 +135,162 @@ def tile_list_matting_patch_weave_kernel(
         nc.scalar.activation(slope_less_one[:], slopes[:], ACT.Identity, bias=-1.0)
 
         def gather_words(dst, window, lst, h):
-            nc.vector.tensor_copy(dst, window[:].indirect(lst[:, h * list_cols : (h + 1) * list_cols]))
+            nc.vector.tensor_copy(dst, window.indirect(lst[:, h * list_cols : (h + 1) * list_cols]))
 
-        v2_codes = keep.tile([P, S], U32, name="v2_codes", tag="tab2_plane", align_bytes=64)
+        v2_codes = [
+            keep.tile([P, HALF], U32, name="v2_codes0", align_bytes=64),
+            head.tile([P, HALF], U32, name="v2_codes1", offset=0, align_bytes=64),
+        ]
         for h in range(halves):
-            gather_words(v2_codes[:, h * HALF : (h + 1) * HALF], tab2_window, list2, h)
-        v_plane = keep.tile([P, S], U8, name="v_plane", tag="wi_plane_raw", align_bytes=64)
-        nc.vector.tensor_copy(v_plane[:], tab_plane[:].indirect(list1[:]))
+            gather_words(v2_codes[h][:], tab2_window[:], list2, h)
         for q in range(4):
             nc.sync.dma_start(
-                v_plane1[QUAD * q : QUAD * q + 4, :].bitcast(I32), v_plane[QUAD * q + 4 : QUAD * q + 8, :].bitcast(I32)
+                v_planes[QUAD * q : QUAD * q + 4, :].bitcast(I32).rearrange("p (a c) -> p a c", a=2),
+                v_rows[P - 32 + 8 * q : P - 24 + 8 * q, :].bitcast(I32),
             )
-        wb_codes = keep.tile([P, 2, 2 * H], U8, name="wb_codes", align_bytes=64)
-        nc.vector.tensor_copy(
-            wb_codes[:].bitcast(U16).rearrange("p a (t m) -> p a m t", t=PACK),
-            wb_raw[:].bitcast(U16).rearrange("p a (m t) -> p a m t", t=PACK),
-        )
         wb_plane = keep.tile([P, 2 * H], U8, name="wb_plane", align_bytes=64)
         nc.vector.tensor_copy(
             wb_plane[:].rearrange("p (a t m) -> p a m t", a=2, t=PACK),
             wb_plane_raw[:].rearrange("p (a m t) -> p a m t", a=2, t=PACK),
         )
 
-        def quantize_first_weight(src, a, name):
-            raw = load_weight(src[a * 512 : (a + 1) * 512, :], name + "_raw")
-            grouped = ring.tile([P, PACK * H], BF16, name=name + "_grouped", tag="grouped", bufs=4, align_bytes=64)
-            nc.scalar.copy(
-                grouped[:].rearrange("p (t m i) -> p m t i", t=PACK, i=PACK),
-                raw[:].rearrange("p i (m t) -> p m t i", t=PACK),
-            )
-            codes = keep.tile([P, H], U32, name=name + "_codes", align_bytes=64)
-            plane = keep.tile([P, H], U8, name=name + "_plane", align_bytes=64)
-            nc.vector.quantize_mx(codes[:].bitcast(FP8X4), plane[:], grouped[:])
+        def quantize_first_weight(raw, name, place):
+            grouped = ring.tile([P, 2, PACK * H], BF16, name=name + "_grouped", tag="grouped", align_bytes=64)
+            for a in range(2):
+                nc.scalar.copy(
+                    grouped[:, a, :].rearrange("p (t m i) -> p m t i", t=PACK, i=PACK),
+                    raw[:, a, :, :].rearrange("p i (m t) -> p m t i", t=PACK),
+                )
+            codes = keep.tile([P, 2 * H], U32, name=name + "_codes", align_bytes=64)
+            plane = scratch.tile([P, 2 * H], U8, name=name + "_plane", offset=8 * HALF + place * 2 * H, align_bytes=64)
+            nc.vector.quantize_mx(codes[:].bitcast(FP8X4), plane[:], grouped[:].rearrange("p a x -> p (a x)"))
             return codes, plane
 
         pages = []
 
-        def interior_slice(t, page):
+        def interior_piece(t, c0, width, bank_number, work_offset):
+            h, name = c0 // HALF, f"{t}_{c0}"
             cols_w = slice(t * P, (t + 1) * P)
-            for h in range(halves):
-                cols = slice(h * HALF, (h + 1) * HALF)
-                d = bank(f"d{t}{h}", "fg")
-                nc.tensor.matmul_mx(
-                    d[:], lhsT=wi_codes[:, cols_w].bitcast(FP8X4), lhsT_scale=wi_plane[:, cols_w],
-                    rhs=v2_codes[:, cols].bitcast(FP8X4), rhs_scale=v2_plane[:, cols], start=True, stop=True,
-                )
-                value = unit([P, HALF], F32, f"value2_{t}{h}", "value")
-                nc.scalar.copy(value[:], d[:])
-                lift = unit([P, HALF], F32, f"lift{t}{h}", "second")
-                nc.scalar.activation(lift[:], d[:], ACT.Relu, scale=slope_less_one[:, t : t + 1])
-                nc.gpsimd.tensor_tensor(value[:], value[:], lift[:], ALU.add)
-                nc.gpsimd.tensor_tensor(value[:], value[:], gains2[t][:, cols], ALU.mult)
-                nc.vector.tensor_copy(page[:].indirect(list4[:, h * list_cols : (h + 1) * list_cols]), value[:])
+            cols = slice(c0, c0 + width)
+            d = bank("d" + name, bank_number)[:, 0:width]
+            nc.tensor.matmul_mx(
+                d, lhsT=wi_codes[:, cols_w].bitcast(FP8X4), lhsT_scale=wi_plane[:, cols_w],
+                rhs=v2_codes[h][:, c0 - h * HALF : c0 - h * HALF + width].bitcast(FP8X4), rhs_scale=v2_plane[:, cols],
+                start=True, stop=True,
+            )
+            if (t, h) == (1, 1):
+                value = scratch.tile([P, width], F32, name="value2_" + name, offset=8 * HALF)
+            else:
+                value = unit([P, width], F32, "value2_" + name, "value")
+            nc.scalar.copy(value[:], d)
+            lift = unit([P, width], F32, "lift" + name, "second")
+            nc.scalar.activation(lift[:], d, ACT.Relu, scale=slope_less_one[:, t : t + 1])
+            work = scratch.tile([P, HALF], F32, name="work2_" + name, offset=work_offset)[:, 0:width]
+            nc.gpsimd.tensor_tensor(work, value[:], lift[:], ALU.add)
+            nc.gpsimd.tensor_tensor(value[:], work, gains2[t // 2][:, t % 2, cols], ALU.mult)
+            nc.vector.tensor_copy(pages[t][:].indirect(list4[:, c0 // 16 : (c0 + width) // 16]), value[:])
 
-        wq = {}
-        for t, (src, name) in enumerate(((wf, "wf"), (wm, "wm"))):
-            pages.append(keep.tile([P, T2], F32, name=f"page{t}"))
-            interior_slice(t, pages[t])
-            wq[name] = [quantize_first_weight(src, a, f"{name}{a}") for a in range(2)]
-            if t == 0:
-                gains2.append(load_gain(wg2, 1, "gain2_1"))
+        def interior_pair(pair):
+            for h, t in itertools.product(range(halves), (2 * pair, 2 * pair + 1)):
+                alone = pair == 0 and (h, t) != (1, 1)
+                work_offset = 2 * HALF if alone else 4 * HALF * (t % 2)
+                if (h, t) == (0, 0):
+                    interior_piece(t, 0, HALF // 2, 0, work_offset)
+                    interior_piece(t, HALF // 2, HALF // 2, 4, work_offset)
+                else:
+                    interior_piece(t, h * HALF, HALF, 2 * h + t % 2, work_offset)
 
-        windows = [load_words(tab_words[0], "tab_window0", "window_a"), load_words(tab_words[1], "tab_window1", "window_b")]
+        pages.extend(keep.tile([P, T2], F32, name=f"page{t}") for t in (0, 1))
+        interior_pair(0)
+        gains2.append(load_gain(wg2, 1, "gain2_1"))
+        tab_window = wide.tile([P, 2, T], U32, name="tab_window", offset=4 * T)
+        nc.sync.dma_start(tab_window[:].bitcast(I32), tab_words.rearrange("a p t i -> p a (t i)").bitcast(I32))
         v_codes = [[keep.tile([P, HALF], U32, name=f"v_codes{h}{a}", align_bytes=64) for a in range(2)] for h in range(halves)]
         for h in range(halves):
             for a in range(2):
-                gather_words(v_codes[h][a][:], windows[a], list1, h)
-        for t, tag in ((2, "window_b"), (3, "window_a")):
-            gains2.append(load_gain(wg2, t, f"gain2_{t}"))
-            pages.append(keep.tile([P, T2], F32, name=f"page{t}", tag=tag))
-            interior_slice(t, pages[t])
+                gather_words(v_codes[h][a][:], tab_window[:, a, :], list1, h)
+        pages.extend(wide.tile([P, T2], F32, name=f"page{t}", offset=4 * T + 4 * T2 * (t - 2)) for t in (2, 3))
+        interior_pair(1)
+        wq = {"wf": quantize_first_weight(wf_raw, "wf", 0), "wm": quantize_first_weight(wm_raw, "wm", 1)}
 
         gains1 = [load_gain(wg1, 0, "gain1_0")]
-        wo_raw = load_weight(wo, "wo_raw")
-        for t in range(1, PACK):
-            gains1.append(load_gain(wg1, t, f"gain1_{t}"))
+        wo_raw = load_weight(wo, "wo_raw", "wf_raw")
+        gains1.append(load_gain(wg1, 1, "gain1_1"))
 
-        wo_grouped = ring.tile([P, PACK * N], BF16, name="wo_grouped", tag="grouped", bufs=4, align_bytes=64)
+        wo_grouped = ring.tile([P, PACK * N], BF16, name="wo_grouped", tag="grouped", align_bytes=64)
         nc.scalar.copy(
             wo_grouped[:].rearrange("p (c n i) -> p c i n", n=4, i=PACK),
-            wo_raw[:].rearrange("p i (c n) -> p c i n", n=4),
+            wo_raw[:, 0, :, :].rearrange("p i (c n) -> p c i n", n=4),
         )
-        wo_codes = keep.tile([P, N], U32, name="wo_codes", align_bytes=64)
-        wo_plane = keep.tile([P, N], U8, name="wo_plane", align_bytes=64)
-        for c0, c1 in ((0, 256), (256, N)):
-            nc.vector.quantize_mx(wo_codes[:, c0:c1].bitcast(FP8X4), wo_plane[:, c0:c1], wo_grouped[:, PACK * c0 : PACK * c1])
-
         for t in range(PACK):
             cols_w = slice(t * P, (t + 1) * P)
             for h in range(halves):
                 cols = slice(h * HALF, (h + 1) * HALF)
-                moving_planes = (v_plane[:, cols], v_plane[4:P, cols])
-                mt, bg, fg = bank(f"mt{t}{h}", "mt"), bank(f"bg{t}{h}", "bg"), bank(f"fg{t}{h}", "fg")
-                for a in range(2):
-                    codes, plane = wq["wm"][a]
-                    nc.tensor.matmul_mx(
-                        mt[:], lhsT=codes[:, cols_w].bitcast(FP8X4), lhsT_scale=plane[:, cols_w],
-                        rhs=v_codes[h][a][:].bitcast(FP8X4), rhs_scale=moving_planes[a], start=(a == 0), stop=(a == 1),
-                    )
+                moving_planes = [v_planes[:, a * S + h * HALF : a * S + (h + 1) * HALF] for a in range(2)]
+                mt, bg, fg = bank(f"mt{t}{h}", 4 + h), bank(f"bg{t}{h}", 6 + h), bank(f"fg{t}{h}", (2 if t == 2 else 0) + h)
                 for a in range(2):
                     nc.tensor.matmul_mx(
                         bg[:], lhsT=wb_codes[:, a, 2 * t * P : 2 * (t + 1) * P].bitcast(FP4X4),
                         lhsT_scale=wb_plane[:, a * H + t * P : a * H + (t + 1) * P],
-                        rhs=v_codes[h][a][:].bitcast(FP8X4), rhs_scale=(v_plane, v_plane1)[a][:, cols],
+                        rhs=v_codes[h][a][:].bitcast(FP8X4), rhs_scale=moving_planes[a],
                         start=(a == 0), stop=(a == 1),
                     )
                 for a in range(2):
-                    codes, plane = wq["wf"][a]
+                    codes, plane = wq["wf"]
+                    cols_a = slice(a * H + t * P, a * H + (t + 1) * P)
                     nc.tensor.matmul_mx(
-                        fg[:], lhsT=codes[:, cols_w].bitcast(FP8X4), lhsT_scale=plane[:, cols_w],
+                        fg[:], lhsT=codes[:, cols_a].bitcast(FP8X4), lhsT_scale=plane[:, cols_a],
+                        rhs=v_codes[h][a][:].bitcast(FP8X4), rhs_scale=moving_planes[a], start=(a == 0), stop=(a == 1),
+                    )
+                for a in range(2):
+                    codes, plane = wq["wm"]
+                    cols_a = slice(a * H + t * P, a * H + (t + 1) * P)
+                    nc.tensor.matmul_mx(
+                        mt[:], lhsT=codes[:, cols_a].bitcast(FP8X4), lhsT_scale=plane[:, cols_a],
                         rhs=v_codes[h][a][:].bitcast(FP8X4), rhs_scale=moving_planes[a], start=(a == 0), stop=(a == 1),
                     )
                 bg_sb = unit([P, HALF], F32, f"bg_sb{t}{h}", "first")
                 nc.scalar.copy(bg_sb[:], bg[:])
                 value = unit([P, HALF], F32, f"value1_{t}{h}", "value")
-                if t < 2:
-                    nc.scalar.copy(value[:], fg[:])
-                    nc.gpsimd.tensor_tensor(value[:], value[:], bg_sb[:], ALU.subtract)
-                else:
-                    nc.vector.tensor_tensor(value[:], fg[:], bg_sb[:], ALU.subtract)
                 matte = unit([P, HALF], F32, f"matte{t}{h}", "second")
                 nc.scalar.activation(matte[:], mt[:], ACT.Sigmoid)
-                nc.gpsimd.tensor_tensor(value[:], value[:], matte[:], ALU.mult)
-                nc.gpsimd.tensor_tensor(value[:], value[:], bg_sb[:], ALU.add)
-                nc.gpsimd.tensor_tensor(value[:], value[:], gains1[t][:, cols], ALU.mult)
+                work = scratch.tile([P, HALF], F32, name=f"work1_{t}{h}", offset=4 * HALF * h)
+                if halves * t + h < POOL_DIFFS:
+                    nc.scalar.copy(value[:], fg[:])
+                    nc.gpsimd.tensor_tensor(work[:], value[:], bg_sb[:], ALU.subtract)
+                    nc.gpsimd.tensor_tensor(work[:], work[:], matte[:], ALU.mult)
+                else:
+                    nc.vector.tensor_tensor(value[:], fg[:], bg_sb[:], ALU.subtract)
+                    nc.gpsimd.tensor_tensor(work[:], value[:], matte[:], ALU.mult)
+                nc.gpsimd.tensor_tensor(work[:], work[:], bg_sb[:], ALU.add)
+                nc.gpsimd.tensor_tensor(value[:], work[:], gains1[t // 2][:, t % 2, cols], ALU.mult)
                 nc.vector.tensor_copy(pages[t][:].indirect(list3[:, h * list_cols : (h + 1) * list_cols]), value[:])
 
+        wo_codes = keep.tile([P, N], U32, name="wo_codes", align_bytes=64)
+        wo_plane = scratch.tile([P, N], U8, name="wo_plane", offset=0, align_bytes=64)
+        for c0, c1 in ((0, 256), (256, N)):
+            nc.vector.quantize_mx(wo_codes[:, c0:c1].bitcast(FP8X4), wo_plane[:, c0:c1], wo_grouped[:, PACK * c0 : PACK * c1])
+
         starts = [sum(CHUNKS[:i]) for i in range(len(CHUNKS))]
-        low = ring.tile([P, 2, T2], BF16, name="low", tag="raw", bufs=4)
-        for t in range(2):
-            nc.scalar.copy(low[:, t, :], pages[t][:])
-        woven, high = [], []
+        woven = [wide.tile([P, width, PACK], BF16, name=f"woven{i}", offset=2 * PACK * starts[i], align_bytes=64) for i, width in enumerate(CHUNKS)]
+        for t in range(PACK - 1):
+            for i, width in enumerate(CHUNKS):
+                src = pages[t][:, starts[i] : starts[i] + width]
+                if t < 2:
+                    nc.scalar.copy(woven[i][:, :, t], src)
+                else:
+                    nc.scalar.copy(woven[i][:, :, 2:4], src.unsqueeze(2).to_broadcast([P, width, 2]))
         for i, width in enumerate(CHUNKS):
             cols = slice(starts[i], starts[i] + width)
-            tile = keep.tile([P, width, PACK], BF16, name=f"woven{i}", align_bytes=64)
-            nc.scalar.copy(tile[:, :, 0:2], low[:, :, cols].rearrange("p t c -> p c t"))
-            woven.append(tile)
-        for i, width in enumerate(CHUNKS):
-            cols = slice(starts[i], starts[i] + width)
-            tile = unit([P, 2, width], BF16, f"high{i}", "second")
-            nc.scalar.copy(tile[:, 0, :], pages[2][:, cols])
-            high.append(tile)
-        for i, width in enumerate(CHUNKS):
-            cols = slice(starts[i], starts[i] + width)
-            nc.vector.tensor_copy(high[i][:, 1, :], pages[3][:, cols])
-            nc.vector.tensor_copy(woven[i][:, :, 2:4], high[i][:].rearrange("p t c -> p c t"))
+            last = ring.tile([P, width], BF16, name=f"last{i}", tag="last")
+            nc.vector.tensor_copy(last[:], pages[3][:, cols])
+            nc.vector.tensor_copy(woven[i][:, :, 3], last[:])
             codes = ring.tile([P, width], U32, name=f"page_codes{i}", tag="page_codes", align_bytes=64)
             plane = ring.tile([P, width], U8, name=f"page_plane{i}", tag="page_plane", align_bytes=64)
             nc.vector.quantize_mx(codes[:].bitcast(FP8X4), plane[:], woven[i][:].rearrange("p c t -> p (c t)"))
             for n in range(N // P):
                 rows = slice(n * P, (n + 1) * P)
-                acc = bank(f"acc{i}{n}", ("mt", "bg", "fg")[n])
+                acc = bank(f"acc{i}{n}", (3 * i + n) % 8)
                 nc.tensor.matmul_mx(
                     acc[:, 0:width], lhsT=wo_codes[:, rows].bitcast(FP8X4), lhsT_scale=wo_plane[:, rows],
                     rhs=codes[:].bitcast(FP8X4), rhs_scale=plane[:], start=True, stop=True,

@@ -1,4 +1,3 @@
-import itertools
 from contextlib import ExitStack
 
 import concourse.mybir as mybir
@@ -22,7 +21,10 @@ PACK = 4
 QUAD = 32
 HALF = 512
 POOL_DIFFS = 4
+FG_BANKS = (0, 1, 0, 1, 2, 3, 0, 1)
+FIRST_PIECES = ((0, 256), (256, 256), (512, 512))
 CHUNKS = (256, 256, 512, 512, 512)
+VEC_CHUNKS, VEC_FROM = 1, 1
 
 
 def tile_list_matting_patch_weave_kernel(
@@ -37,7 +39,6 @@ def tile_list_matting_patch_weave_kernel(
         lists = ctx.enter_context(tc.tile_pool(name="lists", bufs=1))
         keep = ctx.enter_context(tc.tile_pool(name="keep", bufs=1))
         ring = ctx.enter_context(tc.tile_pool(name="ring", bufs=2))
-        head = ctx.enter_context(tc.tile_pool(name="head", bufs=1))
         wide = ctx.enter_context(tc.tile_pool(name="wide", bufs=1))
         scratch = ctx.enter_context(tc.tile_pool(name="scratch", bufs=1))
         psum = ctx.enter_context(tc.psum_pool(name="psum", bufs=1))
@@ -73,7 +74,7 @@ def tile_list_matting_patch_weave_kernel(
         def bank(name, number):
             return psum.tile([P, HALF], F32, name=name, tag=f"bank{number}")
 
-        wi_plane_raw = head.tile([P, H], U8, name="wi_plane_raw", offset=0)
+        wi_plane_raw = keep.tile([P, H], U8, name="wi_plane_raw")
         nc.vector.memset(wi_plane_raw[:].bitcast(I32), 0)
         tab2_rows = keep.tile([P, T], U8, name="tab2_rows")
         nc.vector.memset(tab2_rows[0 : P - 16, :].bitcast(I32), 0)
@@ -82,33 +83,33 @@ def tile_list_matting_patch_weave_kernel(
         v2_plane = zeroed_plane(S, "v2_plane")
         wb_plane_raw = zeroed_plane(2 * H, "wb_plane_raw")
         v_planes = zeroed_plane(2 * S, "v_planes")
+        nc.gpsimd.dma_start(tab_rows[P - 32 : P, :].bitcast(I32), tab_scales.bitcast(I32).rearrange("a r t -> r a t"))
         for q in range(4):
             nc.gpsimd.dma_start(
                 wi_plane_raw[QUAD * q : QUAD * q + 4, :].bitcast(I32), wi_scales[0, 4 * q : 4 * q + 4, :].bitcast(I32)
             )
         list2 = load_list(offs2, "list2")
         nc.sync.dma_start(tab2_rows[P - 16 : P, :].bitcast(I32), tab2_scales[0].bitcast(I32))
+        list1 = load_list(offs, "list1")
+        wi_raw = keep.tile([P, H], I32, name="wi_raw")
+        nc.sync.dma_start(wi_raw[:], wi_words[0].rearrange("p c i -> p (c i)").bitcast(I32))
+        list4 = load_list(offs4, "list4")
+        slopes = keep.tile([P, PACK], F32, name="slopes")
+        nc.sync.dma_start(slopes[:], slope.rearrange("(p t) -> p t", t=PACK))
+        tab2_window = wide.tile([P, T], U32, name="tab2_window", offset=0)
+        nc.sync.dma_start(tab2_window[:].bitcast(I32), tab2_words[0].rearrange("p t i -> p (t i)").bitcast(I32))
         v2_rows = keep.tile([P, S], U8, name="v2_rows")
         nc.vector.tensor_copy(v2_rows[:], tab2_rows[:].indirect(list2[:]))
         for q in range(4):
-            nc.sync.dma_start(
+            nc.scalar.dma_start(
                 v2_plane[QUAD * q : QUAD * q + 4, :].bitcast(I32),
                 v2_rows[P - 16 + 4 * q : P - 12 + 4 * q, :].bitcast(I32),
             )
-        list1 = load_list(offs, "list1")
-        nc.sync.dma_start(tab_rows[P - 32 : P, :].bitcast(I32), tab_scales.bitcast(I32).rearrange("a r t -> r a t"))
-        slopes = keep.tile([P, PACK], F32, name="slopes")
-        nc.sync.dma_start(slopes[:], slope.rearrange("(p t) -> p t", t=PACK))
-        list4 = load_list(offs4, "list4")
-        wi_raw = keep.tile([P, H], I32, name="wi_raw")
-        nc.sync.dma_start(wi_raw[:], wi_words[0].rearrange("p c i -> p (c i)").bitcast(I32))
-        tab2_window = wide.tile([P, T], U32, name="tab2_window", offset=0)
-        nc.sync.dma_start(tab2_window[:].bitcast(I32), tab2_words[0].rearrange("p t i -> p (t i)").bitcast(I32))
-        list3 = load_list(offs3, "list3")
-        wb_raw = head.tile([P, 2, 2 * H], U8, name="wb_raw", offset=4 * HALF)
-        nc.sync.dma_start(wb_raw[:].bitcast(I32), wb_words.bitcast(I32).rearrange("a p c -> p a c"))
         gains2 = [load_gain(wg2, 0, "gain2_0")]
         wf_raw = load_weight(wf, "wf_raw", "wf_raw")
+        list3 = load_list(offs3, "list3")
+        wb_raw = keep.tile([P, 2, 2 * H], U8, name="wb_raw")
+        nc.sync.dma_start(wb_raw[:].bitcast(I32), wb_words.bitcast(I32).rearrange("a p c -> p a c"))
         for q in range(4):
             nc.sync.dma_start(
                 wb_plane_raw[QUAD * q : QUAD * q + 4, :].bitcast(I32).rearrange("p (a c) -> p a c", a=2),
@@ -119,17 +120,18 @@ def tile_list_matting_patch_weave_kernel(
         v_rows = keep.tile([P, S], U8, name="v_rows")
         nc.vector.tensor_copy(v_rows[:], tab_rows[:].indirect(list1[:]))
         wi_codes = keep.tile([P, H], I32, name="wi_codes", align_bytes=64)
-        nc.vector.tensor_copy(
-            wi_codes[:].rearrange("p (t m) -> p m t", t=PACK), wi_raw[:].rearrange("p (m t) -> p m t", t=PACK)
+        nc.scalar.copy(
+            wi_codes[:].bitcast(U16).rearrange("p (t m e) -> p m t e", t=PACK, e=2),
+            wi_raw[:].bitcast(U16).rearrange("p (m t e) -> p m t e", t=PACK, e=2),
         )
-        wb_codes = keep.tile([P, 2, 2 * H], U8, name="wb_codes", align_bytes=64)
-        nc.vector.tensor_copy(
-            wb_codes[:].bitcast(U16).rearrange("p a (t m) -> p a m t", t=PACK),
-            wb_raw[:].bitcast(U16).rearrange("p a (m t) -> p a m t", t=PACK),
-        )
-        wi_plane = head.tile([P, H], U8, name="wi_plane", offset=4 * HALF, align_bytes=64)
+        wi_plane = keep.tile([P, H], U8, name="wi_plane", align_bytes=64)
         nc.vector.tensor_copy(
             wi_plane[:].rearrange("p (t m) -> p m t", t=PACK), wi_plane_raw[:].rearrange("p (m t) -> p m t", t=PACK)
+        )
+        wb_codes = keep.tile([P, 2, 2 * H], U8, name="wb_codes", align_bytes=64)
+        nc.scalar.copy(
+            wb_codes[:].bitcast(U16).rearrange("p a (t m) -> p a m t", t=PACK),
+            wb_raw[:].bitcast(U16).rearrange("p a (m t) -> p a m t", t=PACK),
         )
         slope_less_one = keep.tile([P, PACK], F32, name="slope_less_one")
         nc.scalar.activation(slope_less_one[:], slopes[:], ACT.Identity, bias=-1.0)
@@ -137,10 +139,7 @@ def tile_list_matting_patch_weave_kernel(
         def gather_words(dst, window, lst, h):
             nc.vector.tensor_copy(dst, window.indirect(lst[:, h * list_cols : (h + 1) * list_cols]))
 
-        v2_codes = [
-            keep.tile([P, HALF], U32, name="v2_codes0", align_bytes=64),
-            head.tile([P, HALF], U32, name="v2_codes1", offset=0, align_bytes=64),
-        ]
+        v2_codes = [keep.tile([P, HALF], U32, name=f"v2_codes{h}", align_bytes=64) for h in range(halves)]
         for h in range(halves):
             gather_words(v2_codes[h][:], tab2_window[:], list2, h)
         for q in range(4):
@@ -148,60 +147,55 @@ def tile_list_matting_patch_weave_kernel(
                 v_planes[QUAD * q : QUAD * q + 4, :].bitcast(I32).rearrange("p (a c) -> p a c", a=2),
                 v_rows[P - 32 + 8 * q : P - 24 + 8 * q, :].bitcast(I32),
             )
-        wb_plane = keep.tile([P, 2 * H], U8, name="wb_plane", align_bytes=64)
+        wb_plane = wide.tile([P, 2 * H], U8, name="wb_plane", offset=0, align_bytes=64)
         nc.vector.tensor_copy(
             wb_plane[:].rearrange("p (a t m) -> p a m t", a=2, t=PACK),
             wb_plane_raw[:].rearrange("p (a m t) -> p a m t", a=2, t=PACK),
         )
 
-        def quantize_first_weight(raw, name, place):
-            grouped = ring.tile([P, 2, PACK * H], BF16, name=name + "_grouped", tag="grouped", align_bytes=64)
-            for a in range(2):
-                nc.scalar.copy(
-                    grouped[:, a, :].rearrange("p (t m i) -> p m t i", t=PACK, i=PACK),
-                    raw[:, a, :, :].rearrange("p i (m t) -> p m t i", t=PACK),
-                )
-            codes = keep.tile([P, 2 * H], U32, name=name + "_codes", align_bytes=64)
-            plane = scratch.tile([P, 2 * H], U8, name=name + "_plane", offset=8 * HALF + place * 2 * H, align_bytes=64)
-            nc.vector.quantize_mx(codes[:].bitcast(FP8X4), plane[:], grouped[:].rearrange("p a x -> p (a x)"))
-            return codes, plane
-
         pages = []
 
-        def interior_piece(t, c0, width, bank_number, work_offset):
+        def interior_piece(t, value, c0, width):
             h, name = c0 // HALF, f"{t}_{c0}"
             cols_w = slice(t * P, (t + 1) * P)
             cols = slice(c0, c0 + width)
-            d = bank("d" + name, bank_number)[:, 0:width]
+            d = bank("d" + name, (0, 4, 1)[(halves * t + h + (0 if (t, c0) == (0, 0) else 1)) % 3])[:, 0:width]
             nc.tensor.matmul_mx(
                 d, lhsT=wi_codes[:, cols_w].bitcast(FP8X4), lhsT_scale=wi_plane[:, cols_w],
                 rhs=v2_codes[h][:, c0 - h * HALF : c0 - h * HALF + width].bitcast(FP8X4), rhs_scale=v2_plane[:, cols],
                 start=True, stop=True,
             )
-            if (t, h) == (1, 1):
-                value = scratch.tile([P, width], F32, name="value2_" + name, offset=8 * HALF)
-            else:
-                value = unit([P, width], F32, "value2_" + name, "value")
-            nc.scalar.copy(value[:], d)
             lift = unit([P, width], F32, "lift" + name, "second")
             nc.scalar.activation(lift[:], d, ACT.Relu, scale=slope_less_one[:, t : t + 1])
-            work = scratch.tile([P, HALF], F32, name="work2_" + name, offset=work_offset)[:, 0:width]
-            nc.gpsimd.tensor_tensor(work, value[:], lift[:], ALU.add)
-            nc.gpsimd.tensor_tensor(value[:], work, gains2[t // 2][:, t % 2, cols], ALU.mult)
-            nc.vector.tensor_copy(pages[t][:].indirect(list4[:, c0 // 16 : (c0 + width) // 16]), value[:])
+            gain = gains2[t // 2][:, t % 2, cols]
+            if t == 0:
+                leaky = lift if h == 0 else scratch.tile([P, HALF], F32, name="leaky_0", offset=2 * HALF)
+                nc.vector.tensor_tensor(leaky[:], d, lift[:], ALU.add)
+            else:
+                nc.scalar.copy(value[:, cols], d)
+                leaky = scratch.tile([P, HALF], F32, name="leaky_" + name, offset=4 * HALF * h)
+                nc.gpsimd.tensor_tensor(leaky[:], value[:, cols], lift[:], ALU.add)
+            nc.gpsimd.tensor_tensor(value[:, cols], leaky[:], gain, ALU.mult)
 
-        def interior_pair(pair):
-            for h, t in itertools.product(range(halves), (2 * pair, 2 * pair + 1)):
-                alone = pair == 0 and (h, t) != (1, 1)
-                work_offset = 2 * HALF if alone else 4 * HALF * (t % 2)
-                if (h, t) == (0, 0):
-                    interior_piece(t, 0, HALF // 2, 0, work_offset)
-                    interior_piece(t, HALF // 2, HALF // 2, 4, work_offset)
-                else:
-                    interior_piece(t, h * HALF, HALF, 2 * h + t % 2, work_offset)
+        def interior_slice(t):
+            if t == 1:
+                value = scratch.tile([P, S], F32, name="value2_1", offset=8 * HALF)
+            else:
+                value = keep.tile([P, S], F32, name=f"value2_{t}", tag=f"value{max(t - 1, 0)}", align_bytes=64)
+            if t == 0:
+                for c0, width in FIRST_PIECES:
+                    interior_piece(t, value, c0, width)
+                    nc.vector.tensor_copy(
+                        pages[t][:].indirect(list4[:, c0 // 16 : (c0 + width) // 16]), value[:, c0 : c0 + width]
+                    )
+            else:
+                for h in range(halves):
+                    interior_piece(t, value, h * HALF, HALF)
+                nc.vector.tensor_copy(pages[t][:].indirect(list4[:]), value[:])
 
         pages.extend(keep.tile([P, T2], F32, name=f"page{t}") for t in (0, 1))
-        interior_pair(0)
+        interior_slice(0)
+        interior_slice(1)
         gains2.append(load_gain(wg2, 1, "gain2_1"))
         tab_window = wide.tile([P, 2, T], U32, name="tab_window", offset=4 * T)
         nc.sync.dma_start(tab_window[:].bitcast(I32), tab_words.rearrange("a p t i -> p a (t i)").bitcast(I32))
@@ -209,25 +203,41 @@ def tile_list_matting_patch_weave_kernel(
         for h in range(halves):
             for a in range(2):
                 gather_words(v_codes[h][a][:], tab_window[:, a, :], list1, h)
-        pages.extend(wide.tile([P, T2], F32, name=f"page{t}", offset=4 * T + 4 * T2 * (t - 2)) for t in (2, 3))
-        interior_pair(1)
-        wq = {"wf": quantize_first_weight(wf_raw, "wf", 0), "wm": quantize_first_weight(wm_raw, "wm", 1)}
+        pages.extend(wide.tile([P, T2], F32, name=f"page{t}", offset=8 * T + 4 * T2 * (t - 2)) for t in (2, 3))
+        interior_slice(2)
+        interior_slice(3)
+        grouped = keep.tile([P, 4, PACK * H], BF16, name="w_grouped", tag="grouped", align_bytes=64)
+        for w, raw in enumerate((wf_raw, wm_raw)):
+            for a in range(2):
+                nc.scalar.copy(
+                    grouped[:, 2 * w + a, :].rearrange("p (t m i) -> p m t i", t=PACK, i=PACK),
+                    raw[:, a, :, :].rearrange("p i (m t) -> p m t i", t=PACK),
+                )
+        w_codes = keep.tile([P, 4 * H], U32, name="w_codes", align_bytes=64)
+        w_plane = scratch.tile([P, 4 * H], U8, name="w_plane", offset=8 * HALF, align_bytes=64)
+        for w in range(2):
+            half = slice(2 * w * H, 2 * (w + 1) * H)
+            nc.vector.quantize_mx(
+                w_codes[:, half].bitcast(FP8X4), w_plane[:, half],
+                grouped[:, 2 * w : 2 * w + 2, :].rearrange("p a x -> p (a x)"),
+            )
 
         gains1 = [load_gain(wg1, 0, "gain1_0")]
         wo_raw = load_weight(wo, "wo_raw", "wf_raw")
         gains1.append(load_gain(wg1, 1, "gain1_1"))
 
-        wo_grouped = ring.tile([P, PACK * N], BF16, name="wo_grouped", tag="grouped", align_bytes=64)
+        wo_grouped = keep.tile([P, PACK * N], BF16, name="wo_grouped", tag="grouped", align_bytes=64)
         nc.scalar.copy(
             wo_grouped[:].rearrange("p (c n i) -> p c i n", n=4, i=PACK),
             wo_raw[:, 0, :, :].rearrange("p i (c n) -> p c i n", n=4),
         )
         for t in range(PACK):
-            cols_w = slice(t * P, (t + 1) * P)
+            value = keep.tile([P, S], F32, name=f"value1_{t}", tag=f"value{t % 3}", align_bytes=64)
+            gain = gains1[t // 2][:, t % 2, :]
             for h in range(halves):
                 cols = slice(h * HALF, (h + 1) * HALF)
                 moving_planes = [v_planes[:, a * S + h * HALF : a * S + (h + 1) * HALF] for a in range(2)]
-                mt, bg, fg = bank(f"mt{t}{h}", 4 + h), bank(f"bg{t}{h}", 6 + h), bank(f"fg{t}{h}", (2 if t == 2 else 0) + h)
+                mt, bg, fg = bank(f"mt{t}{h}", 4 + h), bank(f"bg{t}{h}", 6 + h), bank(f"fg{t}{h}", FG_BANKS[halves * t + h])
                 for a in range(2):
                     nc.tensor.matmul_mx(
                         bg[:], lhsT=wb_codes[:, a, 2 * t * P : 2 * (t + 1) * P].bitcast(FP4X4),
@@ -236,38 +246,41 @@ def tile_list_matting_patch_weave_kernel(
                         start=(a == 0), stop=(a == 1),
                     )
                 for a in range(2):
-                    codes, plane = wq["wf"]
                     cols_a = slice(a * H + t * P, a * H + (t + 1) * P)
                     nc.tensor.matmul_mx(
-                        fg[:], lhsT=codes[:, cols_a].bitcast(FP8X4), lhsT_scale=plane[:, cols_a],
+                        fg[:], lhsT=w_codes[:, cols_a].bitcast(FP8X4), lhsT_scale=w_plane[:, cols_a],
                         rhs=v_codes[h][a][:].bitcast(FP8X4), rhs_scale=moving_planes[a], start=(a == 0), stop=(a == 1),
                     )
                 for a in range(2):
-                    codes, plane = wq["wm"]
-                    cols_a = slice(a * H + t * P, a * H + (t + 1) * P)
+                    cols_a = slice((2 + a) * H + t * P, (2 + a) * H + (t + 1) * P)
                     nc.tensor.matmul_mx(
-                        mt[:], lhsT=codes[:, cols_a].bitcast(FP8X4), lhsT_scale=plane[:, cols_a],
+                        mt[:], lhsT=w_codes[:, cols_a].bitcast(FP8X4), lhsT_scale=w_plane[:, cols_a],
                         rhs=v_codes[h][a][:].bitcast(FP8X4), rhs_scale=moving_planes[a], start=(a == 0), stop=(a == 1),
                     )
                 bg_sb = unit([P, HALF], F32, f"bg_sb{t}{h}", "first")
                 nc.scalar.copy(bg_sb[:], bg[:])
-                value = unit([P, HALF], F32, f"value1_{t}{h}", "value")
                 matte = unit([P, HALF], F32, f"matte{t}{h}", "second")
                 nc.scalar.activation(matte[:], mt[:], ACT.Sigmoid)
                 work = scratch.tile([P, HALF], F32, name=f"work1_{t}{h}", offset=4 * HALF * h)
                 if halves * t + h < POOL_DIFFS:
-                    nc.scalar.copy(value[:], fg[:])
-                    nc.gpsimd.tensor_tensor(work[:], value[:], bg_sb[:], ALU.subtract)
+                    nc.scalar.copy(value[:, cols], fg[:])
+                    nc.gpsimd.tensor_tensor(work[:], value[:, cols], bg_sb[:], ALU.subtract)
                     nc.gpsimd.tensor_tensor(work[:], work[:], matte[:], ALU.mult)
                 else:
-                    nc.vector.tensor_tensor(value[:], fg[:], bg_sb[:], ALU.subtract)
-                    nc.gpsimd.tensor_tensor(work[:], value[:], matte[:], ALU.mult)
-                nc.gpsimd.tensor_tensor(work[:], work[:], bg_sb[:], ALU.add)
-                nc.gpsimd.tensor_tensor(value[:], work[:], gains1[t // 2][:, t % 2, cols], ALU.mult)
-                nc.vector.tensor_copy(pages[t][:].indirect(list3[:, h * list_cols : (h + 1) * list_cols]), value[:])
+                    nc.vector.tensor_tensor(value[:, cols], fg[:], bg_sb[:], ALU.subtract)
+                    nc.gpsimd.tensor_tensor(work[:], value[:, cols], matte[:], ALU.mult)
+                if t < PACK - 1:
+                    nc.gpsimd.tensor_tensor(work[:], work[:], bg_sb[:], ALU.add)
+                    nc.gpsimd.tensor_tensor(value[:, cols], work[:], gain[:, cols], ALU.mult)
+                else:
+                    nc.gpsimd.tensor_tensor(value[:, cols], work[:], bg_sb[:], ALU.add)
+            if t < PACK - 1:
+                nc.vector.tensor_copy(pages[t][:].indirect(list3[:]), value[:])
+            else:
+                nc.vector.tensor_tensor(pages[t][:].indirect(list3[:]), value[:], gain, ALU.mult)
 
         wo_codes = keep.tile([P, N], U32, name="wo_codes", align_bytes=64)
-        wo_plane = scratch.tile([P, N], U8, name="wo_plane", offset=0, align_bytes=64)
+        wo_plane = keep.tile([P, N], U8, name="wo_plane", tag="value2", align_bytes=64)
         for c0, c1 in ((0, 256), (256, N)):
             nc.vector.quantize_mx(wo_codes[:, c0:c1].bitcast(FP8X4), wo_plane[:, c0:c1], wo_grouped[:, PACK * c0 : PACK * c1])
 
@@ -296,5 +309,8 @@ def tile_list_matting_patch_weave_kernel(
                     rhs=codes[:].bitcast(FP8X4), rhs_scale=plane[:], start=True, stop=True,
                 )
                 result = unit([P, width], F32, f"result{i}{n}", "first")
-                nc.scalar.copy(result[:], acc[:, 0:width])
+                if i >= len(CHUNKS) - VEC_CHUNKS and n >= VEC_FROM:
+                    nc.vector.tensor_copy(result[:], acc[:, 0:width])
+                else:
+                    nc.scalar.copy(result[:], acc[:, 0:width])
                 nc.sync.dma_start(out[rows, cols], result[:])

@@ -19,12 +19,16 @@ ACT = mybir.ActivationFunctionType
 P = 128
 PACK = 4
 QUAD = 32
+LIVE = 4
+GROUP = 16
+PASS = P * PACK
 HALF = 512
-POOL_DIFFS = 4
-FG_BANKS = (0, 1, 0, 1, 2, 3, 0, 1)
+BANKS = 8
+WORD = 4
 FIRST_PIECES = ((0, 256), (256, 256), (512, 512))
 CHUNKS = (256, 256, 512, 512, 512)
-VEC_CHUNKS, VEC_FROM = 1, 1
+INTERIOR_BANKS = (0, 4, 1)
+UNITS = PACK * S // HALF
 
 
 def tile_list_matting_patch_weave_kernel(
@@ -33,7 +37,10 @@ def tile_list_matting_patch_weave_kernel(
 ):
     nc = tc.nc
     halves = S // HALF
-    list_cols = HALF // 16
+    list_cols = HALF // GROUP
+
+    slot_bytes = WORD * HALF
+    window_bytes = WORD * T
 
     with ExitStack() as ctx:
         lists = ctx.enter_context(tc.tile_pool(name="lists", bufs=1))
@@ -44,7 +51,7 @@ def tile_list_matting_patch_weave_kernel(
         psum = ctx.enter_context(tc.psum_pool(name="psum", bufs=1))
 
         def load_list(src, name):
-            tile = lists.tile([P, S // 16], U16, name=name)
+            tile = lists.tile([P, S // GROUP], U16, name=name)
             nc.sync.dma_start(tile[:], src)
             return tile
 
@@ -53,15 +60,15 @@ def tile_list_matting_patch_weave_kernel(
             nc.vector.memset(tile[:].bitcast(I32), 0)
             return tile
 
-        def load_gain(src, pair, name):
+        def load_gain(src, pair, name, upper_queue):
             tile = ring.tile([P, 2, S], F32, name=name, tag="gain")
             rows = src.rearrange("(b u t) j -> u b t j", u=2, t=2)[pair]
             for q in (0, 2, 1, 3):
-                nc.sync.dma_start(tile[QUAD * q : QUAD * (q + 1), :, :], rows)
+                (upper_queue if q >= 2 else nc.sync).dma_start(tile[QUAD * q : QUAD * (q + 1), :, :], rows)
             return tile
 
         def load_weight(src, name, tag):
-            passes, width = src.shape[0] // 512, src.shape[1]
+            passes, width = src.shape[0] // PASS, src.shape[1]
             tile = keep.tile([P, passes, PACK, width], F32, name=name, tag=tag)
             nc.sync.dma_start(
                 tile[:].rearrange("p a i c -> p a (i c)"), src.rearrange("(a p i) c -> p a (i c)", p=P, i=PACK)
@@ -69,7 +76,7 @@ def tile_list_matting_patch_weave_kernel(
             return tile
 
         def unit(shape, dtype, name, tag):
-            return ring.tile(shape, dtype, name=name, tag=tag, bufs=9 if tag == "second" else 8, align_bytes=64)
+            return ring.tile(shape, dtype, name=name, tag=tag, bufs=UNITS + (tag == "activated"), align_bytes=64)
 
         def bank(name, number):
             return psum.tile([P, HALF], F32, name=name, tag=f"bank{number}")
@@ -77,19 +84,22 @@ def tile_list_matting_patch_weave_kernel(
         wi_plane_raw = keep.tile([P, H], U8, name="wi_plane_raw")
         nc.vector.memset(wi_plane_raw[:].bitcast(I32), 0)
         tab2_rows = keep.tile([P, T], U8, name="tab2_rows")
-        nc.vector.memset(tab2_rows[0 : P - 16, :].bitcast(I32), 0)
+        nc.vector.memset(tab2_rows[0 : P - GROUP, :].bitcast(I32), 0)
         tab_rows = keep.tile([P, T], U8, name="tab_rows")
-        nc.vector.memset(tab_rows[0 : P - 32, :].bitcast(I32), 0)
+        nc.vector.memset(tab_rows[0 : P - 2 * GROUP, :].bitcast(I32), 0)
         v2_plane = zeroed_plane(S, "v2_plane")
         wb_plane_raw = zeroed_plane(2 * H, "wb_plane_raw")
         v_planes = zeroed_plane(2 * S, "v_planes")
-        nc.gpsimd.dma_start(tab_rows[P - 32 : P, :].bitcast(I32), tab_scales.bitcast(I32).rearrange("a r t -> r a t"))
-        for q in range(4):
+        nc.gpsimd.dma_start(
+            tab_rows[P - 2 * GROUP : P, :].bitcast(I32), tab_scales.bitcast(I32).rearrange("a r t -> r a t")
+        )
+        for q in range(P // QUAD):
             nc.gpsimd.dma_start(
-                wi_plane_raw[QUAD * q : QUAD * q + 4, :].bitcast(I32), wi_scales[0, 4 * q : 4 * q + 4, :].bitcast(I32)
+                wi_plane_raw[QUAD * q : QUAD * q + LIVE, :].bitcast(I32),
+                wi_scales[0, LIVE * q : LIVE * (q + 1), :].bitcast(I32),
             )
         list2 = load_list(offs2, "list2")
-        nc.sync.dma_start(tab2_rows[P - 16 : P, :].bitcast(I32), tab2_scales[0].bitcast(I32))
+        nc.sync.dma_start(tab2_rows[P - GROUP : P, :].bitcast(I32), tab2_scales[0].bitcast(I32))
         list1 = load_list(offs, "list1")
         wi_raw = keep.tile([P, H], I32, name="wi_raw")
         nc.sync.dma_start(wi_raw[:], wi_words[0].rearrange("p c i -> p (c i)").bitcast(I32))
@@ -100,36 +110,35 @@ def tile_list_matting_patch_weave_kernel(
         nc.sync.dma_start(tab2_window[:].bitcast(I32), tab2_words[0].rearrange("p t i -> p (t i)").bitcast(I32))
         v2_rows = keep.tile([P, S], U8, name="v2_rows")
         nc.vector.tensor_copy(v2_rows[:], tab2_rows[:].indirect(list2[:]))
-        for q in range(4):
+        for q in range(P // QUAD):
             nc.scalar.dma_start(
-                v2_plane[QUAD * q : QUAD * q + 4, :].bitcast(I32),
-                v2_rows[P - 16 + 4 * q : P - 12 + 4 * q, :].bitcast(I32),
+                v2_plane[QUAD * q : QUAD * q + LIVE, :].bitcast(I32),
+                v2_rows[P - GROUP + LIVE * q : P - GROUP + LIVE * (q + 1), :].bitcast(I32),
             )
-        gains2 = [load_gain(wg2, 0, "gain2_0")]
+        gains2 = [load_gain(wg2, 0, "gain2_0", nc.scalar)]
         wf_raw = load_weight(wf, "wf_raw", "wf_raw")
         list3 = load_list(offs3, "list3")
         wb_raw = keep.tile([P, 2, 2 * H], U8, name="wb_raw")
         nc.sync.dma_start(wb_raw[:].bitcast(I32), wb_words.bitcast(I32).rearrange("a p c -> p a c"))
-        for q in range(4):
+        for q in range(P // QUAD):
             nc.sync.dma_start(
-                wb_plane_raw[QUAD * q : QUAD * q + 4, :].bitcast(I32).rearrange("p (a c) -> p a c", a=2),
-                wb_scales[:, 4 * q : 4 * q + 4, :].bitcast(I32).rearrange("a r c -> r a c"),
+                wb_plane_raw[QUAD * q : QUAD * q + LIVE, :].bitcast(I32).rearrange("p (a c) -> p a c", a=2),
+                wb_scales[:, LIVE * q : LIVE * (q + 1), :].bitcast(I32).rearrange("a r c -> r a c"),
             )
         wm_raw = load_weight(wm, "wm_raw", "wm_raw")
 
         v_rows = keep.tile([P, S], U8, name="v_rows")
         nc.vector.tensor_copy(v_rows[:], tab_rows[:].indirect(list1[:]))
         wi_codes = keep.tile([P, H], I32, name="wi_codes", align_bytes=64)
-        nc.scalar.copy(
-            wi_codes[:].bitcast(U16).rearrange("p (t m e) -> p m t e", t=PACK, e=2),
-            wi_raw[:].bitcast(U16).rearrange("p (m t e) -> p m t e", t=PACK, e=2),
+        nc.vector.tensor_copy(
+            wi_codes[:].rearrange("p (t m) -> p m t", t=PACK), wi_raw[:].rearrange("p (m t) -> p m t", t=PACK)
         )
         wi_plane = keep.tile([P, H], U8, name="wi_plane", align_bytes=64)
         nc.vector.tensor_copy(
             wi_plane[:].rearrange("p (t m) -> p m t", t=PACK), wi_plane_raw[:].rearrange("p (m t) -> p m t", t=PACK)
         )
         wb_codes = keep.tile([P, 2, 2 * H], U8, name="wb_codes", align_bytes=64)
-        nc.scalar.copy(
+        nc.vector.tensor_copy(
             wb_codes[:].bitcast(U16).rearrange("p a (t m) -> p a m t", t=PACK),
             wb_raw[:].bitcast(U16).rearrange("p a (m t) -> p a m t", t=PACK),
         )
@@ -142,10 +151,10 @@ def tile_list_matting_patch_weave_kernel(
         v2_codes = [keep.tile([P, HALF], U32, name=f"v2_codes{h}", align_bytes=64) for h in range(halves)]
         for h in range(halves):
             gather_words(v2_codes[h][:], tab2_window[:], list2, h)
-        for q in range(4):
+        for q in range(P // QUAD):
             nc.sync.dma_start(
-                v_planes[QUAD * q : QUAD * q + 4, :].bitcast(I32).rearrange("p (a c) -> p a c", a=2),
-                v_rows[P - 32 + 8 * q : P - 24 + 8 * q, :].bitcast(I32),
+                v_planes[QUAD * q : QUAD * q + LIVE, :].bitcast(I32).rearrange("p (a c) -> p a c", a=2),
+                v_rows[P - 2 * GROUP + 2 * LIVE * q : P - 2 * GROUP + 2 * LIVE * (q + 1), :].bitcast(I32),
             )
         wb_plane = wide.tile([P, 2 * H], U8, name="wb_plane", offset=0, align_bytes=64)
         nc.vector.tensor_copy(
@@ -155,57 +164,62 @@ def tile_list_matting_patch_weave_kernel(
 
         pages = []
 
-        def interior_piece(t, value, c0, width):
+        def interior_piece(number, t, value, c0, width):
             h, name = c0 // HALF, f"{t}_{c0}"
             cols_w = slice(t * P, (t + 1) * P)
             cols = slice(c0, c0 + width)
-            d = bank("d" + name, (0, 4, 1)[(halves * t + h + (0 if (t, c0) == (0, 0) else 1)) % 3])[:, 0:width]
+            d = bank("d" + name, INTERIOR_BANKS[number % len(INTERIOR_BANKS)])[:, 0:width]
             nc.tensor.matmul_mx(
                 d, lhsT=wi_codes[:, cols_w].bitcast(FP8X4), lhsT_scale=wi_plane[:, cols_w],
                 rhs=v2_codes[h][:, c0 - h * HALF : c0 - h * HALF + width].bitcast(FP8X4), rhs_scale=v2_plane[:, cols],
                 start=True, stop=True,
             )
-            lift = unit([P, width], F32, "lift" + name, "second")
+            lift = unit([P, width], F32, "lift" + name, "activated")
             nc.scalar.activation(lift[:], d, ACT.Relu, scale=slope_less_one[:, t : t + 1])
             gain = gains2[t // 2][:, t % 2, cols]
             if t == 0:
-                leaky = lift if h == 0 else scratch.tile([P, HALF], F32, name="leaky_0", offset=2 * HALF)
+                leaky = lift if h == 0 else scratch.tile([P, HALF], F32, name="leaky_0", offset=slot_bytes // 2)
                 nc.vector.tensor_tensor(leaky[:], d, lift[:], ALU.add)
             else:
                 nc.scalar.copy(value[:, cols], d)
-                leaky = scratch.tile([P, HALF], F32, name="leaky_" + name, offset=4 * HALF * h)
+                leaky = scratch.tile([P, HALF], F32, name="leaky_" + name, offset=slot_bytes * h)
                 nc.gpsimd.tensor_tensor(leaky[:], value[:, cols], lift[:], ALU.add)
             nc.gpsimd.tensor_tensor(value[:, cols], leaky[:], gain, ALU.mult)
 
         def interior_slice(t):
             if t == 1:
-                value = scratch.tile([P, S], F32, name="value2_1", offset=8 * HALF)
+                value = scratch.tile([P, S], F32, name="value2_1", offset=2 * slot_bytes)
             else:
                 value = keep.tile([P, S], F32, name=f"value2_{t}", tag=f"value{max(t - 1, 0)}", align_bytes=64)
             if t == 0:
-                for c0, width in FIRST_PIECES:
-                    interior_piece(t, value, c0, width)
+                for number, (c0, width) in enumerate(FIRST_PIECES):
+                    interior_piece(number, t, value, c0, width)
                     nc.vector.tensor_copy(
-                        pages[t][:].indirect(list4[:, c0 // 16 : (c0 + width) // 16]), value[:, c0 : c0 + width]
+                        pages[t][:].indirect(list4[:, c0 // GROUP : (c0 + width) // GROUP]), value[:, c0 : c0 + width]
                     )
             else:
                 for h in range(halves):
-                    interior_piece(t, value, h * HALF, HALF)
+                    interior_piece(len(FIRST_PIECES) + halves * (t - 1) + h, t, value, h * HALF, HALF)
                 nc.vector.tensor_copy(pages[t][:].indirect(list4[:]), value[:])
 
         pages.extend(keep.tile([P, T2], F32, name=f"page{t}") for t in (0, 1))
         interior_slice(0)
         interior_slice(1)
-        gains2.append(load_gain(wg2, 1, "gain2_1"))
-        tab_window = wide.tile([P, 2, T], U32, name="tab_window", offset=4 * T)
+        tab_window = wide.tile([P, 2, T], U32, name="tab_window", offset=window_bytes)
         nc.sync.dma_start(tab_window[:].bitcast(I32), tab_words.rearrange("a p t i -> p a (t i)").bitcast(I32))
-        v_codes = [[keep.tile([P, HALF], U32, name=f"v_codes{h}{a}", align_bytes=64) for a in range(2)] for h in range(halves)]
+        gains2.append(load_gain(wg2, 1, "gain2_1", nc.scalar))
+        v_codes = [
+            [keep.tile([P, HALF], U32, name=f"v_codes{h}{a}", align_bytes=64) for a in range(2)] for h in range(halves)
+        ]
         for h in range(halves):
             for a in range(2):
                 gather_words(v_codes[h][a][:], tab_window[:, a, :], list1, h)
-        pages.extend(wide.tile([P, T2], F32, name=f"page{t}", offset=8 * T + 4 * T2 * (t - 2)) for t in (2, 3))
+        pages.extend(
+            wide.tile([P, T2], F32, name=f"page{t}", offset=2 * window_bytes + WORD * T2 * (t - 2)) for t in (2, 3)
+        )
         interior_slice(2)
         interior_slice(3)
+
         grouped = keep.tile([P, 4, PACK * H], BF16, name="w_grouped", tag="grouped", align_bytes=64)
         for w, raw in enumerate((wf_raw, wm_raw)):
             for a in range(2):
@@ -214,30 +228,31 @@ def tile_list_matting_patch_weave_kernel(
                     raw[:, a, :, :].rearrange("p i (m t) -> p m t i", t=PACK),
                 )
         w_codes = keep.tile([P, 4 * H], U32, name="w_codes", align_bytes=64)
-        w_plane = scratch.tile([P, 4 * H], U8, name="w_plane", offset=8 * HALF, align_bytes=64)
+        w_plane = scratch.tile([P, 4 * H], U8, name="w_plane", offset=2 * slot_bytes, align_bytes=64)
         for w in range(2):
-            half = slice(2 * w * H, 2 * (w + 1) * H)
+            weight_cols = slice(2 * w * H, 2 * (w + 1) * H)
             nc.vector.quantize_mx(
-                w_codes[:, half].bitcast(FP8X4), w_plane[:, half],
+                w_codes[:, weight_cols].bitcast(FP8X4), w_plane[:, weight_cols],
                 grouped[:, 2 * w : 2 * w + 2, :].rearrange("p a x -> p (a x)"),
             )
 
-        gains1 = [load_gain(wg1, 0, "gain1_0")]
+        gains1 = [load_gain(wg1, 0, "gain1_0", nc.sync)]
         wo_raw = load_weight(wo, "wo_raw", "wf_raw")
-        gains1.append(load_gain(wg1, 1, "gain1_1"))
+        gains1.append(load_gain(wg1, 1, "gain1_1", nc.sync))
 
         wo_grouped = keep.tile([P, PACK * N], BF16, name="wo_grouped", tag="grouped", align_bytes=64)
         nc.scalar.copy(
             wo_grouped[:].rearrange("p (c n i) -> p c i n", n=4, i=PACK),
             wo_raw[:, 0, :, :].rearrange("p i (c n) -> p c i n", n=4),
         )
+
         for t in range(PACK):
             value = keep.tile([P, S], F32, name=f"value1_{t}", tag=f"value{t % 3}", align_bytes=64)
             gain = gains1[t // 2][:, t % 2, :]
             for h in range(halves):
                 cols = slice(h * HALF, (h + 1) * HALF)
                 moving_planes = [v_planes[:, a * S + h * HALF : a * S + (h + 1) * HALF] for a in range(2)]
-                mt, bg, fg = bank(f"mt{t}{h}", 4 + h), bank(f"bg{t}{h}", 6 + h), bank(f"fg{t}{h}", FG_BANKS[halves * t + h])
+                mt, bg, fg = bank(f"mt{t}{h}", 4 + h), bank(f"bg{t}{h}", 6 + h), bank(f"fg{t}{h}", 2 * (t % 2) + h)
                 for a in range(2):
                     nc.tensor.matmul_mx(
                         bg[:], lhsT=wb_codes[:, a, 2 * t * P : 2 * (t + 1) * P].bitcast(FP4X4),
@@ -257,16 +272,17 @@ def tile_list_matting_patch_weave_kernel(
                         mt[:], lhsT=w_codes[:, cols_a].bitcast(FP8X4), lhsT_scale=w_plane[:, cols_a],
                         rhs=v_codes[h][a][:].bitcast(FP8X4), rhs_scale=moving_planes[a], start=(a == 0), stop=(a == 1),
                     )
-                bg_sb = unit([P, HALF], F32, f"bg_sb{t}{h}", "first")
+                matte = unit([P, HALF], F32, f"matte{t}{h}", "activated")
+                bg_sb = unit([P, HALF], F32, f"bg_sb{t}{h}", "copied")
+                work = scratch.tile([P, HALF], F32, name=f"work1_{t}{h}", offset=slot_bytes * h)
                 nc.scalar.copy(bg_sb[:], bg[:])
-                matte = unit([P, HALF], F32, f"matte{t}{h}", "second")
-                nc.scalar.activation(matte[:], mt[:], ACT.Sigmoid)
-                work = scratch.tile([P, HALF], F32, name=f"work1_{t}{h}", offset=4 * HALF * h)
-                if halves * t + h < POOL_DIFFS:
+                if t == 0:
                     nc.scalar.copy(value[:, cols], fg[:])
+                    nc.scalar.activation(matte[:], mt[:], ACT.Sigmoid)
                     nc.gpsimd.tensor_tensor(work[:], value[:, cols], bg_sb[:], ALU.subtract)
                     nc.gpsimd.tensor_tensor(work[:], work[:], matte[:], ALU.mult)
                 else:
+                    nc.scalar.activation(matte[:], mt[:], ACT.Sigmoid)
                     nc.vector.tensor_tensor(value[:, cols], fg[:], bg_sb[:], ALU.subtract)
                     nc.gpsimd.tensor_tensor(work[:], value[:, cols], matte[:], ALU.mult)
                 if t < PACK - 1:
@@ -281,11 +297,16 @@ def tile_list_matting_patch_weave_kernel(
 
         wo_codes = keep.tile([P, N], U32, name="wo_codes", align_bytes=64)
         wo_plane = keep.tile([P, N], U8, name="wo_plane", tag="value2", align_bytes=64)
-        for c0, c1 in ((0, 256), (256, N)):
-            nc.vector.quantize_mx(wo_codes[:, c0:c1].bitcast(FP8X4), wo_plane[:, c0:c1], wo_grouped[:, PACK * c0 : PACK * c1])
+        for c0, c1 in ((0, 2 * P), (2 * P, N)):
+            nc.vector.quantize_mx(
+                wo_codes[:, c0:c1].bitcast(FP8X4), wo_plane[:, c0:c1], wo_grouped[:, PACK * c0 : PACK * c1]
+            )
 
         starts = [sum(CHUNKS[:i]) for i in range(len(CHUNKS))]
-        woven = [wide.tile([P, width, PACK], BF16, name=f"woven{i}", offset=2 * PACK * starts[i], align_bytes=64) for i, width in enumerate(CHUNKS)]
+        woven = [
+            wide.tile([P, width, PACK], BF16, name=f"woven{i}", offset=2 * PACK * starts[i], align_bytes=64)
+            for i, width in enumerate(CHUNKS)
+        ]
         for t in range(PACK - 1):
             for i, width in enumerate(CHUNKS):
                 src = pages[t][:, starts[i] : starts[i] + width]
@@ -303,13 +324,13 @@ def tile_list_matting_patch_weave_kernel(
             nc.vector.quantize_mx(codes[:].bitcast(FP8X4), plane[:], woven[i][:].rearrange("p c t -> p (c t)"))
             for n in range(N // P):
                 rows = slice(n * P, (n + 1) * P)
-                acc = bank(f"acc{i}{n}", (3 * i + n) % 8)
+                acc = bank(f"acc{i}{n}", (N // P * i + n) % BANKS)
                 nc.tensor.matmul_mx(
                     acc[:, 0:width], lhsT=wo_codes[:, rows].bitcast(FP8X4), lhsT_scale=wo_plane[:, rows],
                     rhs=codes[:].bitcast(FP8X4), rhs_scale=plane[:], start=True, stop=True,
                 )
-                result = unit([P, width], F32, f"result{i}{n}", "first")
-                if i >= len(CHUNKS) - VEC_CHUNKS and n >= VEC_FROM:
+                result = unit([P, width], F32, f"result{i}{n}", "copied")
+                if i == len(CHUNKS) - 1 and n > 0:
                     nc.vector.tensor_copy(result[:], acc[:, 0:width])
                 else:
                     nc.scalar.copy(result[:], acc[:, 0:width])

@@ -24,11 +24,15 @@ GROUP = 16
 PASS = P * PACK
 HALF = 512
 BANKS = 8
-WORD = 4
+KIB = 1024
 FIRST_PIECES = ((0, 256), (256, 256), (512, 512))
 CHUNKS = (256, 256, 512, 512, 512)
 INTERIOR_BANKS = (0, 4, 1)
-UNITS = PACK * S // HALF
+DIFF_BANKS = 5
+SUMMED_UNITS = 3
+AT_TAB2, AT_TAB, AT_GROUPED, AT_RAW, AT_CODES, AT_LIFT, AT_VALUE, AT_GAIN, AT_SLOT = (
+    0, 16 * KIB, 48 * KIB, 64 * KIB, 96 * KIB, 112 * KIB, 128 * KIB, 144 * KIB, 160 * KIB,
+)
 
 
 def tile_list_matting_patch_weave_kernel(
@@ -38,17 +42,17 @@ def tile_list_matting_patch_weave_kernel(
     nc = tc.nc
     halves = S // HALF
     list_cols = HALF // GROUP
-
-    slot_bytes = WORD * HALF
-    window_bytes = WORD * T
+    row_bytes = 4 * S
 
     with ExitStack() as ctx:
         lists = ctx.enter_context(tc.tile_pool(name="lists", bufs=1))
         keep = ctx.enter_context(tc.tile_pool(name="keep", bufs=1))
         ring = ctx.enter_context(tc.tile_pool(name="ring", bufs=2))
-        wide = ctx.enter_context(tc.tile_pool(name="wide", bufs=1))
-        scratch = ctx.enter_context(tc.tile_pool(name="scratch", bufs=1))
+        big = ctx.enter_context(tc.tile_pool(name="big", bufs=1))
         psum = ctx.enter_context(tc.psum_pool(name="psum", bufs=1))
+
+        def placed(shape, dtype, name, offset):
+            return big.tile(shape, dtype, name=name, offset=offset, align_bytes=64)
 
         def load_list(src, name):
             tile = lists.tile([P, S // GROUP], U16, name=name)
@@ -60,36 +64,35 @@ def tile_list_matting_patch_weave_kernel(
             nc.vector.memset(tile[:].bitcast(I32), 0)
             return tile
 
-        def load_gain(src, pair, name, upper_queue):
-            tile = ring.tile([P, 2, S], F32, name=name, tag="gain")
-            rows = src.rearrange("(b u t) j -> u b t j", u=2, t=2)[pair]
+        def load_gain(src, t, name):
+            tile = placed([P, S], F32, name, AT_GAIN + row_bytes * t)
+            rows = src.rearrange("(b t) j -> t b j", t=PACK)[t]
             for q in (0, 2, 1, 3):
-                (upper_queue if q >= 2 else nc.sync).dma_start(tile[QUAD * q : QUAD * (q + 1), :, :], rows)
+                nc.sync.dma_start(tile[QUAD * q : QUAD * (q + 1), :], rows)
             return tile
 
-        def load_weight(src, name, tag):
-            passes, width = src.shape[0] // PASS, src.shape[1]
-            tile = keep.tile([P, passes, PACK, width], F32, name=name, tag=tag)
+        def load_pass(src, a, name, offset):
+            width = src.shape[1]
+            tile = placed([P, PACK, width], F32, name, offset)
             nc.sync.dma_start(
-                tile[:].rearrange("p a i c -> p a (i c)"), src.rearrange("(a p i) c -> p a (i c)", p=P, i=PACK)
+                tile[:].rearrange("p i c -> p (i c)"),
+                src[a * PASS : (a + 1) * PASS, :].rearrange("(p i) c -> p (i c)", i=PACK),
             )
             return tile
-
-        def unit(shape, dtype, name, tag):
-            return ring.tile(shape, dtype, name=name, tag=tag, bufs=UNITS + (tag == "activated"), align_bytes=64)
 
         def bank(name, number):
             return psum.tile([P, HALF], F32, name=name, tag=f"bank{number}")
 
-        wi_plane_raw = keep.tile([P, H], U8, name="wi_plane_raw")
-        nc.vector.memset(wi_plane_raw[:].bitcast(I32), 0)
+        def slot(width, name):
+            return placed([P, width], F32, name, AT_SLOT)
+
+        wi_plane_raw = zeroed_plane(H, "wi_plane_raw")
+        wb_plane_raw = zeroed_plane(2 * H, "wb_plane_raw")
         tab2_rows = keep.tile([P, T], U8, name="tab2_rows")
         nc.vector.memset(tab2_rows[0 : P - GROUP, :].bitcast(I32), 0)
         tab_rows = keep.tile([P, T], U8, name="tab_rows")
         nc.vector.memset(tab_rows[0 : P - 2 * GROUP, :].bitcast(I32), 0)
         v2_plane = zeroed_plane(S, "v2_plane")
-        wb_plane_raw = zeroed_plane(2 * H, "wb_plane_raw")
-        v_planes = zeroed_plane(2 * S, "v_planes")
         nc.gpsimd.dma_start(
             tab_rows[P - 2 * GROUP : P, :].bitcast(I32), tab_scales.bitcast(I32).rearrange("a r t -> r a t")
         )
@@ -103,11 +106,32 @@ def tile_list_matting_patch_weave_kernel(
         list1 = load_list(offs, "list1")
         wi_raw = keep.tile([P, H], I32, name="wi_raw")
         nc.sync.dma_start(wi_raw[:], wi_words[0].rearrange("p c i -> p (c i)").bitcast(I32))
-        list4 = load_list(offs4, "list4")
         slopes = keep.tile([P, PACK], F32, name="slopes")
         nc.sync.dma_start(slopes[:], slope.rearrange("(p t) -> p t", t=PACK))
-        tab2_window = wide.tile([P, T], U32, name="tab2_window", offset=0)
+        list4 = load_list(offs4, "list4")
+        list3 = load_list(offs3, "list3")
+        tab2_window = placed([P, T], U32, "tab2_window", AT_TAB2)
         nc.sync.dma_start(tab2_window[:].bitcast(I32), tab2_words[0].rearrange("p t i -> p (t i)").bitcast(I32))
+        gains2 = [load_gain(wg2, 0, "gain2_0")]
+        wb_raw = keep.tile([P, 2, 2 * H], U8, name="wb_raw")
+        nc.sync.dma_start(wb_raw[:].bitcast(I32), wb_words.bitcast(I32).rearrange("a p c -> p a c"))
+        gains2.append(load_gain(wg2, 1, "gain2_1"))
+        for q in range(P // QUAD):
+            nc.sync.dma_start(
+                wb_plane_raw[QUAD * q : QUAD * q + LIVE, :].bitcast(I32).rearrange("p (a c) -> p a c", a=2),
+                wb_scales[:, LIVE * q : LIVE * (q + 1), :].bitcast(I32).rearrange("a r c -> r a c"),
+            )
+        wf_raw = [load_pass(wf, a, f"wf_raw{a}", AT_RAW + 8 * KIB * a) for a in range(2)]
+        tab_window = placed([P, 2, T], U32, "tab_window", AT_TAB)
+        nc.sync.dma_start(tab_window[:].bitcast(I32), tab_words.rearrange("a p t i -> p a (t i)").bitcast(I32))
+        wm_raw = [load_pass(wm, a, f"wm_raw{a}", AT_RAW + 8 * KIB * (2 + a)) for a in range(2)]
+        gains2.extend(load_gain(wg2, t, f"gain2_{t}") for t in (2, 3))
+
+        warm = keep.tile([P, 1], F32, name="warm")
+        nc.scalar.activation(warm[:], slopes[:, 0:1], ACT.Sigmoid)
+        slope_less_one = keep.tile([P, PACK], F32, name="slope_less_one")
+        nc.scalar.activation(slope_less_one[:], slopes[:], ACT.Identity, bias=-1.0)
+
         v2_rows = keep.tile([P, S], U8, name="v2_rows")
         nc.vector.tensor_copy(v2_rows[:], tab2_rows[:].indirect(list2[:]))
         for q in range(P // QUAD):
@@ -115,18 +139,6 @@ def tile_list_matting_patch_weave_kernel(
                 v2_plane[QUAD * q : QUAD * q + LIVE, :].bitcast(I32),
                 v2_rows[P - GROUP + LIVE * q : P - GROUP + LIVE * (q + 1), :].bitcast(I32),
             )
-        gains2 = [load_gain(wg2, 0, "gain2_0", nc.scalar)]
-        wf_raw = load_weight(wf, "wf_raw", "wf_raw")
-        list3 = load_list(offs3, "list3")
-        wb_raw = keep.tile([P, 2, 2 * H], U8, name="wb_raw")
-        nc.sync.dma_start(wb_raw[:].bitcast(I32), wb_words.bitcast(I32).rearrange("a p c -> p a c"))
-        for q in range(P // QUAD):
-            nc.sync.dma_start(
-                wb_plane_raw[QUAD * q : QUAD * q + LIVE, :].bitcast(I32).rearrange("p (a c) -> p a c", a=2),
-                wb_scales[:, LIVE * q : LIVE * (q + 1), :].bitcast(I32).rearrange("a r c -> r a c"),
-            )
-        wm_raw = load_weight(wm, "wm_raw", "wm_raw")
-
         v_rows = keep.tile([P, S], U8, name="v_rows")
         nc.vector.tensor_copy(v_rows[:], tab_rows[:].indirect(list1[:]))
         wi_codes = keep.tile([P, H], I32, name="wi_codes", align_bytes=64)
@@ -137,13 +149,6 @@ def tile_list_matting_patch_weave_kernel(
         nc.vector.tensor_copy(
             wi_plane[:].rearrange("p (t m) -> p m t", t=PACK), wi_plane_raw[:].rearrange("p (m t) -> p m t", t=PACK)
         )
-        wb_codes = keep.tile([P, 2, 2 * H], U8, name="wb_codes", align_bytes=64)
-        nc.vector.tensor_copy(
-            wb_codes[:].bitcast(U16).rearrange("p a (t m) -> p a m t", t=PACK),
-            wb_raw[:].bitcast(U16).rearrange("p a (m t) -> p a m t", t=PACK),
-        )
-        slope_less_one = keep.tile([P, PACK], F32, name="slope_less_one")
-        nc.scalar.activation(slope_less_one[:], slopes[:], ACT.Identity, bias=-1.0)
 
         def gather_words(dst, window, lst, h):
             nc.vector.tensor_copy(dst, window.indirect(lst[:, h * list_cols : (h + 1) * list_cols]))
@@ -151,152 +156,174 @@ def tile_list_matting_patch_weave_kernel(
         v2_codes = [keep.tile([P, HALF], U32, name=f"v2_codes{h}", align_bytes=64) for h in range(halves)]
         for h in range(halves):
             gather_words(v2_codes[h][:], tab2_window[:], list2, h)
+        wb_codes = keep.tile([P, 2, 2 * H], U8, name="wb_codes", align_bytes=64)
+        nc.vector.tensor_copy(
+            wb_codes[:].bitcast(U16).rearrange("p a (t m) -> p a m t", t=PACK),
+            wb_raw[:].bitcast(U16).rearrange("p a (m t) -> p a m t", t=PACK),
+        )
+
+        pages = [keep.tile([P, T2], F32, name=f"page{t}") for t in range(2)]
+        pages.extend(placed([P, T2], F32, f"page{t}", AT_GROUPED + 8 * KIB * (t - 2) - 4 * KIB) for t in (2, 3))
+
+        def scatter(t, lst, value, c0, width):
+            offsets = lst[:] if width == S else lst[:, c0 // GROUP : (c0 + width) // GROUP]
+            nc.vector.tensor_copy(pages[t][:].indirect(offsets), value[:, c0 : c0 + width])
+
+        def interior_product(number, t, c0, width):
+            h = c0 // HALF
+            cols_w = slice(t * P, (t + 1) * P)
+            d = bank(f"d{t}_{c0}", INTERIOR_BANKS[number % len(INTERIOR_BANKS)])[:, 0:width]
+            nc.tensor.matmul_mx(
+                d, lhsT=wi_codes[:, cols_w].bitcast(FP8X4), lhsT_scale=wi_plane[:, cols_w],
+                rhs=v2_codes[h][:, c0 - h * HALF : c0 - h * HALF + width].bitcast(FP8X4),
+                rhs_scale=v2_plane[:, c0 : c0 + width], start=True, stop=True,
+            )
+            return d
+
+        def leak_and_gain(t, value, lift, c0, width):
+            cols = slice(c0, c0 + width)
+            work = slot(width, f"leaky{t}_{c0}") if t < 3 else placed([P, S], F32, "leaky3", AT_LIFT + row_bytes)
+            nc.gpsimd.tensor_tensor(work[:], value[:, cols], lift[:, cols], ALU.add)
+            nc.gpsimd.tensor_tensor(value[:, cols], work[:], gains2[t][:, cols], ALU.mult)
+
+        def interior_slice(t):
+            value = placed([P, S], F32, f"value2_{t}", AT_VALUE + row_bytes * t)
+            lift = placed([P, S], F32, f"lift{t}", AT_LIFT + row_bytes * t)
+            pieces = FIRST_PIECES if t == 0 else ((0, HALF), (HALF, HALF))
+            first = 0 if t == 0 else len(FIRST_PIECES) + halves * (t - 1)
+            for number, (c0, width) in enumerate(pieces):
+                cols = slice(c0, c0 + width)
+                d = interior_product(first + number, t, c0, width)
+                nc.scalar.activation(lift[:, cols], d, ACT.Relu, scale=slope_less_one[:, t : t + 1])
+                if width < HALF:
+                    nc.vector.tensor_tensor(lift[:, cols], d, lift[:, cols], ALU.add)
+                    nc.gpsimd.tensor_tensor(value[:, cols], lift[:, cols], gains2[t][:, cols], ALU.mult)
+                else:
+                    nc.scalar.copy(value[:, cols], d)
+                    if t < 2:
+                        leak_and_gain(t, value, lift, c0, width)
+                if t < 2:
+                    scatter(t, list4, value, c0, width)
+            if t >= 2:
+                leak_and_gain(t, value, lift, 0, S)
+            return value
+
+        values2 = [interior_slice(t) for t in range(PACK)]
+        v_planes = placed([P, 2 * S], U8, "v_planes", AT_LIFT + 2 * KIB)
+        nc.gpsimd.memset(v_planes[:].bitcast(I32), 0)
         for q in range(P // QUAD):
             nc.sync.dma_start(
                 v_planes[QUAD * q : QUAD * q + LIVE, :].bitcast(I32).rearrange("p (a c) -> p a c", a=2),
                 v_rows[P - 2 * GROUP + 2 * LIVE * q : P - 2 * GROUP + 2 * LIVE * (q + 1), :].bitcast(I32),
             )
-        wb_plane = wide.tile([P, 2 * H], U8, name="wb_plane", offset=0, align_bytes=64)
+        wb_plane = placed([P, 2 * H], U8, "wb_plane", AT_VALUE + row_bytes + 2 * KIB)
         nc.vector.tensor_copy(
             wb_plane[:].rearrange("p (a t m) -> p a m t", a=2, t=PACK),
             wb_plane_raw[:].rearrange("p (a m t) -> p a m t", a=2, t=PACK),
         )
 
-        pages = []
+        grouped = [placed([P, 2, PACK * H], BF16, f"grouped{w}", AT_GROUPED + 8 * KIB * (1 - w)) for w in range(2)]
+        for w, raw in enumerate((wf_raw, wm_raw)):
+            for a in range(2):
+                nc.scalar.activation(
+                    grouped[w][:, a, :].rearrange("p (t m i) -> p m t i", t=PACK, i=PACK),
+                    raw[a][:].rearrange("p i (m t) -> p m t i", t=PACK),
+                    ACT.Copy, scale=(-1.0, 1.0)[w],
+                )
+        w_codes = [placed([P, 2 * H], U32, f"w_codes{w}", AT_CODES + 6 * KIB + 4 * KIB * w) for w in range(2)]
+        w_plane = [placed([P, 2 * H], U8, f"w_plane{w}", AT_VALUE + row_bytes + KIB * w) for w in range(2)]
 
-        def interior_piece(number, t, value, c0, width):
-            h, name = c0 // HALF, f"{t}_{c0}"
-            cols_w = slice(t * P, (t + 1) * P)
-            cols = slice(c0, c0 + width)
-            d = bank("d" + name, INTERIOR_BANKS[number % len(INTERIOR_BANKS)])[:, 0:width]
-            nc.tensor.matmul_mx(
-                d, lhsT=wi_codes[:, cols_w].bitcast(FP8X4), lhsT_scale=wi_plane[:, cols_w],
-                rhs=v2_codes[h][:, c0 - h * HALF : c0 - h * HALF + width].bitcast(FP8X4), rhs_scale=v2_plane[:, cols],
-                start=True, stop=True,
+        def quantise_weight(w):
+            nc.vector.quantize_mx(
+                w_codes[w][:].bitcast(FP8X4), w_plane[w][:], grouped[w][:].rearrange("p a x -> p (a x)")
             )
-            lift = unit([P, width], F32, "lift" + name, "activated")
-            nc.scalar.activation(lift[:], d, ACT.Relu, scale=slope_less_one[:, t : t + 1])
-            gain = gains2[t // 2][:, t % 2, cols]
-            if t == 0:
-                leaky = lift if h == 0 else scratch.tile([P, HALF], F32, name="leaky_0", offset=slot_bytes // 2)
-                nc.vector.tensor_tensor(leaky[:], d, lift[:], ALU.add)
-            else:
-                nc.scalar.copy(value[:, cols], d)
-                leaky = scratch.tile([P, HALF], F32, name="leaky_" + name, offset=slot_bytes * h)
-                nc.gpsimd.tensor_tensor(leaky[:], value[:, cols], lift[:], ALU.add)
-            nc.gpsimd.tensor_tensor(value[:, cols], leaky[:], gain, ALU.mult)
 
-        def interior_slice(t):
-            if t == 1:
-                value = scratch.tile([P, S], F32, name="value2_1", offset=2 * slot_bytes)
-            else:
-                value = keep.tile([P, S], F32, name=f"value2_{t}", tag=f"value{max(t - 1, 0)}", align_bytes=64)
-            if t == 0:
-                for number, (c0, width) in enumerate(FIRST_PIECES):
-                    interior_piece(number, t, value, c0, width)
-                    nc.vector.tensor_copy(
-                        pages[t][:].indirect(list4[:, c0 // GROUP : (c0 + width) // GROUP]), value[:, c0 : c0 + width]
-                    )
-            else:
-                for h in range(halves):
-                    interior_piece(len(FIRST_PIECES) + halves * (t - 1) + h, t, value, h * HALF, HALF)
-                nc.vector.tensor_copy(pages[t][:].indirect(list4[:]), value[:])
-
-        pages.extend(keep.tile([P, T2], F32, name=f"page{t}") for t in (0, 1))
-        interior_slice(0)
-        interior_slice(1)
-        tab_window = wide.tile([P, 2, T], U32, name="tab_window", offset=window_bytes)
-        nc.sync.dma_start(tab_window[:].bitcast(I32), tab_words.rearrange("a p t i -> p a (t i)").bitcast(I32))
-        gains2.append(load_gain(wg2, 1, "gain2_1", nc.scalar))
+        quantise_weight(0)
+        code_places = ((4 * KIB, 14 * KIB), (2 * KIB, 0))
         v_codes = [
-            [keep.tile([P, HALF], U32, name=f"v_codes{h}{a}", align_bytes=64) for a in range(2)] for h in range(halves)
+            [placed([P, HALF], U32, f"v_codes{h}{a}", AT_CODES + code_places[h][a]) for a in range(2)]
+            for h in range(halves)
         ]
         for h in range(halves):
             for a in range(2):
                 gather_words(v_codes[h][a][:], tab_window[:, a, :], list1, h)
-        pages.extend(
-            wide.tile([P, T2], F32, name=f"page{t}", offset=2 * window_bytes + WORD * T2 * (t - 2)) for t in (2, 3)
-        )
-        interior_slice(2)
-        interior_slice(3)
+        quantise_weight(1)
+        for t in (2, 3):
+            scatter(t, list4, values2[t], 0, S)
 
-        grouped = keep.tile([P, 4, PACK * H], BF16, name="w_grouped", tag="grouped", align_bytes=64)
-        for w, raw in enumerate((wf_raw, wm_raw)):
-            for a in range(2):
-                nc.scalar.copy(
-                    grouped[:, 2 * w + a, :].rearrange("p (t m i) -> p m t i", t=PACK, i=PACK),
-                    raw[:, a, :, :].rearrange("p i (m t) -> p m t i", t=PACK),
+        gains1 = [load_gain(wg1, t, f"gain1_{t}") for t in (0, 1)]
+        wo_raw = load_pass(wo, 0, "wo_raw", AT_LIFT + 2 * row_bytes)
+        gains1.extend(load_gain(wg1, t, f"gain1_{t}") for t in (2, 3))
+
+        def passes(acc, t, h, weights):
+            steps = [(weight, a) for weight in weights for a in range(2)]
+            for number, (weight, a) in enumerate(steps):
+                cols_a = slice(a * H + t * P, a * H + (t + 1) * P)
+                if weight == "b":
+                    codes, plane = wb_codes[:, a, 2 * t * P : 2 * (t + 1) * P].bitcast(FP4X4), wb_plane[:, cols_a]
+                else:
+                    w = "fm".index(weight)
+                    codes, plane = w_codes[w][:, cols_a].bitcast(FP8X4), w_plane[w][:, cols_a]
+                nc.tensor.matmul_mx(
+                    acc[:], lhsT=codes, lhsT_scale=plane, rhs=v_codes[h][a][:].bitcast(FP8X4),
+                    rhs_scale=v_planes[:, a * S + h * HALF : a * S + (h + 1) * HALF],
+                    start=(number == 0), stop=(number == len(steps) - 1),
                 )
-        w_codes = keep.tile([P, 4 * H], U32, name="w_codes", align_bytes=64)
-        w_plane = scratch.tile([P, 4 * H], U8, name="w_plane", offset=2 * slot_bytes, align_bytes=64)
-        for w in range(2):
-            weight_cols = slice(2 * w * H, 2 * (w + 1) * H)
-            nc.vector.quantize_mx(
-                w_codes[:, weight_cols].bitcast(FP8X4), w_plane[:, weight_cols],
-                grouped[:, 2 * w : 2 * w + 2, :].rearrange("p a x -> p (a x)"),
-            )
 
-        gains1 = [load_gain(wg1, 0, "gain1_0", nc.sync)]
-        wo_raw = load_weight(wo, "wo_raw", "wf_raw")
-        gains1.append(load_gain(wg1, 1, "gain1_1", nc.sync))
-
-        wo_grouped = keep.tile([P, PACK * N], BF16, name="wo_grouped", tag="grouped", align_bytes=64)
-        nc.scalar.copy(
-            wo_grouped[:].rearrange("p (c n i) -> p c i n", n=4, i=PACK),
-            wo_raw[:, 0, :, :].rearrange("p i (c n) -> p c i n", n=4),
-        )
+        def blend(t, value, matte, back, c0, width):
+            cols = slice(c0, c0 + width)
+            work = slot(width, f"blend{t}_{c0}")
+            nc.gpsimd.tensor_tensor(work[:], value[:, cols], matte[:, cols], ALU.mult)
+            if t < PACK - 1:
+                nc.gpsimd.tensor_tensor(work[:], back[:, cols], work[:], ALU.subtract)
+                nc.gpsimd.tensor_tensor(value[:, cols], work[:], gains1[t][:, cols], ALU.mult)
+            else:
+                nc.gpsimd.tensor_tensor(value[:, cols], back[:, cols], work[:], ALU.subtract)
 
         for t in range(PACK):
-            value = keep.tile([P, S], F32, name=f"value1_{t}", tag=f"value{t % 3}", align_bytes=64)
-            gain = gains1[t // 2][:, t % 2, :]
+            value = placed([P, S], F32, f"value1_{t}", AT_TAB2 + row_bytes * t)
+            back = placed([P, S], F32, f"back{t}", AT_RAW + row_bytes * t)
+            matte = placed([P, S], F32, f"matte{t}", AT_RAW + row_bytes * (PACK + t))
             for h in range(halves):
+                number = halves * t + h
                 cols = slice(h * HALF, (h + 1) * HALF)
-                moving_planes = [v_planes[:, a * S + h * HALF : a * S + (h + 1) * HALF] for a in range(2)]
-                mt, bg, fg = bank(f"mt{t}{h}", 4 + h), bank(f"bg{t}{h}", 6 + h), bank(f"fg{t}{h}", 2 * (t % 2) + h)
-                for a in range(2):
-                    nc.tensor.matmul_mx(
-                        bg[:], lhsT=wb_codes[:, a, 2 * t * P : 2 * (t + 1) * P].bitcast(FP4X4),
-                        lhsT_scale=wb_plane[:, a * H + t * P : a * H + (t + 1) * P],
-                        rhs=v_codes[h][a][:].bitcast(FP8X4), rhs_scale=moving_planes[a],
-                        start=(a == 0), stop=(a == 1),
-                    )
-                for a in range(2):
-                    cols_a = slice(a * H + t * P, a * H + (t + 1) * P)
-                    nc.tensor.matmul_mx(
-                        fg[:], lhsT=w_codes[:, cols_a].bitcast(FP8X4), lhsT_scale=w_plane[:, cols_a],
-                        rhs=v_codes[h][a][:].bitcast(FP8X4), rhs_scale=moving_planes[a], start=(a == 0), stop=(a == 1),
-                    )
-                for a in range(2):
-                    cols_a = slice((2 + a) * H + t * P, (2 + a) * H + (t + 1) * P)
-                    nc.tensor.matmul_mx(
-                        mt[:], lhsT=w_codes[:, cols_a].bitcast(FP8X4), lhsT_scale=w_plane[:, cols_a],
-                        rhs=v_codes[h][a][:].bitcast(FP8X4), rhs_scale=moving_planes[a], start=(a == 0), stop=(a == 1),
-                    )
-                matte = unit([P, HALF], F32, f"matte{t}{h}", "activated")
-                bg_sb = unit([P, HALF], F32, f"bg_sb{t}{h}", "copied")
-                work = scratch.tile([P, HALF], F32, name=f"work1_{t}{h}", offset=slot_bytes * h)
-                nc.scalar.copy(bg_sb[:], bg[:])
+                diff = bank(f"diff{number}", number % DIFF_BANKS)
+                bg = bank(f"bg{number}", DIFF_BANKS + h)
+                mt = bank(f"mt{number}", BANKS - 1)
+                if number < SUMMED_UNITS:
+                    passes(diff, t, h, "bf")
+                    nc.scalar.copy(value[:, cols], diff[:])
+                    passes(mt, t, h, "m")
+                    nc.scalar.activation(matte[:, cols], mt[:], ACT.Sigmoid)
+                    passes(bg, t, h, "b")
+                    nc.scalar.copy(back[:, cols], bg[:])
+                else:
+                    passes(bg, t, h, "b")
+                    nc.scalar.copy(back[:, cols], bg[:])
+                    passes(mt, t, h, "m")
+                    nc.scalar.activation(matte[:, cols], mt[:], ACT.Sigmoid)
+                    passes(diff, t, h, "f")
+                    if number == SUMMED_UNITS:
+                        nc.scalar.copy(value[:, cols], diff[:])
+                        nc.gpsimd.tensor_tensor(value[:, cols], value[:, cols], back[:, cols], ALU.add)
+                    else:
+                        nc.vector.tensor_tensor(value[:, cols], diff[:], back[:, cols], ALU.add)
                 if t == 0:
-                    nc.scalar.copy(value[:, cols], fg[:])
-                    nc.scalar.activation(matte[:], mt[:], ACT.Sigmoid)
-                    nc.gpsimd.tensor_tensor(work[:], value[:, cols], bg_sb[:], ALU.subtract)
-                    nc.gpsimd.tensor_tensor(work[:], work[:], matte[:], ALU.mult)
-                else:
-                    nc.scalar.activation(matte[:], mt[:], ACT.Sigmoid)
-                    nc.vector.tensor_tensor(value[:, cols], fg[:], bg_sb[:], ALU.subtract)
-                    nc.gpsimd.tensor_tensor(work[:], value[:, cols], matte[:], ALU.mult)
-                if t < PACK - 1:
-                    nc.gpsimd.tensor_tensor(work[:], work[:], bg_sb[:], ALU.add)
-                    nc.gpsimd.tensor_tensor(value[:, cols], work[:], gain[:, cols], ALU.mult)
-                else:
-                    nc.gpsimd.tensor_tensor(value[:, cols], work[:], bg_sb[:], ALU.add)
+                    blend(t, value, matte, back, h * HALF, HALF)
+            if t > 0:
+                blend(t, value, matte, back, 0, S)
             if t < PACK - 1:
-                nc.vector.tensor_copy(pages[t][:].indirect(list3[:]), value[:])
+                scatter(t, list3, value, 0, S)
             else:
-                nc.vector.tensor_tensor(pages[t][:].indirect(list3[:]), value[:], gain, ALU.mult)
+                nc.vector.tensor_tensor(pages[t][:].indirect(list3[:]), value[:], gains1[t][:], ALU.mult)
 
+        wo_grouped = placed([P, PACK * N], BF16, "wo_grouped", AT_VALUE + row_bytes)
+        nc.scalar.copy(
+            wo_grouped[:].rearrange("p (c n i) -> p c i n", n=4, i=PACK),
+            wo_raw[:].rearrange("p i (c n) -> p c i n", n=4),
+        )
         wo_codes = keep.tile([P, N], U32, name="wo_codes", align_bytes=64)
-        wo_plane = keep.tile([P, N], U8, name="wo_plane", tag="value2", align_bytes=64)
+        wo_plane = placed([P, N], U8, "wo_plane", AT_TAB2 + 2 * row_bytes)
         for c0, c1 in ((0, 2 * P), (2 * P, N)):
             nc.vector.quantize_mx(
                 wo_codes[:, c0:c1].bitcast(FP8X4), wo_plane[:, c0:c1], wo_grouped[:, PACK * c0 : PACK * c1]
@@ -304,7 +331,7 @@ def tile_list_matting_patch_weave_kernel(
 
         starts = [sum(CHUNKS[:i]) for i in range(len(CHUNKS))]
         woven = [
-            wide.tile([P, width, PACK], BF16, name=f"woven{i}", offset=2 * PACK * starts[i], align_bytes=64)
+            placed([P, width, PACK], BF16, f"woven{i}", AT_CODES + 2 * PACK * starts[i])
             for i, width in enumerate(CHUNKS)
         ]
         for t in range(PACK - 1):
@@ -329,7 +356,7 @@ def tile_list_matting_patch_weave_kernel(
                     acc[:, 0:width], lhsT=wo_codes[:, rows].bitcast(FP8X4), lhsT_scale=wo_plane[:, rows],
                     rhs=codes[:].bitcast(FP8X4), rhs_scale=plane[:], start=True, stop=True,
                 )
-                result = unit([P, width], F32, f"result{i}{n}", "copied")
+                result = placed([P, width], F32, f"result{i}{n}", AT_TAB + 4 * (N // P * starts[i] + n * width))
                 if i == len(CHUNKS) - 1 and n > 0:
                     nc.vector.tensor_copy(result[:], acc[:, 0:width])
                 else:

@@ -26,9 +26,10 @@ HALF = 512
 BANKS = 8
 KIB = 1024
 FIRST_PIECES = ((0, 256), (256, 256), (512, 512))
-CHUNKS = (256, 256, 512, 512, 512)
+PIECE = 256
+STORE_GROUPS = ((0,), (1,), (2, 3), (4, 5), (6,), (7,))
 INTERIOR_BANKS = (0, 4, 1)
-DIFF_BANKS = 5
+TURN_BANKS = 4
 SUMMED_UNITS = 3
 AT_TAB2, AT_TAB, AT_GROUPED, AT_RAW, AT_CODES, AT_LIFT, AT_VALUE, AT_GAIN, AT_SLOT = (
     0, 16 * KIB, 48 * KIB, 64 * KIB, 96 * KIB, 112 * KIB, 128 * KIB, 144 * KIB, 160 * KIB,
@@ -47,7 +48,6 @@ def tile_list_matting_patch_weave_kernel(
     with ExitStack() as ctx:
         lists = ctx.enter_context(tc.tile_pool(name="lists", bufs=1))
         keep = ctx.enter_context(tc.tile_pool(name="keep", bufs=1))
-        ring = ctx.enter_context(tc.tile_pool(name="ring", bufs=2))
         big = ctx.enter_context(tc.tile_pool(name="big", bufs=1))
         psum = ctx.enter_context(tc.psum_pool(name="psum", bufs=1))
 
@@ -84,15 +84,16 @@ def tile_list_matting_patch_weave_kernel(
             return psum.tile([P, HALF], F32, name=name, tag=f"bank{number}")
 
         def slot(width, name):
-            return placed([P, width], F32, name, AT_SLOT)
+            return placed([P, width], F32, name, AT_SLOT + 3 * KIB)
 
         wi_plane_raw = zeroed_plane(H, "wi_plane_raw")
         wb_plane_raw = zeroed_plane(2 * H, "wb_plane_raw")
         tab2_rows = keep.tile([P, T], U8, name="tab2_rows")
         nc.vector.memset(tab2_rows[0 : P - GROUP, :].bitcast(I32), 0)
-        tab_rows = keep.tile([P, T], U8, name="tab_rows")
+        tab_rows = placed([P, T], U8, "tab_rows", AT_SLOT + 2 * row_bytes)
         nc.vector.memset(tab_rows[0 : P - 2 * GROUP, :].bitcast(I32), 0)
         v2_plane = zeroed_plane(S, "v2_plane")
+        v_planes = zeroed_plane(2 * S, "v_planes")
         nc.gpsimd.dma_start(
             tab_rows[P - 2 * GROUP : P, :].bitcast(I32), tab_scales.bitcast(I32).rearrange("a r t -> r a t")
         )
@@ -101,21 +102,25 @@ def tile_list_matting_patch_weave_kernel(
                 wi_plane_raw[QUAD * q : QUAD * q + LIVE, :].bitcast(I32),
                 wi_scales[0, LIVE * q : LIVE * (q + 1), :].bitcast(I32),
             )
+        slopes = keep.tile([P, PACK], F32, name="slopes")
+        nc.gpsimd.dma_start(slopes[:], slope.rearrange("(p t) -> p t", t=PACK))
+        wi_raw = keep.tile([P, H], I32, name="wi_raw")
+        nc.scalar.dma_start(wi_raw[:], wi_words[0].rearrange("p c i -> p (c i)").bitcast(I32))
+        first_gains = placed([P, 2, S], F32, "gain2_01", AT_GAIN)
+        first_rows = wg2.rearrange("(b u t) j -> u b t j", u=2, t=2)[0]
+        for q in (2, 3):
+            nc.scalar.dma_start(first_gains[QUAD * q : QUAD * (q + 1), :, :], first_rows)
         list2 = load_list(offs2, "list2")
         nc.sync.dma_start(tab2_rows[P - GROUP : P, :].bitcast(I32), tab2_scales[0].bitcast(I32))
         list1 = load_list(offs, "list1")
-        wi_raw = keep.tile([P, H], I32, name="wi_raw")
-        nc.sync.dma_start(wi_raw[:], wi_words[0].rearrange("p c i -> p (c i)").bitcast(I32))
-        slopes = keep.tile([P, PACK], F32, name="slopes")
-        nc.sync.dma_start(slopes[:], slope.rearrange("(p t) -> p t", t=PACK))
         list4 = load_list(offs4, "list4")
-        list3 = load_list(offs3, "list3")
-        tab2_window = placed([P, T], U32, "tab2_window", AT_TAB2)
-        nc.sync.dma_start(tab2_window[:].bitcast(I32), tab2_words[0].rearrange("p t i -> p (t i)").bitcast(I32))
-        gains2 = [load_gain(wg2, 0, "gain2_0")]
         wb_raw = keep.tile([P, 2, 2 * H], U8, name="wb_raw")
         nc.sync.dma_start(wb_raw[:].bitcast(I32), wb_words.bitcast(I32).rearrange("a p c -> p a c"))
-        gains2.append(load_gain(wg2, 1, "gain2_1"))
+        tab2_window = placed([P, T], U32, "tab2_window", AT_TAB2)
+        nc.sync.dma_start(tab2_window[:].bitcast(I32), tab2_words[0].rearrange("p t i -> p (t i)").bitcast(I32))
+        for q in (0, 1):
+            nc.sync.dma_start(first_gains[QUAD * q : QUAD * (q + 1), :, :], first_rows)
+        gains2 = [first_gains[:, t, :] for t in range(2)]
         for q in range(P // QUAD):
             nc.sync.dma_start(
                 wb_plane_raw[QUAD * q : QUAD * q + LIVE, :].bitcast(I32).rearrange("p (a c) -> p a c", a=2),
@@ -124,11 +129,19 @@ def tile_list_matting_patch_weave_kernel(
         wf_raw = [load_pass(wf, a, f"wf_raw{a}", AT_RAW + 8 * KIB * a) for a in range(2)]
         tab_window = placed([P, 2, T], U32, "tab_window", AT_TAB)
         nc.sync.dma_start(tab_window[:].bitcast(I32), tab_words.rearrange("a p t i -> p a (t i)").bitcast(I32))
-        wm_raw = [load_pass(wm, a, f"wm_raw{a}", AT_RAW + 8 * KIB * (2 + a)) for a in range(2)]
+        wm_both = placed([P, 2, PACK, H], F32, "wm_raw", AT_RAW + 16 * KIB)
+        for a in range(2):
+            nc.sync.dma_start(
+                wm_both[:, a, :, :].rearrange("p i c -> p (i c)"),
+                wm[a * PASS : (a + 1) * PASS, :].rearrange("(p i) c -> p (i c)", i=PACK),
+            )
+        wm_raw = [wm_both[:, a, :, :] for a in range(2)]
         gains2.extend(load_gain(wg2, t, f"gain2_{t}") for t in (2, 3))
+        list3 = load_list(offs3, "list3")
 
         warm = keep.tile([P, 1], F32, name="warm")
-        nc.scalar.activation(warm[:], slopes[:, 0:1], ACT.Sigmoid)
+        nc.vector.memset(warm[:], 0.0)
+        nc.scalar.activation(warm[:], warm[:], ACT.Sigmoid)
         slope_less_one = keep.tile([P, PACK], F32, name="slope_less_one")
         nc.scalar.activation(slope_less_one[:], slopes[:], ACT.Identity, bias=-1.0)
 
@@ -141,11 +154,16 @@ def tile_list_matting_patch_weave_kernel(
             )
         v_rows = keep.tile([P, S], U8, name="v_rows")
         nc.vector.tensor_copy(v_rows[:], tab_rows[:].indirect(list1[:]))
+        for q in range(P // QUAD):
+            nc.gpsimd.dma_start(
+                v_planes[QUAD * q : QUAD * q + LIVE, :].bitcast(I32).rearrange("p (a c) -> p a c", a=2),
+                v_rows[P - 2 * GROUP + 2 * LIVE * q : P - 2 * GROUP + 2 * LIVE * (q + 1), :].bitcast(I32),
+            )
         wi_codes = keep.tile([P, H], I32, name="wi_codes", align_bytes=64)
         nc.vector.tensor_copy(
             wi_codes[:].rearrange("p (t m) -> p m t", t=PACK), wi_raw[:].rearrange("p (m t) -> p m t", t=PACK)
         )
-        wi_plane = keep.tile([P, H], U8, name="wi_plane", align_bytes=64)
+        wi_plane = placed([P, H], U8, "wi_plane", AT_SLOT + 2 * row_bytes + 2 * KIB)
         nc.vector.tensor_copy(
             wi_plane[:].rearrange("p (t m) -> p m t", t=PACK), wi_plane_raw[:].rearrange("p (m t) -> p m t", t=PACK)
         )
@@ -153,10 +171,10 @@ def tile_list_matting_patch_weave_kernel(
         def gather_words(dst, window, lst, h):
             nc.vector.tensor_copy(dst, window.indirect(lst[:, h * list_cols : (h + 1) * list_cols]))
 
-        v2_codes = [keep.tile([P, HALF], U32, name=f"v2_codes{h}", align_bytes=64) for h in range(halves)]
+        v2_codes = [placed([P, HALF], U32, f"v2_codes{h}", AT_SLOT + 2 * row_bytes + 4 * KIB * h) for h in range(halves)]
         for h in range(halves):
             gather_words(v2_codes[h][:], tab2_window[:], list2, h)
-        wb_codes = keep.tile([P, 2, 2 * H], U8, name="wb_codes", align_bytes=64)
+        wb_codes = placed([P, 2, 2 * H], U8, "wb_codes", AT_TAB2)
         nc.vector.tensor_copy(
             wb_codes[:].bitcast(U16).rearrange("p a (t m) -> p a m t", t=PACK),
             wb_raw[:].bitcast(U16).rearrange("p a (m t) -> p a m t", t=PACK),
@@ -182,7 +200,7 @@ def tile_list_matting_patch_weave_kernel(
 
         def leak_and_gain(t, value, lift, c0, width):
             cols = slice(c0, c0 + width)
-            work = slot(width, f"leaky{t}_{c0}") if t < 3 else placed([P, S], F32, "leaky3", AT_LIFT + row_bytes)
+            work = slot(width, f"leaky{t}_{c0}") if t < 2 else placed([P, S], F32, f"leaky{t}", AT_SLOT + row_bytes * (t - 2))
             nc.gpsimd.tensor_tensor(work[:], value[:, cols], lift[:, cols], ALU.add)
             nc.gpsimd.tensor_tensor(value[:, cols], work[:], gains2[t][:, cols], ALU.mult)
 
@@ -209,13 +227,7 @@ def tile_list_matting_patch_weave_kernel(
             return value
 
         values2 = [interior_slice(t) for t in range(PACK)]
-        v_planes = placed([P, 2 * S], U8, "v_planes", AT_LIFT + 2 * KIB)
-        nc.gpsimd.memset(v_planes[:].bitcast(I32), 0)
-        for q in range(P // QUAD):
-            nc.sync.dma_start(
-                v_planes[QUAD * q : QUAD * q + LIVE, :].bitcast(I32).rearrange("p (a c) -> p a c", a=2),
-                v_rows[P - 2 * GROUP + 2 * LIVE * q : P - 2 * GROUP + 2 * LIVE * (q + 1), :].bitcast(I32),
-            )
+
         wb_plane = placed([P, 2 * H], U8, "wb_plane", AT_VALUE + row_bytes + 2 * KIB)
         nc.vector.tensor_copy(
             wb_plane[:].rearrange("p (a t m) -> p a m t", a=2, t=PACK),
@@ -227,10 +239,10 @@ def tile_list_matting_patch_weave_kernel(
             for a in range(2):
                 nc.scalar.activation(
                     grouped[w][:, a, :].rearrange("p (t m i) -> p m t i", t=PACK, i=PACK),
-                    raw[a][:].rearrange("p i (m t) -> p m t i", t=PACK),
+                    raw[a][:, :, :].rearrange("p i (m t) -> p m t i", t=PACK),
                     ACT.Copy, scale=(-1.0, 1.0)[w],
                 )
-        w_codes = [placed([P, 2 * H], U32, f"w_codes{w}", AT_CODES + 6 * KIB + 4 * KIB * w) for w in range(2)]
+        w_codes = [placed([P, 2 * H], U32, f"w_codes{w}", AT_CODES + 8 * KIB + 4 * KIB * w) for w in range(2)]
         w_plane = [placed([P, 2 * H], U8, f"w_plane{w}", AT_VALUE + row_bytes + KIB * w) for w in range(2)]
 
         def quantise_weight(w):
@@ -239,7 +251,7 @@ def tile_list_matting_patch_weave_kernel(
             )
 
         quantise_weight(0)
-        code_places = ((4 * KIB, 14 * KIB), (2 * KIB, 0))
+        code_places = ((2 * KIB, 6 * KIB), (4 * KIB, 0))
         v_codes = [
             [placed([P, HALF], U32, f"v_codes{h}{a}", AT_CODES + code_places[h][a]) for a in range(2)]
             for h in range(halves)
@@ -272,25 +284,39 @@ def tile_list_matting_patch_weave_kernel(
 
         def blend(t, value, matte, back, c0, width):
             cols = slice(c0, c0 + width)
-            work = slot(width, f"blend{t}_{c0}")
-            nc.gpsimd.tensor_tensor(work[:], value[:, cols], matte[:, cols], ALU.mult)
+            work = placed([P, width], F32, f"blend{t}_{c0}", AT_SLOT + 3 * KIB)
+            if halves * t + c0 // HALF == SUMMED_UNITS:
+                nc.gpsimd.tensor_tensor(work[:], value[:, cols], back[:, cols], ALU.add)
+                nc.gpsimd.tensor_tensor(work[:], work[:], matte[:, cols], ALU.mult)
+            else:
+                nc.gpsimd.tensor_tensor(work[:], value[:, cols], matte[:, cols], ALU.mult)
             if t < PACK - 1:
                 nc.gpsimd.tensor_tensor(work[:], back[:, cols], work[:], ALU.subtract)
                 nc.gpsimd.tensor_tensor(value[:, cols], work[:], gains1[t][:, cols], ALU.mult)
             else:
                 nc.gpsimd.tensor_tensor(value[:, cols], back[:, cols], work[:], ALU.subtract)
 
+        turns = []
+
+        def next_bank(name):
+            turns.append(name)
+            return bank(name, (len(turns) - 1) % TURN_BANKS)
+
         for t in range(PACK):
-            value = placed([P, S], F32, f"value1_{t}", AT_TAB2 + row_bytes * t)
-            back = placed([P, S], F32, f"back{t}", AT_RAW + row_bytes * t)
-            matte = placed([P, S], F32, f"matte{t}", AT_RAW + row_bytes * (PACK + t))
+            region = AT_RAW + 16 * KIB if t < 2 else AT_TAB2 + 2 * KIB
+            value = placed([P, S], F32, f"value1_{t}", region + row_bytes * (t % 2))
+            back = placed([P, S], F32, f"back{t}", region + row_bytes * (2 + t % 2))
+            matte = placed([P, S], F32, f"matte{t}", AT_RAW + row_bytes * t)
             for h in range(halves):
                 number = halves * t + h
                 cols = slice(h * HALF, (h + 1) * HALF)
-                diff = bank(f"diff{number}", number % DIFF_BANKS)
-                bg = bank(f"bg{number}", DIFF_BANKS + h)
-                mt = bank(f"mt{number}", BANKS - 1)
+                if 1 <= number <= BANKS - TURN_BANKS:
+                    mt = bank(f"mt{number}", TURN_BANKS + number - 1)
                 if number < SUMMED_UNITS:
+                    diff = next_bank(f"diff{number}")
+                    if number == 0:
+                        mt = next_bank(f"mt{number}")
+                    bg = next_bank(f"bg{number}")
                     passes(diff, t, h, "bf")
                     nc.scalar.copy(value[:, cols], diff[:])
                     passes(mt, t, h, "m")
@@ -298,6 +324,10 @@ def tile_list_matting_patch_weave_kernel(
                     passes(bg, t, h, "b")
                     nc.scalar.copy(back[:, cols], bg[:])
                 else:
+                    bg = next_bank(f"bg{number}")
+                    if number > BANKS - TURN_BANKS:
+                        mt = next_bank(f"mt{number}")
+                    diff = next_bank(f"diff{number}") if number == SUMMED_UNITS else bank(f"diff{number}", number)
                     passes(bg, t, h, "b")
                     nc.scalar.copy(back[:, cols], bg[:])
                     passes(mt, t, h, "m")
@@ -305,12 +335,11 @@ def tile_list_matting_patch_weave_kernel(
                     passes(diff, t, h, "f")
                     if number == SUMMED_UNITS:
                         nc.scalar.copy(value[:, cols], diff[:])
-                        nc.gpsimd.tensor_tensor(value[:, cols], value[:, cols], back[:, cols], ALU.add)
                     else:
                         nc.vector.tensor_tensor(value[:, cols], diff[:], back[:, cols], ALU.add)
-                if t == 0:
+                if t < 2:
                     blend(t, value, matte, back, h * HALF, HALF)
-            if t > 0:
+            if t >= 2:
                 blend(t, value, matte, back, 0, S)
             if t < PACK - 1:
                 scatter(t, list3, value, 0, S)
@@ -323,41 +352,51 @@ def tile_list_matting_patch_weave_kernel(
             wo_raw[:].rearrange("p i (c n) -> p c i n", n=4),
         )
         wo_codes = keep.tile([P, N], U32, name="wo_codes", align_bytes=64)
-        wo_plane = placed([P, N], U8, "wo_plane", AT_TAB2 + 2 * row_bytes)
+        wo_plane = placed([P, N], U8, "wo_plane", AT_TAB2 + 2 * KIB)
         for c0, c1 in ((0, 2 * P), (2 * P, N)):
             nc.vector.quantize_mx(
                 wo_codes[:, c0:c1].bitcast(FP8X4), wo_plane[:, c0:c1], wo_grouped[:, PACK * c0 : PACK * c1]
             )
 
-        starts = [sum(CHUNKS[:i]) for i in range(len(CHUNKS))]
         woven = [
-            placed([P, width, PACK], BF16, f"woven{i}", AT_CODES + 2 * PACK * starts[i])
-            for i, width in enumerate(CHUNKS)
+            placed([P, PIECE, PACK], BF16, f"woven{i}", AT_CODES + KIB + 2 * PACK * PIECE * i)
+            for i in range(T2 // PIECE)
         ]
         for t in range(PACK - 1):
-            for i, width in enumerate(CHUNKS):
-                src = pages[t][:, starts[i] : starts[i] + width]
+            for i, tile in enumerate(woven):
+                src = pages[t][:, i * PIECE : (i + 1) * PIECE]
                 if t < 2:
-                    nc.scalar.copy(woven[i][:, :, t], src)
+                    nc.scalar.copy(tile[:, :, t], src)
                 else:
-                    nc.scalar.copy(woven[i][:, :, 2:4], src.unsqueeze(2).to_broadcast([P, width, 2]))
-        for i, width in enumerate(CHUNKS):
-            cols = slice(starts[i], starts[i] + width)
-            last = ring.tile([P, width], BF16, name=f"last{i}", tag="last")
-            nc.vector.tensor_copy(last[:], pages[3][:, cols])
-            nc.vector.tensor_copy(woven[i][:, :, 3], last[:])
-            codes = ring.tile([P, width], U32, name=f"page_codes{i}", tag="page_codes", align_bytes=64)
-            plane = ring.tile([P, width], U8, name=f"page_plane{i}", tag="page_plane", align_bytes=64)
-            nc.vector.quantize_mx(codes[:].bitcast(FP8X4), plane[:], woven[i][:].rearrange("p c t -> p (c t)"))
+                    nc.scalar.copy(tile[:, :, 2:4], src.unsqueeze(2).to_broadcast([P, PIECE, 2]))
+        banks_used = 0
+        for group in STORE_GROUPS:
+            width = PIECE * len(group)
+            cols = slice(group[0] * PIECE, group[0] * PIECE + width)
+            quantised = []
+            for i in group:
+                src = pages[3][:, i * PIECE : (i + 1) * PIECE]
+                if i >= 2:
+                    last = placed([P, PIECE], BF16, f"last{i}", AT_CODES + KIB + 2 * PACK * PIECE * (i - 2))
+                    nc.vector.tensor_copy(last[:], src)
+                    src = last[:]
+                nc.vector.tensor_copy(woven[i][:, :, 3], src)
+                codes = keep.tile([P, PIECE], U32, name=f"page_codes{i}", align_bytes=64)
+                plane = keep.tile([P, PIECE], U8, name=f"page_plane{i}", align_bytes=64)
+                nc.vector.quantize_mx(codes[:].bitcast(FP8X4), plane[:], woven[i][:].rearrange("p c t -> p (c t)"))
+                quantised.append((codes, plane))
             for n in range(N // P):
                 rows = slice(n * P, (n + 1) * P)
-                acc = bank(f"acc{i}{n}", (N // P * i + n) % BANKS)
-                nc.tensor.matmul_mx(
-                    acc[:, 0:width], lhsT=wo_codes[:, rows].bitcast(FP8X4), lhsT_scale=wo_plane[:, rows],
-                    rhs=codes[:].bitcast(FP8X4), rhs_scale=plane[:], start=True, stop=True,
-                )
-                result = placed([P, width], F32, f"result{i}{n}", AT_TAB + 4 * (N // P * starts[i] + n * width))
-                if i == len(CHUNKS) - 1 and n > 0:
+                acc = bank(f"acc{group[0]}{n}", banks_used % BANKS)
+                banks_used = banks_used + 1
+                for j, (codes, plane) in enumerate(quantised):
+                    nc.tensor.matmul_mx(
+                        acc[:, j * PIECE : (j + 1) * PIECE], lhsT=wo_codes[:, rows].bitcast(FP8X4),
+                        lhsT_scale=wo_plane[:, rows], rhs=codes[:].bitcast(FP8X4), rhs_scale=plane[:],
+                        start=True, stop=True,
+                    )
+                result = placed([P, width], F32, f"result{group[0]}{n}", AT_TAB + 4 * (N // P * cols.start + n * width))
+                if group[0] == T2 // PIECE - 1:
                     nc.vector.tensor_copy(result[:], acc[:, 0:width])
                 else:
                     nc.scalar.copy(result[:], acc[:, 0:width])

@@ -26,10 +26,8 @@ HALF = 512
 BANKS = 8
 KIB = 1024
 FIRST_PIECES = ((0, 256), (256, 256), (512, 512))
-PIECE = 256
-STORE_GROUPS = ((0,), (1,), (2, 3), (4, 5), (6,), (7,))
-INTERIOR_BANKS = (0, 4, 1)
-TURN_BANKS = 4
+CHUNKS = (256, 256, 512, 512, 512)
+TURN_BANKS = 3
 SUMMED_UNITS = 3
 AT_TAB2, AT_TAB, AT_GROUPED, AT_RAW, AT_CODES, AT_LIFT, AT_VALUE, AT_GAIN, AT_SLOT = (
     0, 16 * KIB, 48 * KIB, 64 * KIB, 96 * KIB, 112 * KIB, 128 * KIB, 144 * KIB, 160 * KIB,
@@ -48,6 +46,7 @@ def tile_list_matting_patch_weave_kernel(
     with ExitStack() as ctx:
         lists = ctx.enter_context(tc.tile_pool(name="lists", bufs=1))
         keep = ctx.enter_context(tc.tile_pool(name="keep", bufs=1))
+        ring = ctx.enter_context(tc.tile_pool(name="ring", bufs=2))
         big = ctx.enter_context(tc.tile_pool(name="big", bufs=1))
         psum = ctx.enter_context(tc.psum_pool(name="psum", bufs=1))
 
@@ -121,12 +120,12 @@ def tile_list_matting_patch_weave_kernel(
         for q in (0, 1):
             nc.sync.dma_start(first_gains[QUAD * q : QUAD * (q + 1), :, :], first_rows)
         gains2 = [first_gains[:, t, :] for t in range(2)]
+        wf_raw = [load_pass(wf, a, f"wf_raw{a}", AT_RAW + 8 * KIB * a) for a in range(2)]
         for q in range(P // QUAD):
             nc.sync.dma_start(
                 wb_plane_raw[QUAD * q : QUAD * q + LIVE, :].bitcast(I32).rearrange("p (a c) -> p a c", a=2),
                 wb_scales[:, LIVE * q : LIVE * (q + 1), :].bitcast(I32).rearrange("a r c -> r a c"),
             )
-        wf_raw = [load_pass(wf, a, f"wf_raw{a}", AT_RAW + 8 * KIB * a) for a in range(2)]
         tab_window = placed([P, 2, T], U32, "tab_window", AT_TAB)
         nc.sync.dma_start(tab_window[:].bitcast(I32), tab_words.rearrange("a p t i -> p a (t i)").bitcast(I32))
         wm_both = placed([P, 2, PACK, H], F32, "wm_raw", AT_RAW + 16 * KIB)
@@ -155,7 +154,7 @@ def tile_list_matting_patch_weave_kernel(
         v_rows = keep.tile([P, S], U8, name="v_rows")
         nc.vector.tensor_copy(v_rows[:], tab_rows[:].indirect(list1[:]))
         for q in range(P // QUAD):
-            nc.gpsimd.dma_start(
+            nc.scalar.dma_start(
                 v_planes[QUAD * q : QUAD * q + LIVE, :].bitcast(I32).rearrange("p (a c) -> p a c", a=2),
                 v_rows[P - 2 * GROUP + 2 * LIVE * q : P - 2 * GROUP + 2 * LIVE * (q + 1), :].bitcast(I32),
             )
@@ -190,7 +189,7 @@ def tile_list_matting_patch_weave_kernel(
         def interior_product(number, t, c0, width):
             h = c0 // HALF
             cols_w = slice(t * P, (t + 1) * P)
-            d = bank(f"d{t}_{c0}", INTERIOR_BANKS[number % len(INTERIOR_BANKS)])[:, 0:width]
+            d = bank(f"d{t}_{c0}", min(number, len(FIRST_PIECES) - 1))[:, 0:width]
             nc.tensor.matmul_mx(
                 d, lhsT=wi_codes[:, cols_w].bitcast(FP8X4), lhsT_scale=wi_plane[:, cols_w],
                 rhs=v2_codes[h][:, c0 - h * HALF : c0 - h * HALF + width].bitcast(FP8X4),
@@ -214,8 +213,9 @@ def tile_list_matting_patch_weave_kernel(
                 d = interior_product(first + number, t, c0, width)
                 nc.scalar.activation(lift[:, cols], d, ACT.Relu, scale=slope_less_one[:, t : t + 1])
                 if width < HALF:
-                    nc.vector.tensor_tensor(lift[:, cols], d, lift[:, cols], ALU.add)
-                    nc.gpsimd.tensor_tensor(value[:, cols], lift[:, cols], gains2[t][:, cols], ALU.mult)
+                    leaky = placed([P, width], F32, f"leaky{t}_{c0}", AT_SLOT + 3 * KIB + 4 * c0)
+                    nc.vector.tensor_tensor(leaky[:], d, lift[:, cols], ALU.add)
+                    nc.gpsimd.tensor_tensor(value[:, cols], leaky[:], gains2[t][:, cols], ALU.mult)
                 else:
                     nc.scalar.copy(value[:, cols], d)
                     if t < 2:
@@ -242,7 +242,7 @@ def tile_list_matting_patch_weave_kernel(
                     raw[a][:, :, :].rearrange("p i (m t) -> p m t i", t=PACK),
                     ACT.Copy, scale=(-1.0, 1.0)[w],
                 )
-        w_codes = [placed([P, 2 * H], U32, f"w_codes{w}", AT_CODES + 8 * KIB + 4 * KIB * w) for w in range(2)]
+        w_codes = [placed([P, 2 * H], U32, f"w_codes{w}", AT_CODES + 6 * KIB + 4 * KIB * w) for w in range(2)]
         w_plane = [placed([P, 2 * H], U8, f"w_plane{w}", AT_VALUE + row_bytes + KIB * w) for w in range(2)]
 
         def quantise_weight(w):
@@ -251,7 +251,7 @@ def tile_list_matting_patch_weave_kernel(
             )
 
         quantise_weight(0)
-        code_places = ((2 * KIB, 6 * KIB), (4 * KIB, 0))
+        code_places = ((4 * KIB, 14 * KIB), (2 * KIB, 0))
         v_codes = [
             [placed([P, HALF], U32, f"v_codes{h}{a}", AT_CODES + code_places[h][a]) for a in range(2)]
             for h in range(halves)
@@ -284,12 +284,8 @@ def tile_list_matting_patch_weave_kernel(
 
         def blend(t, value, matte, back, c0, width):
             cols = slice(c0, c0 + width)
-            work = placed([P, width], F32, f"blend{t}_{c0}", AT_SLOT + 3 * KIB)
-            if halves * t + c0 // HALF == SUMMED_UNITS:
-                nc.gpsimd.tensor_tensor(work[:], value[:, cols], back[:, cols], ALU.add)
-                nc.gpsimd.tensor_tensor(work[:], work[:], matte[:, cols], ALU.mult)
-            else:
-                nc.gpsimd.tensor_tensor(work[:], value[:, cols], matte[:, cols], ALU.mult)
+            work = placed([P, width], F32, f"blend{t}_{c0}", AT_SLOT + 3 * KIB + 4 * c0)
+            nc.gpsimd.tensor_tensor(work[:], value[:, cols], matte[:, cols], ALU.mult)
             if t < PACK - 1:
                 nc.gpsimd.tensor_tensor(work[:], back[:, cols], work[:], ALU.subtract)
                 nc.gpsimd.tensor_tensor(value[:, cols], work[:], gains1[t][:, cols], ALU.mult)
@@ -327,16 +323,13 @@ def tile_list_matting_patch_weave_kernel(
                     bg = next_bank(f"bg{number}")
                     if number > BANKS - TURN_BANKS:
                         mt = next_bank(f"mt{number}")
-                    diff = next_bank(f"diff{number}") if number == SUMMED_UNITS else bank(f"diff{number}", number)
+                    diff = bank(f"diff{number}", number)
                     passes(bg, t, h, "b")
                     nc.scalar.copy(back[:, cols], bg[:])
                     passes(mt, t, h, "m")
                     nc.scalar.activation(matte[:, cols], mt[:], ACT.Sigmoid)
                     passes(diff, t, h, "f")
-                    if number == SUMMED_UNITS:
-                        nc.scalar.copy(value[:, cols], diff[:])
-                    else:
-                        nc.vector.tensor_tensor(value[:, cols], diff[:], back[:, cols], ALU.add)
+                    nc.vector.tensor_tensor(value[:, cols], diff[:], back[:, cols], ALU.add)
                 if t < 2:
                     blend(t, value, matte, back, h * HALF, HALF)
             if t >= 2:
@@ -358,45 +351,35 @@ def tile_list_matting_patch_weave_kernel(
                 wo_codes[:, c0:c1].bitcast(FP8X4), wo_plane[:, c0:c1], wo_grouped[:, PACK * c0 : PACK * c1]
             )
 
+        starts = [sum(CHUNKS[:i]) for i in range(len(CHUNKS))]
         woven = [
-            placed([P, PIECE, PACK], BF16, f"woven{i}", AT_CODES + KIB + 2 * PACK * PIECE * i)
-            for i in range(T2 // PIECE)
+            placed([P, width, PACK], BF16, f"woven{i}", AT_CODES + 2 * PACK * starts[i])
+            for i, width in enumerate(CHUNKS)
         ]
         for t in range(PACK - 1):
-            for i, tile in enumerate(woven):
-                src = pages[t][:, i * PIECE : (i + 1) * PIECE]
+            for i, width in enumerate(CHUNKS):
+                src = pages[t][:, starts[i] : starts[i] + width]
                 if t < 2:
-                    nc.scalar.copy(tile[:, :, t], src)
+                    nc.scalar.copy(woven[i][:, :, t], src)
                 else:
-                    nc.scalar.copy(tile[:, :, 2:4], src.unsqueeze(2).to_broadcast([P, PIECE, 2]))
-        banks_used = 0
-        for group in STORE_GROUPS:
-            width = PIECE * len(group)
-            cols = slice(group[0] * PIECE, group[0] * PIECE + width)
-            quantised = []
-            for i in group:
-                src = pages[3][:, i * PIECE : (i + 1) * PIECE]
-                if i >= 2:
-                    last = placed([P, PIECE], BF16, f"last{i}", AT_CODES + KIB + 2 * PACK * PIECE * (i - 2))
-                    nc.vector.tensor_copy(last[:], src)
-                    src = last[:]
-                nc.vector.tensor_copy(woven[i][:, :, 3], src)
-                codes = keep.tile([P, PIECE], U32, name=f"page_codes{i}", align_bytes=64)
-                plane = keep.tile([P, PIECE], U8, name=f"page_plane{i}", align_bytes=64)
-                nc.vector.quantize_mx(codes[:].bitcast(FP8X4), plane[:], woven[i][:].rearrange("p c t -> p (c t)"))
-                quantised.append((codes, plane))
+                    nc.scalar.copy(woven[i][:, :, 2:4], src.unsqueeze(2).to_broadcast([P, width, 2]))
+        for i, width in enumerate(CHUNKS):
+            cols = slice(starts[i], starts[i] + width)
+            last = ring.tile([P, width], BF16, name=f"last{i}", tag="last")
+            nc.vector.tensor_copy(last[:], pages[3][:, cols])
+            nc.vector.tensor_copy(woven[i][:, :, 3], last[:])
+            codes = ring.tile([P, width], U32, name=f"page_codes{i}", tag="page_codes", align_bytes=64)
+            plane = ring.tile([P, width], U8, name=f"page_plane{i}", tag="page_plane", align_bytes=64)
+            nc.vector.quantize_mx(codes[:].bitcast(FP8X4), plane[:], woven[i][:].rearrange("p c t -> p (c t)"))
             for n in range(N // P):
                 rows = slice(n * P, (n + 1) * P)
-                acc = bank(f"acc{group[0]}{n}", banks_used % BANKS)
-                banks_used = banks_used + 1
-                for j, (codes, plane) in enumerate(quantised):
-                    nc.tensor.matmul_mx(
-                        acc[:, j * PIECE : (j + 1) * PIECE], lhsT=wo_codes[:, rows].bitcast(FP8X4),
-                        lhsT_scale=wo_plane[:, rows], rhs=codes[:].bitcast(FP8X4), rhs_scale=plane[:],
-                        start=True, stop=True,
-                    )
-                result = placed([P, width], F32, f"result{group[0]}{n}", AT_TAB + 4 * (N // P * cols.start + n * width))
-                if group[0] == T2 // PIECE - 1:
+                acc = bank(f"acc{i}{n}", (N // P * i + n) % BANKS)
+                nc.tensor.matmul_mx(
+                    acc[:, 0:width], lhsT=wo_codes[:, rows].bitcast(FP8X4), lhsT_scale=wo_plane[:, rows],
+                    rhs=codes[:].bitcast(FP8X4), rhs_scale=plane[:], start=True, stop=True,
+                )
+                result = placed([P, width], F32, f"result{i}{n}", AT_TAB + 4 * (N // P * starts[i] + n * width))
+                if i == len(CHUNKS) - 1 and n > 0:
                     nc.vector.tensor_copy(result[:], acc[:, 0:width])
                 else:
                     nc.scalar.copy(result[:], acc[:, 0:width])

@@ -27,6 +27,8 @@ BANKS = 8
 KIB = 1024
 FIRST_PIECES = ((0, 256), (256, 256), (512, 512))
 CHUNKS = (256, 256, 512, 512, 512)
+PIECE = 256
+INTERIOR_BANKS = (0, 4, 1)
 TURN_BANKS = 3
 SUMMED_UNITS = 3
 AT_TAB2, AT_TAB, AT_GROUPED, AT_RAW, AT_CODES, AT_LIFT, AT_VALUE, AT_GAIN, AT_SLOT = (
@@ -46,7 +48,6 @@ def tile_list_matting_patch_weave_kernel(
     with ExitStack() as ctx:
         lists = ctx.enter_context(tc.tile_pool(name="lists", bufs=1))
         keep = ctx.enter_context(tc.tile_pool(name="keep", bufs=1))
-        ring = ctx.enter_context(tc.tile_pool(name="ring", bufs=2))
         big = ctx.enter_context(tc.tile_pool(name="big", bufs=1))
         psum = ctx.enter_context(tc.psum_pool(name="psum", bufs=1))
 
@@ -58,10 +59,15 @@ def tile_list_matting_patch_weave_kernel(
             nc.sync.dma_start(tile[:], src)
             return tile
 
-        def zeroed_plane(width, name):
-            tile = keep.tile([P, width], U8, name=name, align_bytes=64)
+        def zeroed_planes(width, name):
+            tile = keep.tile([P, width + 4], U8, name=name, align_bytes=64)
             nc.vector.memset(tile[:].bitcast(I32), 0)
             return tile
+
+        def clear_rows(tile, rows):
+            words = tile[0:rows, :].bitcast(I32)
+            nc.vector.memset(words[:, 0 : T // 4 - 1], 0)
+            nc.vector.memset(words[:, T // 4 - 1 : T // 4], 0)
 
         def load_gain(src, t, name):
             tile = placed([P, S], F32, name, AT_GAIN + row_bytes * t)
@@ -85,14 +91,14 @@ def tile_list_matting_patch_weave_kernel(
         def slot(width, name):
             return placed([P, width], F32, name, AT_SLOT + 3 * KIB)
 
-        wi_plane_raw = zeroed_plane(H, "wi_plane_raw")
-        wb_plane_raw = zeroed_plane(2 * H, "wb_plane_raw")
+        raw_planes = zeroed_planes(3 * H, "raw_planes")
+        wi_plane_raw, wb_plane_raw = raw_planes[:, 0:H], raw_planes[:, H : 3 * H]
         tab2_rows = keep.tile([P, T], U8, name="tab2_rows")
-        nc.vector.memset(tab2_rows[0 : P - GROUP, :].bitcast(I32), 0)
+        clear_rows(tab2_rows, P - GROUP)
         tab_rows = placed([P, T], U8, "tab_rows", AT_SLOT + 2 * row_bytes)
-        nc.vector.memset(tab_rows[0 : P - 2 * GROUP, :].bitcast(I32), 0)
-        v2_plane = zeroed_plane(S, "v2_plane")
-        v_planes = zeroed_plane(2 * S, "v_planes")
+        clear_rows(tab_rows, P - 2 * GROUP)
+        moved_planes = zeroed_planes(3 * S, "moved_planes")
+        v2_plane, v_planes = moved_planes[:, 0:S], moved_planes[:, S : 3 * S]
         nc.gpsimd.dma_start(
             tab_rows[P - 2 * GROUP : P, :].bitcast(I32), tab_scales.bitcast(I32).rearrange("a r t -> r a t")
         )
@@ -128,19 +134,10 @@ def tile_list_matting_patch_weave_kernel(
             )
         tab_window = placed([P, 2, T], U32, "tab_window", AT_TAB)
         nc.sync.dma_start(tab_window[:].bitcast(I32), tab_words.rearrange("a p t i -> p a (t i)").bitcast(I32))
-        wm_both = placed([P, 2, PACK, H], F32, "wm_raw", AT_RAW + 16 * KIB)
-        for a in range(2):
-            nc.sync.dma_start(
-                wm_both[:, a, :, :].rearrange("p i c -> p (i c)"),
-                wm[a * PASS : (a + 1) * PASS, :].rearrange("(p i) c -> p (i c)", i=PACK),
-            )
-        wm_raw = [wm_both[:, a, :, :] for a in range(2)]
+        wm_raw = [load_pass(wm, a, f"wm_raw{a}", AT_RAW + 8 * KIB * (2 + a)) for a in range(2)]
         gains2.extend(load_gain(wg2, t, f"gain2_{t}") for t in (2, 3))
         list3 = load_list(offs3, "list3")
 
-        warm = keep.tile([P, 1], F32, name="warm")
-        nc.vector.memset(warm[:], 0.0)
-        nc.scalar.activation(warm[:], warm[:], ACT.Sigmoid)
         slope_less_one = keep.tile([P, PACK], F32, name="slope_less_one")
         nc.scalar.activation(slope_less_one[:], slopes[:], ACT.Identity, bias=-1.0)
 
@@ -164,7 +161,7 @@ def tile_list_matting_patch_weave_kernel(
         )
         wi_plane = placed([P, H], U8, "wi_plane", AT_SLOT + 2 * row_bytes + 2 * KIB)
         nc.vector.tensor_copy(
-            wi_plane[:].rearrange("p (t m) -> p m t", t=PACK), wi_plane_raw[:].rearrange("p (m t) -> p m t", t=PACK)
+            wi_plane[:].rearrange("p (t m) -> p m t", t=PACK), wi_plane_raw.rearrange("p (m t) -> p m t", t=PACK)
         )
 
         def gather_words(dst, window, lst, h):
@@ -189,7 +186,7 @@ def tile_list_matting_patch_weave_kernel(
         def interior_product(number, t, c0, width):
             h = c0 // HALF
             cols_w = slice(t * P, (t + 1) * P)
-            d = bank(f"d{t}_{c0}", min(number, len(FIRST_PIECES) - 1))[:, 0:width]
+            d = bank(f"d{t}_{c0}", INTERIOR_BANKS[number % len(INTERIOR_BANKS)])[:, 0:width]
             nc.tensor.matmul_mx(
                 d, lhsT=wi_codes[:, cols_w].bitcast(FP8X4), lhsT_scale=wi_plane[:, cols_w],
                 rhs=v2_codes[h][:, c0 - h * HALF : c0 - h * HALF + width].bitcast(FP8X4),
@@ -231,7 +228,7 @@ def tile_list_matting_patch_weave_kernel(
         wb_plane = placed([P, 2 * H], U8, "wb_plane", AT_VALUE + row_bytes + 2 * KIB)
         nc.vector.tensor_copy(
             wb_plane[:].rearrange("p (a t m) -> p a m t", a=2, t=PACK),
-            wb_plane_raw[:].rearrange("p (a m t) -> p a m t", a=2, t=PACK),
+            wb_plane_raw.rearrange("p (a m t) -> p a m t", a=2, t=PACK),
         )
 
         grouped = [placed([P, 2, PACK * H], BF16, f"grouped{w}", AT_GROUPED + 8 * KIB * (1 - w)) for w in range(2)]
@@ -299,9 +296,9 @@ def tile_list_matting_patch_weave_kernel(
             return bank(name, (len(turns) - 1) % TURN_BANKS)
 
         for t in range(PACK):
-            region = AT_RAW + 16 * KIB if t < 2 else AT_TAB2 + 2 * KIB
-            value = placed([P, S], F32, f"value1_{t}", region + row_bytes * (t % 2))
-            back = placed([P, S], F32, f"back{t}", region + row_bytes * (2 + t % 2))
+            region = AT_RAW + 8 * KIB * (3 - t) if t < 2 else AT_TAB2 + 2 * KIB + 8 * KIB * (t - 2)
+            value = placed([P, S], F32, f"value1_{t}", region)
+            back = placed([P, S], F32, f"back{t}", region + row_bytes)
             matte = placed([P, S], F32, f"matte{t}", AT_RAW + row_bytes * t)
             for h in range(halves):
                 number = halves * t + h
@@ -365,12 +362,20 @@ def tile_list_matting_patch_weave_kernel(
                     nc.scalar.copy(woven[i][:, :, 2:4], src.unsqueeze(2).to_broadcast([P, width, 2]))
         for i, width in enumerate(CHUNKS):
             cols = slice(starts[i], starts[i] + width)
-            last = ring.tile([P, width], BF16, name=f"last{i}", tag="last")
-            nc.vector.tensor_copy(last[:], pages[3][:, cols])
-            nc.vector.tensor_copy(woven[i][:, :, 3], last[:])
-            codes = ring.tile([P, width], U32, name=f"page_codes{i}", tag="page_codes", align_bytes=64)
-            plane = ring.tile([P, width], U8, name=f"page_plane{i}", tag="page_plane", align_bytes=64)
-            nc.vector.quantize_mx(codes[:].bitcast(FP8X4), plane[:], woven[i][:].rearrange("p c t -> p (c t)"))
+            codes = keep.tile([P, width], U32, name=f"page_codes{i}", align_bytes=64)
+            plane = keep.tile([P, width], U8, name=f"page_plane{i}", align_bytes=64)
+            for j in range(width // PIECE):
+                piece = slice(j * PIECE, (j + 1) * PIECE)
+                src = pages[3][:, starts[i] + j * PIECE : starts[i] + (j + 1) * PIECE]
+                if width > PIECE:
+                    last = placed([P, PIECE], BF16, f"last{i}{j}", AT_CODES + 2 * PACK * PIECE * j)
+                    nc.vector.tensor_copy(last[:], src)
+                    src = last[:]
+                nc.vector.tensor_copy(woven[i][:, piece, 3], src)
+                nc.vector.quantize_mx(
+                    codes[:, piece].bitcast(FP8X4), plane[:, piece],
+                    woven[i][:, piece, :].rearrange("p c t -> p (c t)"),
+                )
             for n in range(N // P):
                 rows = slice(n * P, (n + 1) * P)
                 acc = bank(f"acc{i}{n}", (N // P * i + n) % BANKS)

@@ -24,16 +24,28 @@ GROUP = 16
 PASS = P * PACK
 HALF = 512
 BANKS = 8
+WORD = 4
 KIB = 1024
+ROW = WORD * S
+
 FIRST_PIECES = ((0, 256), (256, 256), (512, 512))
-CHUNKS = (256, 256, 512, 512, 512)
-PIECE = 256
 INTERIOR_BANKS = (0, 4, 1)
-TURN_BANKS = 3
 SUMMED_UNITS = 3
-AT_TAB2, AT_TAB, AT_GROUPED, AT_RAW, AT_CODES, AT_LIFT, AT_VALUE, AT_GAIN, AT_SLOT = (
-    0, 16 * KIB, 48 * KIB, 64 * KIB, 96 * KIB, 112 * KIB, 128 * KIB, 144 * KIB, 160 * KIB,
-)
+TURN_BANKS = 3
+CHUNKS = (256, 256, 512, 512, 256, 256)
+PIECE = 256
+PAIRED = 4
+
+AT_TAB2 = 0
+AT_TAB = 16 * KIB
+AT_GROUPED = 48 * KIB
+AT_RAW = 64 * KIB
+AT_CODES = 96 * KIB
+AT_LIFT = 112 * KIB
+AT_VALUE = 128 * KIB
+AT_GAIN = 144 * KIB
+AT_SLOT = 163 * KIB
+AT_ROWS = 168 * KIB
 
 
 def tile_list_matting_patch_weave_kernel(
@@ -42,8 +54,8 @@ def tile_list_matting_patch_weave_kernel(
 ):
     nc = tc.nc
     halves = S // HALF
-    list_cols = HALF // GROUP
-    row_bytes = 4 * S
+    half_bytes = WORD * HALF
+    pass_bytes = WORD * PACK * H
 
     with ExitStack() as ctx:
         lists = ctx.enter_context(tc.tile_pool(name="lists", bufs=1))
@@ -54,50 +66,44 @@ def tile_list_matting_patch_weave_kernel(
         def placed(shape, dtype, name, offset):
             return big.tile(shape, dtype, name=name, offset=offset, align_bytes=64)
 
+        def bank(name, number):
+            return psum.tile([P, HALF], F32, name=name, tag=f"bank{number}")
+
+        def clear(tile, rows):
+            words = tile[0:rows, :].bitcast(I32)
+            count = words.shape[1]
+            nc.vector.memset(words[:, 0 : count - 1], 0)
+            nc.vector.memset(words[:, count - 1 : count], 0)
+
         def load_list(src, name):
             tile = lists.tile([P, S // GROUP], U16, name=name)
             nc.sync.dma_start(tile[:], src)
             return tile
 
-        def zeroed_planes(width, name):
-            tile = keep.tile([P, width + 4], U8, name=name, align_bytes=64)
-            nc.vector.memset(tile[:].bitcast(I32), 0)
-            return tile
-
-        def clear_rows(tile, rows):
-            words = tile[0:rows, :].bitcast(I32)
-            nc.vector.memset(words[:, 0 : T // 4 - 1], 0)
-            nc.vector.memset(words[:, T // 4 - 1 : T // 4], 0)
-
         def load_gain(src, t, name):
-            tile = placed([P, S], F32, name, AT_GAIN + row_bytes * t)
+            tile = placed([P, S], F32, name, AT_GAIN + ROW * t)
             rows = src.rearrange("(b t) j -> t b j", t=PACK)[t]
             for q in (0, 2, 1, 3):
                 nc.sync.dma_start(tile[QUAD * q : QUAD * (q + 1), :], rows)
             return tile
 
         def load_pass(src, a, name, offset):
-            width = src.shape[1]
-            tile = placed([P, PACK, width], F32, name, offset)
+            tile = placed([P, PACK, src.shape[1]], F32, name, offset)
             nc.sync.dma_start(
                 tile[:].rearrange("p i c -> p (i c)"),
                 src[a * PASS : (a + 1) * PASS, :].rearrange("(p i) c -> p (i c)", i=PACK),
             )
             return tile
 
-        def bank(name, number):
-            return psum.tile([P, HALF], F32, name=name, tag=f"bank{number}")
-
-        def slot(width, name):
-            return placed([P, width], F32, name, AT_SLOT + 3 * KIB)
-
-        raw_planes = zeroed_planes(3 * H, "raw_planes")
+        raw_planes = keep.tile([P, 3 * H], U8, name="raw_planes", align_bytes=64)
+        clear(raw_planes, P)
         wi_plane_raw, wb_plane_raw = raw_planes[:, 0:H], raw_planes[:, H : 3 * H]
         tab2_rows = keep.tile([P, T], U8, name="tab2_rows")
-        clear_rows(tab2_rows, P - GROUP)
-        tab_rows = placed([P, T], U8, "tab_rows", AT_SLOT + 2 * row_bytes)
-        clear_rows(tab_rows, P - 2 * GROUP)
-        moved_planes = zeroed_planes(3 * S, "moved_planes")
+        clear(tab2_rows, P - GROUP)
+        tab_rows = placed([P, T], U8, "tab_rows", AT_ROWS)
+        clear(tab_rows, P - 2 * GROUP)
+        moved_planes = keep.tile([P, 3 * S], U8, name="moved_planes", align_bytes=64)
+        clear(moved_planes, P)
         v2_plane, v_planes = moved_planes[:, 0:S], moved_planes[:, S : 3 * S]
         nc.gpsimd.dma_start(
             tab_rows[P - 2 * GROUP : P, :].bitcast(I32), tab_scales.bitcast(I32).rearrange("a r t -> r a t")
@@ -126,7 +132,7 @@ def tile_list_matting_patch_weave_kernel(
         for q in (0, 1):
             nc.sync.dma_start(first_gains[QUAD * q : QUAD * (q + 1), :, :], first_rows)
         gains2 = [first_gains[:, t, :] for t in range(2)]
-        wf_raw = [load_pass(wf, a, f"wf_raw{a}", AT_RAW + 8 * KIB * a) for a in range(2)]
+        wf_raw = [load_pass(wf, a, f"wf_raw{a}", AT_RAW + pass_bytes * a) for a in range(2)]
         for q in range(P // QUAD):
             nc.sync.dma_start(
                 wb_plane_raw[QUAD * q : QUAD * q + LIVE, :].bitcast(I32).rearrange("p (a c) -> p a c", a=2),
@@ -134,7 +140,7 @@ def tile_list_matting_patch_weave_kernel(
             )
         tab_window = placed([P, 2, T], U32, "tab_window", AT_TAB)
         nc.sync.dma_start(tab_window[:].bitcast(I32), tab_words.rearrange("a p t i -> p a (t i)").bitcast(I32))
-        wm_raw = [load_pass(wm, a, f"wm_raw{a}", AT_RAW + 8 * KIB * (2 + a)) for a in range(2)]
+        wm_raw = [load_pass(wm, a, f"wm_raw{a}", AT_RAW + pass_bytes * (2 + a)) for a in range(2)]
         gains2.extend(load_gain(wg2, t, f"gain2_{t}") for t in (2, 3))
         list3 = load_list(offs3, "list3")
 
@@ -155,33 +161,39 @@ def tile_list_matting_patch_weave_kernel(
                 v_planes[QUAD * q : QUAD * q + LIVE, :].bitcast(I32).rearrange("p (a c) -> p a c", a=2),
                 v_rows[P - 2 * GROUP + 2 * LIVE * q : P - 2 * GROUP + 2 * LIVE * (q + 1), :].bitcast(I32),
             )
+
         wi_codes = keep.tile([P, H], I32, name="wi_codes", align_bytes=64)
         nc.vector.tensor_copy(
             wi_codes[:].rearrange("p (t m) -> p m t", t=PACK), wi_raw[:].rearrange("p (m t) -> p m t", t=PACK)
         )
-        wi_plane = placed([P, H], U8, "wi_plane", AT_SLOT + 2 * row_bytes + 2 * KIB)
+        wi_plane = placed([P, H], U8, "wi_plane", AT_ROWS + half_bytes)
         nc.vector.tensor_copy(
-            wi_plane[:].rearrange("p (t m) -> p m t", t=PACK), wi_plane_raw.rearrange("p (m t) -> p m t", t=PACK)
+            wi_plane[:].rearrange("p (t m) -> p t m", t=PACK), wi_plane_raw.rearrange("p (m t) -> p t m", t=PACK)
         )
 
-        def gather_words(dst, window, lst, h):
-            nc.vector.tensor_copy(dst, window.indirect(lst[:, h * list_cols : (h + 1) * list_cols]))
+        def entries(lst, c0, width):
+            return lst[:] if width == S else lst[:, c0 // GROUP : (c0 + width) // GROUP]
 
-        v2_codes = [placed([P, HALF], U32, f"v2_codes{h}", AT_SLOT + 2 * row_bytes + 4 * KIB * h) for h in range(halves)]
+        v2_codes = [placed([P, HALF], U32, f"v2_codes{h}", AT_ROWS + T * h) for h in range(halves)]
         for h in range(halves):
-            gather_words(v2_codes[h][:], tab2_window[:], list2, h)
+            nc.vector.tensor_copy(v2_codes[h][:], tab2_window[:].indirect(entries(list2, h * HALF, HALF)))
         wb_codes = placed([P, 2, 2 * H], U8, "wb_codes", AT_TAB2)
         nc.vector.tensor_copy(
-            wb_codes[:].bitcast(U16).rearrange("p a (t m) -> p a m t", t=PACK),
-            wb_raw[:].bitcast(U16).rearrange("p a (m t) -> p a m t", t=PACK),
+            wb_codes[:].bitcast(U16).rearrange("p a (t m) -> p a t m", t=PACK),
+            wb_raw[:].bitcast(U16).rearrange("p a (m t) -> p a t m", t=PACK),
         )
+        after_wb_codes = AT_TAB2 + 4 * H
 
-        pages = [keep.tile([P, T2], F32, name=f"page{t}") for t in range(2)]
-        pages.extend(placed([P, T2], F32, f"page{t}", AT_GROUPED + 8 * KIB * (t - 2) - 4 * KIB) for t in (2, 3))
+        page2_overlap = 2 * KIB
+        pages = [
+            placed([P, T2], F32, "page2", AT_GROUPED + page2_overlap - WORD * T2)
+            if t == 2
+            else keep.tile([P, T2], F32, name=f"page{t}")
+            for t in range(PACK)
+        ]
 
         def scatter(t, lst, value, c0, width):
-            offsets = lst[:] if width == S else lst[:, c0 // GROUP : (c0 + width) // GROUP]
-            nc.vector.tensor_copy(pages[t][:].indirect(offsets), value[:, c0 : c0 + width])
+            nc.vector.tensor_copy(pages[t][:].indirect(entries(lst, c0, width)), value[:, c0 : c0 + width])
 
         def interior_product(number, t, c0, width):
             h = c0 // HALF
@@ -196,13 +208,14 @@ def tile_list_matting_patch_weave_kernel(
 
         def leak_and_gain(t, value, lift, c0, width):
             cols = slice(c0, c0 + width)
-            work = slot(width, f"leaky{t}_{c0}") if t < 2 else placed([P, S], F32, f"leaky{t}", AT_SLOT + row_bytes * (t - 2))
-            nc.gpsimd.tensor_tensor(work[:], value[:, cols], lift[:, cols], ALU.add)
-            nc.gpsimd.tensor_tensor(value[:, cols], work[:], gains2[t][:, cols], ALU.mult)
+            leaky = placed([P, width], F32, f"leaky{t}_{c0}", AT_SLOT)
+            nc.gpsimd.tensor_tensor(leaky[:], value[:, cols], lift[:, cols], ALU.add)
+            nc.gpsimd.tensor_tensor(value[:, cols], leaky[:], gains2[t][:, cols], ALU.mult)
 
         def interior_slice(t):
-            value = placed([P, S], F32, f"value2_{t}", AT_VALUE + row_bytes * t)
-            lift = placed([P, S], F32, f"lift{t}", AT_LIFT + row_bytes * t)
+            early = t < 2
+            value = placed([P, S], F32, f"value2_{t}", AT_VALUE + ROW * t)
+            lift = placed([P, S], F32, f"lift{t}", AT_LIFT + ROW * t)
             pieces = FIRST_PIECES if t == 0 else ((0, HALF), (HALF, HALF))
             first = 0 if t == 0 else len(FIRST_PIECES) + halves * (t - 1)
             for number, (c0, width) in enumerate(pieces):
@@ -210,58 +223,65 @@ def tile_list_matting_patch_weave_kernel(
                 d = interior_product(first + number, t, c0, width)
                 nc.scalar.activation(lift[:, cols], d, ACT.Relu, scale=slope_less_one[:, t : t + 1])
                 if width < HALF:
-                    leaky = placed([P, width], F32, f"leaky{t}_{c0}", AT_SLOT + 3 * KIB + 4 * c0)
+                    leaky = placed([P, width], F32, f"leaky{t}_{c0}", AT_SLOT + WORD * c0)
                     nc.vector.tensor_tensor(leaky[:], d, lift[:, cols], ALU.add)
                     nc.gpsimd.tensor_tensor(value[:, cols], leaky[:], gains2[t][:, cols], ALU.mult)
                 else:
                     nc.scalar.copy(value[:, cols], d)
-                    if t < 2:
+                    if early:
                         leak_and_gain(t, value, lift, c0, width)
-                if t < 2:
+                if early:
                     scatter(t, list4, value, c0, width)
-            if t >= 2:
-                leak_and_gain(t, value, lift, 0, S)
-            return value
+            return value, lift
 
-        values2 = [interior_slice(t) for t in range(PACK)]
+        interior = [interior_slice(t) for t in range(PACK - 1)]
+        leak_and_gain(2, *interior[2], 0, S)
+        value3, lift3 = interior_slice(3)
 
-        wb_plane = placed([P, 2 * H], U8, "wb_plane", AT_VALUE + row_bytes + 2 * KIB)
+        at_planes = AT_VALUE + ROW
+        wb_plane = placed([P, 2 * H], U8, "wb_plane", at_planes + 4 * H)
         nc.vector.tensor_copy(
-            wb_plane[:].rearrange("p (a t m) -> p a m t", a=2, t=PACK),
-            wb_plane_raw.rearrange("p (a m t) -> p a m t", a=2, t=PACK),
+            wb_plane[:].rearrange("p (a t m) -> p a t m", a=2, t=PACK),
+            wb_plane_raw.rearrange("p (a m t) -> p a t m", a=2, t=PACK),
         )
-
-        grouped = [placed([P, 2, PACK * H], BF16, f"grouped{w}", AT_GROUPED + 8 * KIB * (1 - w)) for w in range(2)]
-        for w, raw in enumerate((wf_raw, wm_raw)):
+        grouped = [
+            placed([P, 2, PACK * H], BF16, f"grouped{w}", AT_GROUPED + pass_bytes * (1 - w)) for w in range(2)
+        ]
+        for w, (raw, sign) in enumerate(((wf_raw, -1.0), (wm_raw, 1.0))):
             for a in range(2):
                 nc.scalar.activation(
                     grouped[w][:, a, :].rearrange("p (t m i) -> p m t i", t=PACK, i=PACK),
-                    raw[a][:, :, :].rearrange("p i (m t) -> p m t i", t=PACK),
-                    ACT.Copy, scale=(-1.0, 1.0)[w],
+                    raw[a][:].rearrange("p i (m t) -> p m t i", t=PACK),
+                    ACT.Copy, scale=sign,
                 )
-        w_codes = [placed([P, 2 * H], U32, f"w_codes{w}", AT_CODES + 6 * KIB + 4 * KIB * w) for w in range(2)]
-        w_plane = [placed([P, 2 * H], U8, f"w_plane{w}", AT_VALUE + row_bytes + KIB * w) for w in range(2)]
+        w_codes = [placed([P, 2 * H], U32, f"w_codes{w}", AT_CODES + half_bytes * (3 + 2 * w)) for w in range(2)]
+        w_plane = [placed([P, 2 * H], U8, f"w_plane{w}", at_planes + 2 * H * w) for w in range(2)]
+        v_places = ((2, 7), (1, 0))
 
         def quantise_weight(w):
             nc.vector.quantize_mx(
                 w_codes[w][:].bitcast(FP8X4), w_plane[w][:], grouped[w][:].rearrange("p a x -> p (a x)")
             )
 
+        at_edge_slot = AT_GROUPED + pass_bytes + ROW
         quantise_weight(0)
-        code_places = ((4 * KIB, 14 * KIB), (2 * KIB, 0))
+        leaky3 = placed([P, S], F32, "leaky3", at_edge_slot)
+        nc.gpsimd.tensor_tensor(leaky3[:], value3[:], lift3[:], ALU.add)
         v_codes = [
-            [placed([P, HALF], U32, f"v_codes{h}{a}", AT_CODES + code_places[h][a]) for a in range(2)]
+            [placed([P, HALF], U32, f"v_codes{h}{a}", AT_CODES + half_bytes * v_places[h][a]) for a in range(2)]
             for h in range(halves)
         ]
         for h in range(halves):
             for a in range(2):
-                gather_words(v_codes[h][a][:], tab_window[:, a, :], list1, h)
+                nc.vector.tensor_copy(v_codes[h][a][:], tab_window[:, a, :].indirect(entries(list1, h * HALF, HALF)))
         quantise_weight(1)
-        for t in (2, 3):
-            scatter(t, list4, values2[t], 0, S)
+        gained3 = placed([P, S], F32, "gained3", AT_GROUPED + page2_overlap)
+        nc.gpsimd.tensor_tensor(gained3[:], leaky3[:], gains2[3][:], ALU.mult)
+        scatter(2, list4, interior[2][0], 0, S)
+        scatter(3, list4, gained3, 0, S)
 
         gains1 = [load_gain(wg1, t, f"gain1_{t}") for t in (0, 1)]
-        wo_raw = load_pass(wo, 0, "wo_raw", AT_LIFT + 2 * row_bytes)
+        wo_raw = load_pass(wo, 0, "wo_raw", AT_LIFT + 2 * ROW)
         gains1.extend(load_gain(wg1, t, f"gain1_{t}") for t in (2, 3))
 
         def passes(acc, t, h, weights):
@@ -271,7 +291,7 @@ def tile_list_matting_patch_weave_kernel(
                 if weight == "b":
                     codes, plane = wb_codes[:, a, 2 * t * P : 2 * (t + 1) * P].bitcast(FP4X4), wb_plane[:, cols_a]
                 else:
-                    w = "fm".index(weight)
+                    w = ("f", "m").index(weight)
                     codes, plane = w_codes[w][:, cols_a].bitcast(FP8X4), w_plane[w][:, cols_a]
                 nc.tensor.matmul_mx(
                     acc[:], lhsT=codes, lhsT_scale=plane, rhs=v_codes[h][a][:].bitcast(FP8X4),
@@ -281,12 +301,14 @@ def tile_list_matting_patch_weave_kernel(
 
         def blend(t, value, matte, back, c0, width):
             cols = slice(c0, c0 + width)
-            work = placed([P, width], F32, f"blend{t}_{c0}", AT_SLOT + 3 * KIB + 4 * c0)
-            nc.gpsimd.tensor_tensor(work[:], value[:, cols], matte[:, cols], ALU.mult)
+            work = placed([P, width], F32, f"blend{t}_{c0}", at_edge_slot + WORD * c0)
             if t < PACK - 1:
+                nc.gpsimd.tensor_tensor(work[:], value[:, cols], matte[:, cols], ALU.mult)
                 nc.gpsimd.tensor_tensor(work[:], back[:, cols], work[:], ALU.subtract)
                 nc.gpsimd.tensor_tensor(value[:, cols], work[:], gains1[t][:, cols], ALU.mult)
             else:
+                nc.gpsimd.tensor_tensor(work[:], value[:, cols], back[:, cols], ALU.add)
+                nc.gpsimd.tensor_tensor(work[:], work[:], matte[:, cols], ALU.mult)
                 nc.gpsimd.tensor_tensor(value[:, cols], back[:, cols], work[:], ALU.subtract)
 
         turns = []
@@ -296,20 +318,20 @@ def tile_list_matting_patch_weave_kernel(
             return bank(name, (len(turns) - 1) % TURN_BANKS)
 
         for t in range(PACK):
-            region = AT_RAW + 8 * KIB * (3 - t) if t < 2 else AT_TAB2 + 2 * KIB + 8 * KIB * (t - 2)
+            region = AT_RAW + pass_bytes * (3 - t) if t < 2 else after_wb_codes + 2 * ROW * (t - 2)
             value = placed([P, S], F32, f"value1_{t}", region)
-            back = placed([P, S], F32, f"back{t}", region + row_bytes)
-            matte = placed([P, S], F32, f"matte{t}", AT_RAW + row_bytes * t)
+            back = placed([P, S], F32, f"back{t}", region + ROW)
+            matte = placed([P, S], F32, f"matte{t}", AT_RAW + ROW * t)
             for h in range(halves):
-                number = halves * t + h
+                unit = halves * t + h
                 cols = slice(h * HALF, (h + 1) * HALF)
-                if 1 <= number <= BANKS - TURN_BANKS:
-                    mt = bank(f"mt{number}", TURN_BANKS + number - 1)
-                if number < SUMMED_UNITS:
-                    diff = next_bank(f"diff{number}")
-                    if number == 0:
-                        mt = next_bank(f"mt{number}")
-                    bg = next_bank(f"bg{number}")
+                if 1 <= unit <= BANKS - TURN_BANKS:
+                    mt = bank(f"mt{unit}", TURN_BANKS + unit - 1)
+                if unit < SUMMED_UNITS:
+                    diff = next_bank(f"diff{unit}")
+                    if unit == 0:
+                        mt = next_bank(f"mt{unit}")
+                    bg = next_bank(f"bg{unit}")
                     passes(diff, t, h, "bf")
                     nc.scalar.copy(value[:, cols], diff[:])
                     passes(mt, t, h, "m")
@@ -317,16 +339,19 @@ def tile_list_matting_patch_weave_kernel(
                     passes(bg, t, h, "b")
                     nc.scalar.copy(back[:, cols], bg[:])
                 else:
-                    bg = next_bank(f"bg{number}")
-                    if number > BANKS - TURN_BANKS:
-                        mt = next_bank(f"mt{number}")
-                    diff = bank(f"diff{number}", number)
+                    bg = next_bank(f"bg{unit}")
+                    if unit > BANKS - TURN_BANKS:
+                        mt = next_bank(f"mt{unit}")
+                    less_fg = bank(f"diff{unit}", unit)
                     passes(bg, t, h, "b")
                     nc.scalar.copy(back[:, cols], bg[:])
                     passes(mt, t, h, "m")
                     nc.scalar.activation(matte[:, cols], mt[:], ACT.Sigmoid)
-                    passes(diff, t, h, "f")
-                    nc.vector.tensor_tensor(value[:, cols], diff[:], back[:, cols], ALU.add)
+                    passes(less_fg, t, h, "f")
+                    if t < PACK - 1:
+                        nc.vector.tensor_tensor(value[:, cols], less_fg[:], back[:, cols], ALU.add)
+                    else:
+                        nc.scalar.copy(value[:, cols], less_fg[:])
                 if t < 2:
                     blend(t, value, matte, back, h * HALF, HALF)
             if t >= 2:
@@ -336,13 +361,13 @@ def tile_list_matting_patch_weave_kernel(
             else:
                 nc.vector.tensor_tensor(pages[t][:].indirect(list3[:]), value[:], gains1[t][:], ALU.mult)
 
-        wo_grouped = placed([P, PACK * N], BF16, "wo_grouped", AT_VALUE + row_bytes)
+        wo_grouped = placed([P, PACK * N], BF16, "wo_grouped", at_planes)
         nc.scalar.copy(
             wo_grouped[:].rearrange("p (c n i) -> p c i n", n=4, i=PACK),
             wo_raw[:].rearrange("p i (c n) -> p c i n", n=4),
         )
         wo_codes = keep.tile([P, N], U32, name="wo_codes", align_bytes=64)
-        wo_plane = placed([P, N], U8, "wo_plane", AT_TAB2 + 2 * KIB)
+        wo_plane = placed([P, N], U8, "wo_plane", after_wb_codes)
         for c0, c1 in ((0, 2 * P), (2 * P, N)):
             nc.vector.quantize_mx(
                 wo_codes[:, c0:c1].bitcast(FP8X4), wo_plane[:, c0:c1], wo_grouped[:, PACK * c0 : PACK * c1]
@@ -353,12 +378,13 @@ def tile_list_matting_patch_weave_kernel(
             placed([P, width, PACK], BF16, f"woven{i}", AT_CODES + 2 * PACK * starts[i])
             for i, width in enumerate(CHUNKS)
         ]
+        scalar_chunk = 1
         for t in range(PACK - 1):
             for i, width in enumerate(CHUNKS):
                 src = pages[t][:, starts[i] : starts[i] + width]
-                if t < 2:
+                if t < 2 or i == scalar_chunk:
                     nc.scalar.copy(woven[i][:, :, t], src)
-                else:
+                elif i < PAIRED:
                     nc.scalar.copy(woven[i][:, :, 2:4], src.unsqueeze(2).to_broadcast([P, width, 2]))
         for i, width in enumerate(CHUNKS):
             cols = slice(starts[i], starts[i] + width)
@@ -366,12 +392,21 @@ def tile_list_matting_patch_weave_kernel(
             plane = keep.tile([P, width], U8, name=f"page_plane{i}", align_bytes=64)
             for j in range(width // PIECE):
                 piece = slice(j * PIECE, (j + 1) * PIECE)
-                src = pages[3][:, starts[i] + j * PIECE : starts[i] + (j + 1) * PIECE]
-                if width > PIECE:
-                    last = placed([P, PIECE], BF16, f"last{i}{j}", AT_CODES + 2 * PACK * PIECE * j)
-                    nc.vector.tensor_copy(last[:], src)
-                    src = last[:]
-                nc.vector.tensor_copy(woven[i][:, piece, 3], src)
+                page_cols = slice(starts[i] + j * PIECE, starts[i] + (j + 1) * PIECE)
+                at_last = AT_CODES + 2 * PACK * PIECE * (page_cols.start // PIECE % 2)
+                if i == 0:
+                    nc.vector.tensor_copy(woven[i][:, piece, 3], pages[3][:, page_cols])
+                elif i == scalar_chunk:
+                    nc.scalar.copy(woven[i][:, piece, 3], pages[3][:, page_cols])
+                elif i < PAIRED:
+                    last = placed([P, PIECE], BF16, f"last{i}{j}", at_last)
+                    nc.vector.tensor_copy(last[:], pages[3][:, page_cols])
+                    nc.vector.tensor_copy(woven[i][:, piece, 3], last[:])
+                else:
+                    last = placed([P, 2, PIECE], BF16, f"last{i}{j}", at_last)
+                    for t in range(2):
+                        nc.vector.tensor_copy(last[:, t, :], pages[2 + t][:, page_cols])
+                    nc.vector.tensor_copy(woven[i][:, piece, 2:4], last[:].rearrange("p t c -> p c t"))
                 nc.vector.quantize_mx(
                     codes[:, piece].bitcast(FP8X4), plane[:, piece],
                     woven[i][:, piece, :].rearrange("p c t -> p (c t)"),
@@ -383,8 +418,8 @@ def tile_list_matting_patch_weave_kernel(
                     acc[:, 0:width], lhsT=wo_codes[:, rows].bitcast(FP8X4), lhsT_scale=wo_plane[:, rows],
                     rhs=codes[:].bitcast(FP8X4), rhs_scale=plane[:], start=True, stop=True,
                 )
-                result = placed([P, width], F32, f"result{i}{n}", AT_TAB + 4 * (N // P * starts[i] + n * width))
-                if i == len(CHUNKS) - 1 and n > 0:
+                result = placed([P, width], F32, f"result{i}{n}", AT_TAB + WORD * (N // P * starts[i] + n * width))
+                if i == len(CHUNKS) - 1:
                     nc.vector.tensor_copy(result[:], acc[:, 0:width])
                 else:
                     nc.scalar.copy(result[:], acc[:, 0:width])

@@ -1,6 +1,7 @@
 from contextlib import ExitStack
 
 import concourse.mybir as mybir
+from concourse.masks import make_identity
 
 K, K2, H, N, T, S, T2 = 1024, 512, 512, 384, 4096, 1024, 2048
 FLOPS = 2 * (3 * K * H * S + K2 * H * S + H * N * T2)
@@ -70,10 +71,7 @@ def tile_list_matting_patch_weave_kernel(
             return psum.tile([P, HALF], F32, name=name, tag=f"bank{number}")
 
         def clear(tile, rows):
-            words = tile[0:rows, :].bitcast(I32)
-            count = words.shape[1]
-            nc.vector.memset(words[:, 0 : count - 1], 0)
-            nc.vector.memset(words[:, count - 1 : count], 0)
+            nc.vector.memset(tile[0:rows, :].bitcast(I32), 0)
 
         def load_list(src, name):
             tile = lists.tile([P, S // GROUP], U16, name=name)
@@ -98,75 +96,91 @@ def tile_list_matting_patch_weave_kernel(
         raw_planes = keep.tile([P, 3 * H], U8, name="raw_planes", align_bytes=64)
         clear(raw_planes, P)
         wi_plane_raw, wb_plane_raw = raw_planes[:, 0:H], raw_planes[:, H : 3 * H]
-        tab2_rows = keep.tile([P, T], U8, name="tab2_rows")
+        tab2_rows = placed([P, T], U8, "tab2_rows", AT_RAW)
         clear(tab2_rows, P - GROUP)
-        tab_rows = placed([P, T], U8, "tab_rows", AT_ROWS)
+        tab_rows = placed([P, T], U8, "tab_rows", AT_RAW + pass_bytes)
         clear(tab_rows, P - 2 * GROUP)
         moved_planes = keep.tile([P, 3 * S], U8, name="moved_planes", align_bytes=64)
         clear(moved_planes, P)
         v2_plane, v_planes = moved_planes[:, 0:S], moved_planes[:, S : 3 * S]
-        nc.gpsimd.dma_start(
-            tab_rows[P - 2 * GROUP : P, :].bitcast(I32), tab_scales.bitcast(I32).rearrange("a r t -> r a t")
-        )
+        identity = keep.tile([P, P], F32, name="identity")
+        make_identity(nc, identity[:])
         for q in range(P // QUAD):
             nc.gpsimd.dma_start(
                 wi_plane_raw[QUAD * q : QUAD * q + LIVE, :].bitcast(I32),
                 wi_scales[0, LIVE * q : LIVE * (q + 1), :].bitcast(I32),
             )
-        slopes = keep.tile([P, PACK], F32, name="slopes")
-        nc.gpsimd.dma_start(slopes[:], slope.rearrange("(p t) -> p t", t=PACK))
-        wi_raw = keep.tile([P, H], I32, name="wi_raw")
-        nc.scalar.dma_start(wi_raw[:], wi_words[0].rearrange("p c i -> p (c i)").bitcast(I32))
-        first_gains = placed([P, 2, S], F32, "gain2_01", AT_GAIN)
-        first_rows = wg2.rearrange("(b u t) j -> u b t j", u=2, t=2)[0]
-        for q in (2, 3):
-            nc.scalar.dma_start(first_gains[QUAD * q : QUAD * (q + 1), :, :], first_rows)
-        list2 = load_list(offs2, "list2")
-        nc.sync.dma_start(tab2_rows[P - GROUP : P, :].bitcast(I32), tab2_scales[0].bitcast(I32))
-        list1 = load_list(offs, "list1")
-        list4 = load_list(offs4, "list4")
-        wb_raw = keep.tile([P, 2, 2 * H], U8, name="wb_raw")
-        nc.sync.dma_start(wb_raw[:].bitcast(I32), wb_words.bitcast(I32).rearrange("a p c -> p a c"))
-        tab2_window = placed([P, T], U32, "tab2_window", AT_TAB2)
-        nc.sync.dma_start(tab2_window[:].bitcast(I32), tab2_words[0].rearrange("p t i -> p (t i)").bitcast(I32))
-        for q in (0, 1):
-            nc.sync.dma_start(first_gains[QUAD * q : QUAD * (q + 1), :, :], first_rows)
-        gains2 = [first_gains[:, t, :] for t in range(2)]
-        wf_raw = [load_pass(wf, a, f"wf_raw{a}", AT_RAW + pass_bytes * a) for a in range(2)]
         for q in range(P // QUAD):
-            nc.sync.dma_start(
+            nc.gpsimd.dma_start(
                 wb_plane_raw[QUAD * q : QUAD * q + LIVE, :].bitcast(I32).rearrange("p (a c) -> p a c", a=2),
                 wb_scales[:, LIVE * q : LIVE * (q + 1), :].bitcast(I32).rearrange("a r c -> r a c"),
             )
-        tab_window = placed([P, 2, T], U32, "tab_window", AT_TAB)
-        nc.sync.dma_start(tab_window[:].bitcast(I32), tab_words.rearrange("a p t i -> p a (t i)").bitcast(I32))
-        wm_raw = [load_pass(wm, a, f"wm_raw{a}", AT_RAW + pass_bytes * (2 + a)) for a in range(2)]
-        gains2.extend(load_gain(wg2, t, f"gain2_{t}") for t in (2, 3))
+        slopes = keep.tile([P, PACK], F32, name="slopes")
+        wi_raw = keep.tile([P, H], I32, name="wi_raw")
+        nc.scalar.dma_start(wi_raw[:], wi_words[0].rearrange("p c i -> p (c i)").bitcast(I32))
+        first_rows = placed([P, HALF], F32, "first_rows", AT_ROWS + ROW)
+        nc.scalar.dma_start(
+            first_rows[:],
+            wg2.rearrange("(b f) j -> b (f j)", f=PACK)[:, 0 : 2 * S].rearrange("b (k j) -> b k j", k=PACK),
+        )
+        nc.scalar.dma_start(slopes[:], slope.rearrange("(p t) -> p t", t=PACK))
+        list2 = load_list(offs2, "list2")
+        nc.sync.dma_start(tab2_rows[P - GROUP : P, :].bitcast(I32), tab2_scales[0].bitcast(I32))
+        list1 = load_list(offs, "list1")
+        nc.sync.dma_start(
+            tab_rows[P - 2 * GROUP : P, :].bitcast(I32), tab_scales.bitcast(I32).rearrange("a r t -> r a t")
+        )
+        tab2_window = placed([P, T], U32, "tab2_window", AT_TAB2)
+        nc.sync.dma_start(tab2_window[:].bitcast(I32), tab2_words[0].rearrange("p t i -> p (t i)").bitcast(I32))
+        list4 = load_list(offs4, "list4")
         list3 = load_list(offs3, "list3")
 
         slope_less_one = keep.tile([P, PACK], F32, name="slope_less_one")
         nc.scalar.activation(slope_less_one[:], slopes[:], ACT.Identity, bias=-1.0)
 
-        v2_rows = keep.tile([P, S], U8, name="v2_rows")
+        v2_rows = placed([P, S], U8, "v2_rows", AT_TAB)
         nc.vector.tensor_copy(v2_rows[:], tab2_rows[:].indirect(list2[:]))
         for q in range(P // QUAD):
             nc.scalar.dma_start(
                 v2_plane[QUAD * q : QUAD * q + LIVE, :].bitcast(I32),
                 v2_rows[P - GROUP + LIVE * q : P - GROUP + LIVE * (q + 1), :].bitcast(I32),
             )
-        v_rows = keep.tile([P, S], U8, name="v_rows")
+        wf_raw = [load_pass(wf, 0, "wf_raw0", AT_RAW)]
+
+        turned = bank("turned", 2)
+        for c in range(PACK):
+            nc.tensor.transpose(turned[:, c * P : (c + 1) * P], first_rows[:, c * P : (c + 1) * P], identity[:])
+        wb_raw = placed([P, 2, 2 * H], U8, "wb_raw", AT_ROWS + ROW)
+        nc.sync.dma_start(wb_raw[:].bitcast(I32), wb_words.bitcast(I32).rearrange("a p c -> p a c"))
+        v_rows = placed([P, S], U8, "v_rows", AT_RAW + 3 * pass_bytes - S // 2)
         nc.vector.tensor_copy(v_rows[:], tab_rows[:].indirect(list1[:]))
         for q in range(P // QUAD):
-            nc.scalar.dma_start(
+            nc.sync.dma_start(
                 v_planes[QUAD * q : QUAD * q + LIVE, :].bitcast(I32).rearrange("p (a c) -> p a c", a=2),
                 v_rows[P - 2 * GROUP + 2 * LIVE * q : P - 2 * GROUP + 2 * LIVE * (q + 1), :].bitcast(I32),
             )
+        wf_raw.append(load_pass(wf, 1, "wf_raw1", AT_RAW + pass_bytes))
+        tab_window = placed([P, 2, T], U32, "tab_window", AT_TAB)
+        nc.sync.dma_start(tab_window[:].bitcast(I32), tab_words.rearrange("a p t i -> p a (t i)").bitcast(I32))
+        wm_raw = [load_pass(wm, a, f"wm_raw{a}", AT_RAW + pass_bytes * (2 + a)) for a in range(2)]
+        gains2 = [placed([P, S], F32, f"gain2_{t}", AT_GAIN + ROW * t) for t in range(2)]
+        for k in range(PACK):
+            repeated = placed([P, PACK, P], F32, f"repeated{k}", AT_CODES + half_bytes * k)
+            nc.scalar.copy(
+                repeated[:].rearrange("p c (q b) -> p c q b", b=QUAD),
+                turned[:].rearrange("p (c b k) -> p k c b", c=PACK, k=PACK)[:, k, :, :]
+                .unsqueeze(2).to_broadcast([P, PACK, P // QUAD, QUAD]),
+            )
+            back_turned = bank(f"back_turned{k}", (3, 5, 6, 7)[k])
+            for c in range(PACK):
+                nc.tensor.transpose(back_turned[:, c * P : (c + 1) * P], repeated[:, c, :], identity[:])
+            nc.scalar.copy(gains2[k // 2][:, HALF * (k % 2) : HALF * (k % 2 + 1)], back_turned[:])
 
         wi_codes = keep.tile([P, H], I32, name="wi_codes", align_bytes=64)
         nc.vector.tensor_copy(
             wi_codes[:].rearrange("p (t m) -> p m t", t=PACK), wi_raw[:].rearrange("p (m t) -> p m t", t=PACK)
         )
-        wi_plane = placed([P, H], U8, "wi_plane", AT_ROWS + half_bytes)
+        wi_plane = keep.tile([P, H], U8, name="wi_plane", align_bytes=64)
         nc.vector.tensor_copy(
             wi_plane[:].rearrange("p (t m) -> p t m", t=PACK), wi_plane_raw.rearrange("p (m t) -> p t m", t=PACK)
         )
@@ -174,14 +188,9 @@ def tile_list_matting_patch_weave_kernel(
         def entries(lst, c0, width):
             return lst[:] if width == S else lst[:, c0 // GROUP : (c0 + width) // GROUP]
 
-        v2_codes = [placed([P, HALF], U32, f"v2_codes{h}", AT_ROWS + T * h) for h in range(halves)]
+        v2_codes = [placed([P, HALF], U32, f"v2_codes{h}", AT_ROWS + half_bytes * h) for h in range(halves)]
         for h in range(halves):
             nc.vector.tensor_copy(v2_codes[h][:], tab2_window[:].indirect(entries(list2, h * HALF, HALF)))
-        wb_codes = placed([P, 2, 2 * H], U8, "wb_codes", AT_TAB2)
-        nc.vector.tensor_copy(
-            wb_codes[:].bitcast(U16).rearrange("p a (t m) -> p a t m", t=PACK),
-            wb_raw[:].bitcast(U16).rearrange("p a (m t) -> p a t m", t=PACK),
-        )
         after_wb_codes = AT_TAB2 + 4 * H
 
         page2_overlap = 2 * KIB
@@ -215,7 +224,7 @@ def tile_list_matting_patch_weave_kernel(
         def interior_slice(t):
             early = t < 2
             value = placed([P, S], F32, f"value2_{t}", AT_VALUE + ROW * t)
-            lift = placed([P, S], F32, f"lift{t}", AT_LIFT + ROW * t)
+            lift = placed([P, S], F32, f"lift{t}", AT_LIFT + ROW * t if t else AT_GAIN + 3 * ROW - half_bytes)
             pieces = FIRST_PIECES if t == 0 else ((0, HALF), (HALF, HALF))
             first = 0 if t == 0 else len(FIRST_PIECES) + halves * (t - 1)
             for number, (c0, width) in enumerate(pieces):
@@ -234,7 +243,14 @@ def tile_list_matting_patch_weave_kernel(
                     scatter(t, list4, value, c0, width)
             return value, lift
 
-        interior = [interior_slice(t) for t in range(PACK - 1)]
+        interior = [interior_slice(0)]
+        wb_codes = placed([P, 2, 2 * H], U8, "wb_codes", AT_VALUE)
+        nc.vector.tensor_copy(
+            wb_codes[:].bitcast(U16).rearrange("p a (t m) -> p a t m", t=PACK),
+            wb_raw[:].bitcast(U16).rearrange("p a (m t) -> p a t m", t=PACK),
+        )
+        gains2.extend(load_gain(wg2, t, f"gain2_{t}") for t in (2, 3))
+        interior.extend(interior_slice(t) for t in (1, 2))
         leak_and_gain(2, *interior[2], 0, S)
         value3, lift3 = interior_slice(3)
 

@@ -33,9 +33,8 @@ FIRST_PIECES = ((0, 256), (256, 256), (512, 512))
 INTERIOR_BANKS = (0, 4, 1)
 SUMMED_UNITS = 3
 TURN_BANKS = 3
-CHUNKS = (256, 256, 512, 512, 256, 256)
+CHUNKS = (128, 128, 256, 512, 512, 512)
 PIECE = 256
-PAIRED = 4
 
 AT_TAB2 = 0
 AT_TAB = 16 * KIB
@@ -383,60 +382,54 @@ def tile_list_matting_patch_weave_kernel(
             wo_raw[:].rearrange("p i (c n) -> p c i n", n=4),
         )
         wo_codes = keep.tile([P, N], U32, name="wo_codes", align_bytes=64)
-        wo_plane = placed([P, N], U8, "wo_plane", after_wb_codes)
-        for c0, c1 in ((0, 2 * P), (2 * P, N)):
-            nc.vector.quantize_mx(
-                wo_codes[:, c0:c1].bitcast(FP8X4), wo_plane[:, c0:c1], wo_grouped[:, PACK * c0 : PACK * c1]
-            )
+        wo_plane = placed([P, N], U8, "wo_plane", after_wb_codes + 2 * ROW)
 
         starts = [sum(CHUNKS[:i]) for i in range(len(CHUNKS))]
         woven = [
             placed([P, width, PACK], BF16, f"woven{i}", AT_CODES + 2 * PACK * starts[i])
             for i, width in enumerate(CHUNKS)
         ]
-        scalar_chunk = 1
         for t in range(PACK - 1):
             for i, width in enumerate(CHUNKS):
                 src = pages[t][:, starts[i] : starts[i] + width]
-                if t < 2 or i == scalar_chunk:
+                if t < 2:
                     nc.scalar.copy(woven[i][:, :, t], src)
-                elif i < PAIRED:
+                else:
                     nc.scalar.copy(woven[i][:, :, 2:4], src.unsqueeze(2).to_broadcast([P, width, 2]))
-        for i, width in enumerate(CHUNKS):
-            cols = slice(starts[i], starts[i] + width)
-            codes = keep.tile([P, width], U32, name=f"page_codes{i}", align_bytes=64)
-            plane = keep.tile([P, width], U8, name=f"page_plane{i}", align_bytes=64)
-            for j in range(width // PIECE):
-                piece = slice(j * PIECE, (j + 1) * PIECE)
-                page_cols = slice(starts[i] + j * PIECE, starts[i] + (j + 1) * PIECE)
-                at_last = AT_CODES + 2 * PACK * PIECE * (page_cols.start // PIECE % 2)
-                if i == 0:
-                    nc.vector.tensor_copy(woven[i][:, piece, 3], pages[3][:, page_cols])
-                elif i == scalar_chunk:
-                    nc.scalar.copy(woven[i][:, piece, 3], pages[3][:, page_cols])
-                elif i < PAIRED:
-                    last = placed([P, PIECE], BF16, f"last{i}{j}", at_last)
-                    nc.vector.tensor_copy(last[:], pages[3][:, page_cols])
-                    nc.vector.tensor_copy(woven[i][:, piece, 3], last[:])
+        out_rows = out.rearrange("(n p) c -> p n c", p=P)
+        pieces = [
+            (i, c0, min(width, PIECE)) for i, width in enumerate(CHUNKS) for c0 in range(0, width, PIECE)
+        ]
+        turns.clear()
+        for k, (i, c0, width) in enumerate(pieces):
+            piece = slice(c0, c0 + width)
+            cols = slice(starts[i] + c0, starts[i] + c0 + width)
+            nc.vector.tensor_copy(woven[i][:, piece, 3], pages[3][:, cols])
+            if k == 0:
+                for n0, n1 in ((0, 2 * P), (2 * P, N)):
+                    nc.vector.quantize_mx(
+                        wo_codes[:, n0:n1].bitcast(FP8X4), wo_plane[:, n0:n1], wo_grouped[:, PACK * n0 : PACK * n1]
+                    )
+            codes = keep.tile([P, width], U32, name=f"page_codes{k}", align_bytes=64)
+            plane = keep.tile([P, width], U8, name=f"page_plane{k}", align_bytes=64)
+            nc.vector.quantize_mx(
+                codes[:].bitcast(FP8X4), plane[:], woven[i][:, piece, :].rearrange("p c t -> p (c t)")
+            )
+            result = placed([P, N // P, width], F32, f"result{k}", AT_TAB + WORD * (N // P) * cols.start)
+            for n0 in range(0, N // P, HALF // width):
+                n1 = min(N // P, n0 + HALF // width)
+                turns.append(k)
+                acc = bank(f"acc{k}{n0}", (len(turns) - 1) % BANKS)
+                for n in range(n0, n1):
+                    rows = slice(n * P, (n + 1) * P)
+                    nc.tensor.matmul_mx(
+                        acc[:, (n - n0) * width : (n - n0 + 1) * width],
+                        lhsT=wo_codes[:, rows].bitcast(FP8X4), lhsT_scale=wo_plane[:, rows],
+                        rhs=codes[:].bitcast(FP8X4), rhs_scale=plane[:], start=True, stop=True,
+                    )
+                emptied = result[:, n0:n1, :].rearrange("p n c -> p (n c)")
+                if n0 == 0 and k >= len(pieces) - 2:
+                    nc.vector.tensor_copy(emptied, acc[:, 0 : (n1 - n0) * width])
                 else:
-                    last = placed([P, 2, PIECE], BF16, f"last{i}{j}", at_last)
-                    for t in range(2):
-                        nc.vector.tensor_copy(last[:, t, :], pages[2 + t][:, page_cols])
-                    nc.vector.tensor_copy(woven[i][:, piece, 2:4], last[:].rearrange("p t c -> p c t"))
-                nc.vector.quantize_mx(
-                    codes[:, piece].bitcast(FP8X4), plane[:, piece],
-                    woven[i][:, piece, :].rearrange("p c t -> p (c t)"),
-                )
-            for n in range(N // P):
-                rows = slice(n * P, (n + 1) * P)
-                acc = bank(f"acc{i}{n}", (N // P * i + n) % BANKS)
-                nc.tensor.matmul_mx(
-                    acc[:, 0:width], lhsT=wo_codes[:, rows].bitcast(FP8X4), lhsT_scale=wo_plane[:, rows],
-                    rhs=codes[:].bitcast(FP8X4), rhs_scale=plane[:], start=True, stop=True,
-                )
-                result = placed([P, width], F32, f"result{i}{n}", AT_TAB + WORD * (N // P * starts[i] + n * width))
-                if i == len(CHUNKS) - 1:
-                    nc.vector.tensor_copy(result[:], acc[:, 0:width])
-                else:
-                    nc.scalar.copy(result[:], acc[:, 0:width])
-                nc.sync.dma_start(out[rows, cols], result[:])
+                    nc.scalar.copy(emptied, acc[:, 0 : (n1 - n0) * width])
+            nc.sync.dma_start(out_rows[:, :, cols], result[:])

@@ -95,13 +95,12 @@ def tile_list_matting_patch_weave_kernel(
         raw_planes = keep.tile([P, 3 * H], U8, name="raw_planes", align_bytes=64)
         clear(raw_planes, P)
         wi_plane_raw, wb_plane_raw = raw_planes[:, 0:H], raw_planes[:, H : 3 * H]
-        tab2_rows = placed([P, T], U8, "tab2_rows", AT_RAW)
+        tab2_rows = placed([P, T], U8, "tab2_rows", AT_RAW + pass_bytes - T // 2)
         clear(tab2_rows, P - GROUP)
-        tab_rows = placed([P, T], U8, "tab_rows", AT_RAW + pass_bytes)
+        tab_rows = placed([P, T], U8, "tab_rows", AT_RAW + 3 * pass_bytes - T // 2)
         clear(tab_rows, P - 2 * GROUP)
-        moved_planes = keep.tile([P, 3 * S], U8, name="moved_planes", align_bytes=64)
-        clear(moved_planes, P)
-        v2_plane, v_planes = moved_planes[:, 0:S], moved_planes[:, S : 3 * S]
+        v2_plane = keep.tile([P, S], U8, name="v2_plane", align_bytes=64)
+        clear(v2_plane, P)
         identity = keep.tile([P, P], F32, name="identity")
         make_identity(nc, identity[:])
         for q in range(P // QUAD):
@@ -151,13 +150,8 @@ def tile_list_matting_patch_weave_kernel(
             nc.tensor.transpose(turned[:, c * P : (c + 1) * P], first_rows[:, c * P : (c + 1) * P], identity[:])
         wb_raw = placed([P, 2, 2 * H], U8, "wb_raw", AT_ROWS + ROW)
         nc.sync.dma_start(wb_raw[:].bitcast(I32), wb_words.bitcast(I32).rearrange("a p c -> p a c"))
-        v_rows = placed([P, S], U8, "v_rows", AT_RAW + 3 * pass_bytes - S // 2)
+        v_rows = keep.tile([P, S], U8, name="v_rows")
         nc.vector.tensor_copy(v_rows[:], tab_rows[:].indirect(list1[:]))
-        for q in range(P // QUAD):
-            nc.sync.dma_start(
-                v_planes[QUAD * q : QUAD * q + LIVE, :].bitcast(I32).rearrange("p (a c) -> p a c", a=2),
-                v_rows[P - 2 * GROUP + 2 * LIVE * q : P - 2 * GROUP + 2 * LIVE * (q + 1), :].bitcast(I32),
-            )
         wf_raw.append(load_pass(wf, 1, "wf_raw1", AT_RAW + pass_bytes))
         tab_window = placed([P, 2, T], U32, "tab_window", AT_TAB)
         nc.sync.dma_start(tab_window[:].bitcast(I32), tab_words.rearrange("a p t i -> p a (t i)").bitcast(I32))
@@ -243,17 +237,28 @@ def tile_list_matting_patch_weave_kernel(
             return value, lift
 
         interior = [interior_slice(0)]
-        wb_codes = placed([P, 2, 2 * H], U8, "wb_codes", AT_VALUE)
+        gains2.extend(load_gain(wg2, t, f"gain2_{t}") for t in (2, 3))
+        interior.append(interior_slice(1))
+        v_planes = placed([P, 2 * S], U8, "v_planes", AT_LIFT + ROW)
+        nc.gpsimd.memset(v_planes[:].bitcast(I32), 0)
+        for q in range(P // QUAD):
+            nc.scalar.dma_start(
+                v_planes[QUAD * q : QUAD * q + LIVE, :].bitcast(I32).rearrange("p (a c) -> p a c", a=2),
+                v_rows[P - 2 * GROUP + 2 * LIVE * q : P - 2 * GROUP + 2 * LIVE * (q + 1), :].bitcast(I32),
+            )
+        interior.extend(interior_slice(t) for t in (2, 3))
+        at_edge_slot = AT_LIFT + 2 * ROW
+        late_sums = []
+        for t, at in ((2, AT_SLOT), (3, at_edge_slot)):
+            late_sums.append(placed([P, S], F32, f"leaky{t}", at))
+            nc.gpsimd.tensor_tensor(late_sums[-1][:], interior[t][0][:], interior[t][1][:], ALU.add)
+
+        at_planes = AT_VALUE + ROW + 2 * H
+        wb_codes = placed([P, 2, 2 * H], U8, "wb_codes", at_planes - 4 * H)
         nc.vector.tensor_copy(
             wb_codes[:].bitcast(U16).rearrange("p a (t m) -> p a t m", t=PACK),
             wb_raw[:].bitcast(U16).rearrange("p a (m t) -> p a t m", t=PACK),
         )
-        gains2.extend(load_gain(wg2, t, f"gain2_{t}") for t in (2, 3))
-        interior.extend(interior_slice(t) for t in (1, 2))
-        leak_and_gain(2, *interior[2], 0, S)
-        value3, lift3 = interior_slice(3)
-
-        at_planes = AT_VALUE + ROW
         wb_plane = placed([P, 2 * H], U8, "wb_plane", at_planes + 4 * H)
         nc.vector.tensor_copy(
             wb_plane[:].rearrange("p (a t m) -> p a t m", a=2, t=PACK),
@@ -278,10 +283,9 @@ def tile_list_matting_patch_weave_kernel(
                 w_codes[w][:].bitcast(FP8X4), w_plane[w][:], grouped[w][:].rearrange("p a x -> p (a x)")
             )
 
-        at_edge_slot = AT_GROUPED + pass_bytes + ROW
         quantise_weight(0)
-        leaky3 = placed([P, S], F32, "leaky3", at_edge_slot)
-        nc.gpsimd.tensor_tensor(leaky3[:], value3[:], lift3[:], ALU.add)
+        gained2 = placed([P, S], F32, "gained2", AT_GROUPED + pass_bytes)
+        nc.gpsimd.tensor_tensor(gained2[:], late_sums[0][:], gains2[2][:], ALU.mult)
         v_codes = [
             [placed([P, HALF], U32, f"v_codes{h}{a}", AT_CODES + half_bytes * v_places[h][a]) for a in range(2)]
             for h in range(halves)
@@ -291,12 +295,12 @@ def tile_list_matting_patch_weave_kernel(
                 nc.vector.tensor_copy(v_codes[h][a][:], tab_window[:, a, :].indirect(entries(list1, h * HALF, HALF)))
         quantise_weight(1)
         gained3 = placed([P, S], F32, "gained3", AT_GROUPED + page2_overlap)
-        nc.gpsimd.tensor_tensor(gained3[:], leaky3[:], gains2[3][:], ALU.mult)
-        scatter(2, list4, interior[2][0], 0, S)
+        nc.gpsimd.tensor_tensor(gained3[:], late_sums[1][:], gains2[3][:], ALU.mult)
+        scatter(2, list4, gained2, 0, S)
         scatter(3, list4, gained3, 0, S)
 
         gains1 = [load_gain(wg1, t, f"gain1_{t}") for t in (0, 1)]
-        wo_raw = load_pass(wo, 0, "wo_raw", AT_LIFT + 2 * ROW)
+        wo_raw = load_pass(wo, 0, "wo_raw", AT_VALUE + 2 * ROW)
         gains1.extend(load_gain(wg1, t, f"gain1_{t}") for t in (2, 3))
 
         def passes(acc, t, h, weights):

@@ -95,12 +95,13 @@ def tile_list_matting_patch_weave_kernel(
         raw_planes = keep.tile([P, 3 * H], U8, name="raw_planes", align_bytes=64)
         clear(raw_planes, P)
         wi_plane_raw, wb_plane_raw = raw_planes[:, 0:H], raw_planes[:, H : 3 * H]
-        tab2_rows = placed([P, T], U8, "tab2_rows", AT_RAW + pass_bytes - T // 2)
+        tab2_rows = placed([P, T], U8, "tab2_rows", AT_RAW)
         clear(tab2_rows, P - GROUP)
-        tab_rows = placed([P, T], U8, "tab_rows", AT_RAW + 3 * pass_bytes - T // 2)
+        tab_rows = placed([P, T], U8, "tab_rows", AT_RAW + pass_bytes)
         clear(tab_rows, P - 2 * GROUP)
-        v2_plane = keep.tile([P, S], U8, name="v2_plane", align_bytes=64)
-        clear(v2_plane, P)
+        moved_planes = keep.tile([P, 3 * S], U8, name="moved_planes", align_bytes=64)
+        clear(moved_planes, P)
+        v2_plane, v_planes = moved_planes[:, 0:S], moved_planes[:, S : 3 * S]
         identity = keep.tile([P, P], F32, name="identity")
         make_identity(nc, identity[:])
         for q in range(P // QUAD):
@@ -150,8 +151,13 @@ def tile_list_matting_patch_weave_kernel(
             nc.tensor.transpose(turned[:, c * P : (c + 1) * P], first_rows[:, c * P : (c + 1) * P], identity[:])
         wb_raw = placed([P, 2, 2 * H], U8, "wb_raw", AT_ROWS + ROW)
         nc.sync.dma_start(wb_raw[:].bitcast(I32), wb_words.bitcast(I32).rearrange("a p c -> p a c"))
-        v_rows = keep.tile([P, S], U8, name="v_rows")
+        v_rows = placed([P, S], U8, "v_rows", AT_RAW + 3 * pass_bytes - S // 2)
         nc.vector.tensor_copy(v_rows[:], tab_rows[:].indirect(list1[:]))
+        for q in range(P // QUAD):
+            nc.sync.dma_start(
+                v_planes[QUAD * q : QUAD * q + LIVE, :].bitcast(I32).rearrange("p (a c) -> p a c", a=2),
+                v_rows[P - 2 * GROUP + 2 * LIVE * q : P - 2 * GROUP + 2 * LIVE * (q + 1), :].bitcast(I32),
+            )
         wf_raw.append(load_pass(wf, 1, "wf_raw1", AT_RAW + pass_bytes))
         tab_window = placed([P, 2, T], U32, "tab_window", AT_TAB)
         nc.sync.dma_start(tab_window[:].bitcast(I32), tab_words.rearrange("a p t i -> p a (t i)").bitcast(I32))
@@ -238,20 +244,9 @@ def tile_list_matting_patch_weave_kernel(
 
         interior = [interior_slice(0)]
         gains2.extend(load_gain(wg2, t, f"gain2_{t}") for t in (2, 3))
-        interior.append(interior_slice(1))
-        v_planes = placed([P, 2 * S], U8, "v_planes", AT_LIFT + ROW)
-        nc.gpsimd.memset(v_planes[:].bitcast(I32), 0)
-        for q in range(P // QUAD):
-            nc.scalar.dma_start(
-                v_planes[QUAD * q : QUAD * q + LIVE, :].bitcast(I32).rearrange("p (a c) -> p a c", a=2),
-                v_rows[P - 2 * GROUP + 2 * LIVE * q : P - 2 * GROUP + 2 * LIVE * (q + 1), :].bitcast(I32),
-            )
-        interior.extend(interior_slice(t) for t in (2, 3))
-        at_edge_slot = AT_LIFT + 2 * ROW
-        late_sums = []
-        for t, at in ((2, AT_SLOT), (3, at_edge_slot)):
-            late_sums.append(placed([P, S], F32, f"leaky{t}", at))
-            nc.gpsimd.tensor_tensor(late_sums[-1][:], interior[t][0][:], interior[t][1][:], ALU.add)
+        interior.extend(interior_slice(t) for t in (1, 2, 3))
+        leaky2 = placed([P, S], F32, "leaky2", AT_SLOT)
+        nc.gpsimd.tensor_tensor(leaky2[:], interior[2][0][:], interior[2][1][:], ALU.add)
 
         at_planes = AT_VALUE + ROW + 2 * H
         wb_codes = placed([P, 2, 2 * H], U8, "wb_codes", at_planes - 4 * H)
@@ -283,9 +278,12 @@ def tile_list_matting_patch_weave_kernel(
                 w_codes[w][:].bitcast(FP8X4), w_plane[w][:], grouped[w][:].rearrange("p a x -> p (a x)")
             )
 
+        at_edge_slot = AT_GROUPED + pass_bytes + ROW
         quantise_weight(0)
+        leaky3 = placed([P, S], F32, "leaky3", at_edge_slot)
+        nc.gpsimd.tensor_tensor(leaky3[:], interior[3][0][:], interior[3][1][:], ALU.add)
         gained2 = placed([P, S], F32, "gained2", AT_GROUPED + pass_bytes)
-        nc.gpsimd.tensor_tensor(gained2[:], late_sums[0][:], gains2[2][:], ALU.mult)
+        nc.gpsimd.tensor_tensor(gained2[:], leaky2[:], gains2[2][:], ALU.mult)
         v_codes = [
             [placed([P, HALF], U32, f"v_codes{h}{a}", AT_CODES + half_bytes * v_places[h][a]) for a in range(2)]
             for h in range(halves)
@@ -295,12 +293,12 @@ def tile_list_matting_patch_weave_kernel(
                 nc.vector.tensor_copy(v_codes[h][a][:], tab_window[:, a, :].indirect(entries(list1, h * HALF, HALF)))
         quantise_weight(1)
         gained3 = placed([P, S], F32, "gained3", AT_GROUPED + page2_overlap)
-        nc.gpsimd.tensor_tensor(gained3[:], late_sums[1][:], gains2[3][:], ALU.mult)
+        nc.gpsimd.tensor_tensor(gained3[:], leaky3[:], gains2[3][:], ALU.mult)
         scatter(2, list4, gained2, 0, S)
         scatter(3, list4, gained3, 0, S)
 
         gains1 = [load_gain(wg1, t, f"gain1_{t}") for t in (0, 1)]
-        wo_raw = load_pass(wo, 0, "wo_raw", AT_VALUE + 2 * ROW)
+        wo_raw = load_pass(wo, 0, "wo_raw", AT_LIFT + 2 * ROW)
         gains1.extend(load_gain(wg1, t, f"gain1_{t}") for t in (2, 3))
 
         def passes(acc, t, h, weights):

@@ -19,6 +19,7 @@ ACT = mybir.ActivationFunctionType
 
 P = 128
 PACK = 4
+PAIR = 2
 QUAD = 32
 LIVE = 4
 GROUP = 16
@@ -79,7 +80,7 @@ def tile_list_matting_patch_weave_kernel(
 
         def load_gain(src, t, name):
             tile = placed([P, S], F32, name, AT_GAIN + ROW * t)
-            rows = src.rearrange("(b t) j -> t b j", t=PACK)[t]
+            rows = src.rearrange("(u t e) j -> t u e j", t=PACK, e=PAIR)[t]
             for q in (0, 2, 1, 3):
                 nc.sync.dma_start(tile[QUAD * q : QUAD * (q + 1), :], rows)
             return tile
@@ -114,15 +115,20 @@ def tile_list_matting_patch_weave_kernel(
                 wb_plane_raw[QUAD * q : QUAD * q + LIVE, :].bitcast(I32).rearrange("p (a c) -> p a c", a=2),
                 wb_scales[:, LIVE * q : LIVE * (q + 1), :].bitcast(I32).rearrange("a r c -> r a c"),
             )
-        slopes = keep.tile([P, PACK], F32, name="slopes")
+        slopes = keep.tile([P, PAIR * PACK - 1], F32, name="slopes")
         wi_raw = keep.tile([P, H], I32, name="wi_raw")
         nc.scalar.dma_start(wi_raw[:], wi_words[0].rearrange("p c i -> p (c i)").bitcast(I32))
         first_rows = placed([P, HALF], F32, "first_rows", AT_ROWS + ROW)
         nc.scalar.dma_start(
             first_rows[:],
-            wg2.rearrange("(b f) j -> b (f j)", f=PACK)[:, 0 : 2 * S].rearrange("b (k j) -> b k j", k=PACK),
+            wg2.rearrange("(u f) j -> u (f j)", f=PACK * PAIR)[:, 0 : 2 * PAIR * S].rearrange(
+                "u (x j) -> u x j", j=HALF
+            ),
         )
-        nc.scalar.dma_start(slopes[:], slope.rearrange("(p t) -> p t", t=PACK))
+        for e in range(PAIR):
+            nc.scalar.dma_start(
+                slopes[e:P:PAIR, :], slope.rearrange("(u x) -> u x", x=PACK * PAIR)[:, e : e + PAIR * PACK - 1]
+            )
         list2 = load_list(offs2, "list2")
         nc.sync.dma_start(tab2_rows[P - GROUP : P, :].bitcast(I32), tab2_scales[0].bitcast(I32))
         list1 = load_list(offs, "list1")
@@ -135,7 +141,7 @@ def tile_list_matting_patch_weave_kernel(
         list3 = load_list(offs3, "list3")
 
         slope_less_one = keep.tile([P, PACK], F32, name="slope_less_one")
-        nc.scalar.activation(slope_less_one[:], slopes[:], ACT.Identity, bias=-1.0)
+        nc.scalar.activation(slope_less_one[:], slopes[:, 0 : PAIR * PACK - 1 : PAIR], ACT.Identity, bias=-1.0)
 
         v2_rows = placed([P, S], U8, "v2_rows", AT_TAB)
         nc.vector.tensor_copy(v2_rows[:], tab2_rows[:].indirect(list2[:]))
@@ -166,9 +172,9 @@ def tile_list_matting_patch_weave_kernel(
         for k in range(PACK):
             repeated = placed([P, PACK, P], F32, f"repeated{k}", AT_CODES + half_bytes * k)
             nc.scalar.copy(
-                repeated[:].rearrange("p c (q b) -> p c q b", b=QUAD),
-                turned[:].rearrange("p (c b k) -> p k c b", c=PACK, k=PACK)[:, k, :, :]
-                .unsqueeze(2).to_broadcast([P, PACK, P // QUAD, QUAD]),
+                repeated[:].rearrange("p c (q u e) -> p c q u e", e=PAIR, u=QUAD // PAIR),
+                turned[:].rearrange("p (c u t e h) -> p t h c u e", c=PACK, t=2, e=PAIR, h=halves)[:, k // 2, k % 2]
+                .unsqueeze(2).to_broadcast([P, PACK, P // QUAD, QUAD // PAIR, PAIR]),
             )
             back_turned = bank(f"back_turned{k}", (3, 5, 6, 7)[k])
             for c in range(PACK):
@@ -177,11 +183,13 @@ def tile_list_matting_patch_weave_kernel(
 
         wi_codes = keep.tile([P, H], I32, name="wi_codes", align_bytes=64)
         nc.vector.tensor_copy(
-            wi_codes[:].rearrange("p (t m) -> p m t", t=PACK), wi_raw[:].rearrange("p (m t) -> p m t", t=PACK)
+            wi_codes[:].rearrange("p (t u e) -> p u t e", t=PACK, e=PAIR),
+            wi_raw[:].rearrange("p (u t e) -> p u t e", t=PACK, e=PAIR),
         )
         wi_plane = keep.tile([P, H], U8, name="wi_plane", align_bytes=64)
         nc.vector.tensor_copy(
-            wi_plane[:].rearrange("p (t m) -> p t m", t=PACK), wi_plane_raw.rearrange("p (m t) -> p t m", t=PACK)
+            wi_plane[:].bitcast(U16).rearrange("p (t u) -> p t u", t=PACK),
+            wi_plane_raw.bitcast(U16).rearrange("p (u t) -> p t u", t=PACK),
         )
 
         def entries(lst, c0, width):
@@ -251,13 +259,13 @@ def tile_list_matting_patch_weave_kernel(
         at_planes = AT_VALUE + ROW + 2 * H
         wb_codes = placed([P, 2, 2 * H], U8, "wb_codes", at_planes - 4 * H)
         nc.vector.tensor_copy(
-            wb_codes[:].bitcast(U16).rearrange("p a (t m) -> p a t m", t=PACK),
-            wb_raw[:].bitcast(U16).rearrange("p a (m t) -> p a t m", t=PACK),
+            wb_codes[:].bitcast(I32).rearrange("p a (t u) -> p a u t", t=PACK),
+            wb_raw[:].bitcast(I32).rearrange("p a (u t) -> p a u t", t=PACK),
         )
         wb_plane = placed([P, 2 * H], U8, "wb_plane", at_planes + 4 * H)
         nc.vector.tensor_copy(
-            wb_plane[:].rearrange("p (a t m) -> p a t m", a=2, t=PACK),
-            wb_plane_raw.rearrange("p (a m t) -> p a t m", a=2, t=PACK),
+            wb_plane[:].bitcast(U16).rearrange("p (a t u) -> p a t u", a=2, t=PACK),
+            wb_plane_raw.bitcast(U16).rearrange("p (a u t) -> p a t u", a=2, t=PACK),
         )
         grouped = [
             placed([P, 2, PACK * H], BF16, f"grouped{w}", AT_GROUPED + pass_bytes * (1 - w)) for w in range(2)
@@ -265,8 +273,8 @@ def tile_list_matting_patch_weave_kernel(
         for w, (raw, sign) in enumerate(((wf_raw, -1.0), (wm_raw, 1.0))):
             for a in range(2):
                 nc.scalar.activation(
-                    grouped[w][:, a, :].rearrange("p (t m i) -> p m t i", t=PACK, i=PACK),
-                    raw[a][:].rearrange("p i (m t) -> p m t i", t=PACK),
+                    grouped[w][:, a, :].rearrange("p (t u x) -> p u t x", t=PACK, x=PAIR * PACK),
+                    raw[a][:].rearrange("p i c -> p c i"),
                     ACT.Copy, scale=sign,
                 )
         w_codes = [placed([P, 2 * H], U32, f"w_codes{w}", AT_CODES + half_bytes * (3 + 2 * w)) for w in range(2)]
@@ -298,7 +306,9 @@ def tile_list_matting_patch_weave_kernel(
         scatter(3, list4, gained3, 0, S)
 
         gains1 = [load_gain(wg1, t, f"gain1_{t}") for t in (0, 1)]
-        wo_raw = load_pass(wo, 0, "wo_raw", AT_LIFT + 2 * ROW)
+        wo_raw = placed([P, PACK, N], F32, "wo_raw", AT_LIFT + 2 * ROW)
+        for t in range(PACK):
+            nc.sync.dma_start(wo_raw[:, t, :], wo.rearrange("(u t e) n -> t u e n", t=PACK, e=PAIR)[t])
         gains1.extend(load_gain(wg1, t, f"gain1_{t}") for t in (2, 3))
 
         def passes(acc, t, h, weights):

@@ -73,6 +73,9 @@ def tile_list_matting_patch_weave_kernel(
         def clear(tile, rows):
             nc.vector.memset(tile[0:rows, :].bitcast(I32), 0)
 
+        def clear_plane(tile):
+            nc.gpsimd.memset(tile[:].bitcast(I32), 0)
+
         def load_list(src, name):
             tile = lists.tile([P, S // GROUP], U16, name=name)
             nc.sync.dma_start(tile[:], src)
@@ -93,50 +96,45 @@ def tile_list_matting_patch_weave_kernel(
             )
             return tile
 
-        raw_planes = keep.tile([P, 3 * H], U8, name="raw_planes", align_bytes=64)
-        clear(raw_planes, P)
-        wi_plane_raw, wb_plane_raw = raw_planes[:, 0:H], raw_planes[:, H : 3 * H]
-        tab2_rows = placed([P, T], U8, "tab2_rows", AT_RAW)
+        wi_plane_tile = placed([P, H], U8, "wi_plane_raw", AT_ROWS + 2 * half_bytes)
+        clear_plane(wi_plane_tile)
+        tab2_rows = placed([P, T], U8, "tab2_rows", AT_CODES + 8 * KIB)
         clear(tab2_rows, P - GROUP)
-        tab_rows = placed([P, T], U8, "tab_rows", AT_RAW + pass_bytes)
+        tab_rows = placed([P, T], U8, "tab_rows", AT_RAW)
         clear(tab_rows, P - 2 * GROUP)
-        moved_planes = keep.tile([P, 3 * S], U8, name="moved_planes", align_bytes=64)
-        clear(moved_planes, P)
-        v2_plane, v_planes = moved_planes[:, 0:S], moved_planes[:, S : 3 * S]
+        v2_plane = keep.tile([P, S], U8, name="v2_plane", align_bytes=64)
+        v_planes = keep.tile([P, 2 * S], U8, name="v_planes", align_bytes=64)
         identity = keep.tile([P, P], F32, name="identity")
         make_identity(nc, identity[:])
+        clear_plane(v2_plane)
         for q in range(P // QUAD):
             nc.gpsimd.dma_start(
-                wi_plane_raw[QUAD * q : QUAD * q + LIVE, :].bitcast(I32),
+                wi_plane_tile[QUAD * q : QUAD * q + LIVE, :].bitcast(I32),
                 wi_scales[0, LIVE * q : LIVE * (q + 1), :].bitcast(I32),
             )
-        for q in range(P // QUAD):
-            nc.gpsimd.dma_start(
-                wb_plane_raw[QUAD * q : QUAD * q + LIVE, :].bitcast(I32).rearrange("p (a c) -> p a c", a=2),
-                wb_scales[:, LIVE * q : LIVE * (q + 1), :].bitcast(I32).rearrange("a r c -> r a c"),
-            )
+        clear_plane(v_planes)
         slopes = keep.tile([P, PAIR * PACK - 1], F32, name="slopes")
-        wi_raw = keep.tile([P, H], I32, name="wi_raw")
-        nc.scalar.dma_start(wi_raw[:], wi_words[0].rearrange("p c i -> p (c i)").bitcast(I32))
-        first_rows = placed([P, HALF], F32, "first_rows", AT_ROWS + ROW)
-        nc.scalar.dma_start(
+        list2 = load_list(offs2, "list2")
+        nc.sync.dma_start(tab2_rows[P - GROUP : P, :].bitcast(I32), tab2_scales[0].bitcast(I32))
+        first_rows = placed([P, HALF], F32, "first_rows", AT_ROWS + ROW + KIB)
+        nc.sync.dma_start(
             first_rows[:],
             wg2.rearrange("(u f) j -> u (f j)", f=PACK * PAIR)[:, 0 : 2 * PAIR * S].rearrange(
                 "u (x j) -> u x j", j=HALF
             ),
         )
+        list1 = load_list(offs, "list1")
         for e in range(PAIR):
-            nc.scalar.dma_start(
+            nc.sync.dma_start(
                 slopes[e:P:PAIR, :], slope.rearrange("(u x) -> u x", x=PACK * PAIR)[:, e : e + PAIR * PACK - 1]
             )
-        list2 = load_list(offs2, "list2")
-        nc.sync.dma_start(tab2_rows[P - GROUP : P, :].bitcast(I32), tab2_scales[0].bitcast(I32))
-        list1 = load_list(offs, "list1")
         nc.sync.dma_start(
             tab_rows[P - 2 * GROUP : P, :].bitcast(I32), tab_scales.bitcast(I32).rearrange("a r t -> r a t")
         )
         tab2_window = placed([P, T], U32, "tab2_window", AT_TAB2)
         nc.sync.dma_start(tab2_window[:].bitcast(I32), tab2_words[0].rearrange("p t i -> p (t i)").bitcast(I32))
+        wi_raw = placed([P, H], I32, "wi_raw", AT_ROWS + half_bytes)
+        nc.sync.dma_start(wi_raw[:], wi_words[0].rearrange("p c i -> p (c i)").bitcast(I32))
         list4 = load_list(offs4, "list4")
         list3 = load_list(offs3, "list3")
 
@@ -146,31 +144,25 @@ def tile_list_matting_patch_weave_kernel(
         v2_rows = placed([P, S], U8, "v2_rows", AT_TAB)
         nc.vector.tensor_copy(v2_rows[:], tab2_rows[:].indirect(list2[:]))
         for q in range(P // QUAD):
-            nc.scalar.dma_start(
+            nc.sync.dma_start(
                 v2_plane[QUAD * q : QUAD * q + LIVE, :].bitcast(I32),
                 v2_rows[P - GROUP + LIVE * q : P - GROUP + LIVE * (q + 1), :].bitcast(I32),
             )
-        wf_raw = [load_pass(wf, 0, "wf_raw0", AT_RAW)]
 
         turned = bank("turned", 2)
         for c in range(PACK):
             nc.tensor.transpose(turned[:, c * P : (c + 1) * P], first_rows[:, c * P : (c + 1) * P], identity[:])
-        wb_raw = placed([P, 2, 2 * H], U8, "wb_raw", AT_ROWS + ROW)
-        nc.sync.dma_start(wb_raw[:].bitcast(I32), wb_words.bitcast(I32).rearrange("a p c -> p a c"))
         v_rows = placed([P, S], U8, "v_rows", AT_RAW + 3 * pass_bytes - S // 2)
         nc.vector.tensor_copy(v_rows[:], tab_rows[:].indirect(list1[:]))
+        wf_raw = [load_pass(wf, 0, "wf_raw0", AT_RAW)]
         for q in range(P // QUAD):
             nc.sync.dma_start(
                 v_planes[QUAD * q : QUAD * q + LIVE, :].bitcast(I32).rearrange("p (a c) -> p a c", a=2),
                 v_rows[P - 2 * GROUP + 2 * LIVE * q : P - 2 * GROUP + 2 * LIVE * (q + 1), :].bitcast(I32),
             )
-        wf_raw.append(load_pass(wf, 1, "wf_raw1", AT_RAW + pass_bytes))
-        tab_window = placed([P, 2, T], U32, "tab_window", AT_TAB)
-        nc.sync.dma_start(tab_window[:].bitcast(I32), tab_words.rearrange("a p t i -> p a (t i)").bitcast(I32))
-        wm_raw = [load_pass(wm, a, f"wm_raw{a}", AT_RAW + pass_bytes * (2 + a)) for a in range(2)]
         gains2 = [placed([P, S], F32, f"gain2_{t}", AT_GAIN + ROW * t) for t in range(2)]
         for k in range(PACK):
-            repeated = placed([P, PACK, P], F32, f"repeated{k}", AT_CODES + half_bytes * k)
+            repeated = placed([P, PACK, P], F32, f"repeated{k}", AT_CODES + half_bytes * k if k else AT_RAW + pass_bytes)
             nc.scalar.copy(
                 repeated[:].rearrange("p c (q u e) -> p c q u e", e=PAIR, u=QUAD // PAIR),
                 turned[:].rearrange("p (c u t e h) -> p t h c u e", c=PACK, t=2, e=PAIR, h=halves)[:, k // 2, k % 2]
@@ -181,6 +173,20 @@ def tile_list_matting_patch_weave_kernel(
                 nc.tensor.transpose(back_turned[:, c * P : (c + 1) * P], repeated[:, c, :], identity[:])
             nc.scalar.copy(gains2[k // 2][:, HALF * (k % 2) : HALF * (k % 2 + 1)], back_turned[:])
 
+        wf_raw.append(load_pass(wf, 1, "wf_raw1", AT_RAW + pass_bytes))
+        wb_raw = placed([P, 2, 2 * H], U8, "wb_raw", AT_CODES + half_bytes)
+        nc.sync.dma_start(wb_raw[:].bitcast(I32), wb_words.bitcast(I32).rearrange("a p c -> p a c"))
+        wb_plane_raw = placed([P, 2 * H], U8, "wb_plane_raw", AT_CODES + half_bytes * 2)
+        clear_plane(wb_plane_raw)
+        for q in range(P // QUAD):
+            nc.sync.dma_start(
+                wb_plane_raw[QUAD * q : QUAD * q + LIVE, :].bitcast(I32).rearrange("p (a c) -> p a c", a=2),
+                wb_scales[:, LIVE * q : LIVE * (q + 1), :].bitcast(I32).rearrange("a r c -> r a c"),
+            )
+        tab_window = placed([P, 2, T], U32, "tab_window", AT_TAB)
+        nc.sync.dma_start(tab_window[:].bitcast(I32), tab_words.rearrange("a p t i -> p a (t i)").bitcast(I32))
+        wm_raw = [load_pass(wm, a, f"wm_raw{a}", AT_RAW + pass_bytes * (2 + a)) for a in range(2)]
+
         wi_codes = keep.tile([P, H], I32, name="wi_codes", align_bytes=64)
         nc.vector.tensor_copy(
             wi_codes[:].rearrange("p (t u e) -> p u t e", t=PACK, e=PAIR),
@@ -189,13 +195,13 @@ def tile_list_matting_patch_weave_kernel(
         wi_plane = keep.tile([P, H], U8, name="wi_plane", align_bytes=64)
         nc.vector.tensor_copy(
             wi_plane[:].bitcast(U16).rearrange("p (t u) -> p t u", t=PACK),
-            wi_plane_raw.bitcast(U16).rearrange("p (u t) -> p t u", t=PACK),
+            wi_plane_tile[:].bitcast(U16).rearrange("p (u t) -> p t u", t=PACK),
         )
 
         def entries(lst, c0, width):
             return lst[:] if width == S else lst[:, c0 // GROUP : (c0 + width) // GROUP]
 
-        v2_codes = [placed([P, HALF], U32, f"v2_codes{h}", AT_ROWS + half_bytes * h) for h in range(halves)]
+        v2_codes = [placed([P, HALF], U32, f"v2_codes{h}", AT_ROWS + (half_bytes + H) * h) for h in range(halves)]
         for h in range(halves):
             nc.vector.tensor_copy(v2_codes[h][:], tab2_window[:].indirect(entries(list2, h * HALF, HALF)))
         after_wb_codes = AT_TAB2 + 4 * H
@@ -265,7 +271,7 @@ def tile_list_matting_patch_weave_kernel(
         wb_plane = placed([P, 2 * H], U8, "wb_plane", at_planes + 4 * H)
         nc.vector.tensor_copy(
             wb_plane[:].bitcast(U16).rearrange("p (a t u) -> p a t u", a=2, t=PACK),
-            wb_plane_raw.bitcast(U16).rearrange("p (a u t) -> p a t u", a=2, t=PACK),
+            wb_plane_raw[:].bitcast(U16).rearrange("p (a u t) -> p a t u", a=2, t=PACK),
         )
         grouped = [
             placed([P, 2, PACK * H], BF16, f"grouped{w}", AT_GROUPED + pass_bytes * (1 - w)) for w in range(2)

@@ -263,26 +263,29 @@ def tile_list_matting_patch_weave_kernel(
         nc.gpsimd.tensor_tensor(leaky2[:], interior[2][0][:], interior[2][1][:], ALU.add)
 
         at_planes = AT_VALUE + ROW + 2 * H
-        wb_codes = placed([P, 2, 2 * H], U8, "wb_codes", at_planes - 4 * H)
-        nc.vector.tensor_copy(
-            wb_codes[:].bitcast(I32).rearrange("p a (t u) -> p a u t", t=PACK),
-            wb_raw[:].bitcast(I32).rearrange("p a (u t) -> p a u t", t=PACK),
+        wb_codes = keep.tile([P, 2, 2 * H], U8, name="wb_codes", align_bytes=64)
+        nc.scalar.copy(
+            wb_codes[:].bitcast(U32).rearrange("p a (t u) -> p a u t", t=PACK),
+            wb_raw[:].bitcast(U32).rearrange("p a (u t) -> p a u t", t=PACK),
         )
-        wb_plane = placed([P, 2 * H], U8, "wb_plane", at_planes + 4 * H)
-        nc.vector.tensor_copy(
+        wb_plane = keep.tile([P, 2 * H], U8, name="wb_plane", align_bytes=64)
+        nc.scalar.copy(
             wb_plane[:].bitcast(U16).rearrange("p (a t u) -> p a t u", a=2, t=PACK),
             wb_plane_raw[:].bitcast(U16).rearrange("p (a u t) -> p a t u", a=2, t=PACK),
         )
         grouped = [
             placed([P, 2, PACK * H], BF16, f"grouped{w}", AT_GROUPED + pass_bytes * (1 - w)) for w in range(2)
         ]
-        for w, (raw, sign) in enumerate(((wf_raw, -1.0), (wm_raw, 1.0))):
-            for a in range(2):
-                nc.scalar.activation(
-                    grouped[w][:, a, :].rearrange("p (t u x) -> p u t x", t=PACK, x=PAIR * PACK),
-                    raw[a][:].rearrange("p i c -> p c i"),
-                    ACT.Copy, scale=sign,
-                )
+        for a in range(2):
+            rounded = grouped[0][:, a, :].rearrange("p (t u e i) -> p t u i e", t=PACK, e=PAIR, i=PACK)
+            loaded = wf_raw[a][:].rearrange("p i (u t e) -> p t u i e", t=PACK, e=PAIR)
+            for t in range(PACK):
+                nc.scalar.activation(rounded[:, t], loaded[:, t], ACT.Copy, scale=-1.0)
+        for a in range(2):
+            nc.scalar.copy(
+                grouped[1][:, a, :].rearrange("p (t u e i) -> p u t i e", t=PACK, e=PAIR, i=PACK),
+                wm_raw[a][:].rearrange("p i (u t e) -> p u t i e", t=PACK, e=PAIR),
+            )
         w_codes = [placed([P, 2 * H], U32, f"w_codes{w}", AT_CODES + half_bytes * (3 + 2 * w)) for w in range(2)]
         w_plane = [placed([P, 2 * H], U8, f"w_plane{w}", at_planes + 2 * H * w) for w in range(2)]
         v_places = ((2, 7), (1, 0))

@@ -36,6 +36,7 @@ SUMMED_UNITS = 3
 TURN_BANKS = 3
 CHUNKS = (128, 128, 256, 512, 512, 512)
 PIECE = 256
+PLACE = (0, 2, 3, 1)
 
 AT_TAB2 = 0
 AT_TAB = 16 * KIB
@@ -208,8 +209,8 @@ def tile_list_matting_patch_weave_kernel(
 
         page2_overlap = 2 * KIB
         pages = [
-            placed([P, T2], F32, "page2", AT_GROUPED + page2_overlap - WORD * T2)
-            if t == 2
+            placed([P, T2], F32, f"page{t}", AT_GROUPED + page2_overlap + WORD * T2 * (t - 3))
+            if t >= 2
             else keep.tile([P, T2], F32, name=f"page{t}")
             for t in range(PACK)
         ]
@@ -261,6 +262,9 @@ def tile_list_matting_patch_weave_kernel(
         interior.extend(interior_slice(t) for t in (1, 2, 3))
         leaky2 = placed([P, S], F32, "leaky2", AT_SLOT)
         nc.gpsimd.tensor_tensor(leaky2[:], interior[2][0][:], interior[2][1][:], ALU.add)
+        at_edge_slot = AT_LIFT + 2 * ROW
+        leaky3 = placed([P, S], F32, "leaky3", at_edge_slot)
+        nc.gpsimd.tensor_tensor(leaky3[:], interior[3][0][:], interior[3][1][:], ALU.add)
 
         at_planes = AT_VALUE + ROW + 2 * H
         wb_codes = keep.tile([P, 2, 2 * H], U8, name="wb_codes", align_bytes=64)
@@ -295,12 +299,11 @@ def tile_list_matting_patch_weave_kernel(
                 w_codes[w][:].bitcast(FP8X4), w_plane[w][:], grouped[w][:].rearrange("p a x -> p (a x)")
             )
 
-        at_edge_slot = AT_GROUPED + pass_bytes + ROW
         quantise_weight(0)
-        leaky3 = placed([P, S], F32, "leaky3", at_edge_slot)
-        nc.gpsimd.tensor_tensor(leaky3[:], interior[3][0][:], interior[3][1][:], ALU.add)
         gained2 = placed([P, S], F32, "gained2", AT_GROUPED + pass_bytes)
         nc.gpsimd.tensor_tensor(gained2[:], leaky2[:], gains2[2][:], ALU.mult)
+        gained3 = placed([P, S], F32, "gained3", AT_SLOT)
+        nc.gpsimd.tensor_tensor(gained3[:], leaky3[:], gains2[3][:], ALU.mult)
         v_codes = [
             [placed([P, HALF], U32, f"v_codes{h}{a}", AT_CODES + half_bytes * v_places[h][a]) for a in range(2)]
             for h in range(halves)
@@ -309,15 +312,13 @@ def tile_list_matting_patch_weave_kernel(
             for a in range(2):
                 nc.vector.tensor_copy(v_codes[h][a][:], tab_window[:, a, :].indirect(entries(list1, h * HALF, HALF)))
         quantise_weight(1)
-        gained3 = placed([P, S], F32, "gained3", AT_GROUPED + page2_overlap)
-        nc.gpsimd.tensor_tensor(gained3[:], leaky3[:], gains2[3][:], ALU.mult)
         scatter(2, list4, gained2, 0, S)
         scatter(3, list4, gained3, 0, S)
 
         gains1 = [load_gain(wg1, t, f"gain1_{t}") for t in (0, 1)]
-        wo_raw = placed([P, PACK, N], F32, "wo_raw", AT_LIFT + 2 * ROW)
+        wo_raw = placed([P, PACK, N], F32, "wo_raw", AT_VALUE + 2 * ROW)
         for t in range(PACK):
-            nc.sync.dma_start(wo_raw[:, t, :], wo.rearrange("(u t e) n -> t u e n", t=PACK, e=PAIR)[t])
+            nc.sync.dma_start(wo_raw[:, PLACE[t], :], wo.rearrange("(u t e) n -> t u e n", t=PACK, e=PAIR)[t])
         gains1.extend(load_gain(wg1, t, f"gain1_{t}") for t in (2, 3))
 
         def passes(acc, t, h, weights):
@@ -346,6 +347,22 @@ def tile_list_matting_patch_weave_kernel(
                 nc.gpsimd.tensor_tensor(work[:], value[:, cols], back[:, cols], ALU.add)
                 nc.gpsimd.tensor_tensor(work[:], work[:], matte[:, cols], ALU.mult)
                 nc.gpsimd.tensor_tensor(value[:, cols], back[:, cols], work[:], ALU.subtract)
+
+        def add_by_turning(value, back, unit):
+            blocks = [slice(c * P, (c + 1) * P) for c in range(PACK)]
+            summed = bank(f"summed{unit}", unit)
+            for block in blocks:
+                for number, term in enumerate((value, back)):
+                    nc.tensor.matmul(
+                        summed[:, block], lhsT=term[:, block], rhs=identity[:], is_transpose=True,
+                        start=(number == 0), stop=(number == 1),
+                    )
+            turned_sum = placed([P, HALF], F32, f"turned_sum{unit}", AT_VALUE + half_bytes * (unit % halves))
+            nc.scalar.copy(turned_sum[:], summed[:])
+            upright = bank(f"upright{unit}", unit)
+            for block in blocks:
+                nc.tensor.transpose(upright[:, block], turned_sum[:, block], identity[:])
+            nc.scalar.copy(value, upright[:])
 
         turns = []
 
@@ -384,10 +401,12 @@ def tile_list_matting_patch_weave_kernel(
                     passes(mt, t, h, "m")
                     nc.scalar.activation(matte[:, cols], mt[:], ACT.Sigmoid)
                     passes(less_fg, t, h, "f")
-                    if t < PACK - 1:
+                    if t == 1:
                         nc.vector.tensor_tensor(value[:, cols], less_fg[:], back[:, cols], ALU.add)
                     else:
                         nc.scalar.copy(value[:, cols], less_fg[:])
+                    if t == 2:
+                        add_by_turning(value[:, cols], back[:, cols], unit)
                 if t < 2:
                     blend(t, value, matte, back, h * HALF, HALF)
             if t >= 2:
@@ -406,26 +425,20 @@ def tile_list_matting_patch_weave_kernel(
         wo_plane = placed([P, N], U8, "wo_plane", after_wb_codes + 2 * ROW)
 
         starts = [sum(CHUNKS[:i]) for i in range(len(CHUNKS))]
-        woven = [
-            placed([P, width, PACK], BF16, f"woven{i}", AT_CODES + 2 * PACK * starts[i])
-            for i, width in enumerate(CHUNKS)
-        ]
-        for t in range(PACK - 1):
-            for i, width in enumerate(CHUNKS):
-                src = pages[t][:, starts[i] : starts[i] + width]
-                if t < 2:
-                    nc.scalar.copy(woven[i][:, :, t], src)
-                else:
-                    nc.scalar.copy(woven[i][:, :, 2:4], src.unsqueeze(2).to_broadcast([P, width, 2]))
+        woven = placed([P, T2, PACK], BF16, "woven", AT_CODES)
+        nc.scalar.copy(woven[:, :, 0:2], pages[0][:].unsqueeze(2).to_broadcast([P, T2, 2]))
+        nc.scalar.copy(woven[:, :, PLACE[1]], pages[1][:])
+        for i, width in enumerate(CHUNKS):
+            cols = slice(starts[i], starts[i] + width)
+            nc.scalar.copy(woven[:, cols, PLACE[2]], pages[2][:, cols])
         out_rows = out.rearrange("(n p) c -> p n c", p=P)
         pieces = [
             (i, c0, min(width, PIECE)) for i, width in enumerate(CHUNKS) for c0 in range(0, width, PIECE)
         ]
         turns.clear()
         for k, (i, c0, width) in enumerate(pieces):
-            piece = slice(c0, c0 + width)
             cols = slice(starts[i] + c0, starts[i] + c0 + width)
-            nc.vector.tensor_copy(woven[i][:, piece, 3], pages[3][:, cols])
+            nc.vector.tensor_copy(woven[:, cols, PLACE[3]], pages[3][:, cols])
             if k == 0:
                 for n0, n1 in ((0, 2 * P), (2 * P, N)):
                     nc.vector.quantize_mx(
@@ -434,7 +447,7 @@ def tile_list_matting_patch_weave_kernel(
             codes = keep.tile([P, width], U32, name=f"page_codes{k}", align_bytes=64)
             plane = keep.tile([P, width], U8, name=f"page_plane{k}", align_bytes=64)
             nc.vector.quantize_mx(
-                codes[:].bitcast(FP8X4), plane[:], woven[i][:, piece, :].rearrange("p c t -> p (c t)")
+                codes[:].bitcast(FP8X4), plane[:], woven[:, cols, :].rearrange("p c t -> p (c t)")
             )
             result = placed([P, N // P, width], F32, f"result{k}", AT_TAB + WORD * (N // P) * cols.start)
             for n0 in range(0, N // P, HALF // width):

@@ -25,29 +25,29 @@ LIVE = 4
 GROUP = 16
 PASS = P * PACK
 HALF = 512
+QUARTER = 256
 BANKS = 8
 WORD = 4
 KIB = 1024
 ROW = WORD * S
 
-FIRST_PIECES = ((0, 256), (256, 256), (512, 512))
-INTERIOR_BANKS = (0, 4, 1)
-SUMMED_UNITS = 3
-TURN_BANKS = 3
-CHUNKS = (128, 128, 256, 512, 512, 512)
-PIECE = 256
+SUMMED_UNITS = (0, 1, 2)
+TURNED_UNITS = (4, 5)
+PIECES = (128, 128, 256, 256, 256, 256, 256, 256, 256)
+WEAVE_CHUNKS = (256, 256, 512, 512, 512)
 PLACE = (0, 2, 3, 1)
 
-AT_TAB2 = 0
-AT_TAB = 16 * KIB
-AT_GROUPED = 48 * KIB
-AT_RAW = 64 * KIB
-AT_CODES = 96 * KIB
+AT_RAW = 0
+AT_TAB2 = 32 * KIB
+AT_TAB = 48 * KIB
+AT_GAIN = 80 * KIB
+AT_VALUE = 96 * KIB
 AT_LIFT = 112 * KIB
-AT_VALUE = 128 * KIB
-AT_GAIN = 144 * KIB
-AT_SLOT = 163 * KIB
-AT_ROWS = 168 * KIB
+AT_GROUPED = 128 * KIB
+AT_CODES = 144 * KIB
+AT_SMALL = 152 * KIB
+AT_PAGE0 = 164 * KIB
+AT_EDGE = 172 * KIB
 
 
 def tile_list_matting_patch_weave_kernel(
@@ -55,7 +55,6 @@ def tile_list_matting_patch_weave_kernel(
     wm, wi_words, wi_scales, slope, wg1, wg2, wo, out,
 ):
     nc = tc.nc
-    halves = S // HALF
     half_bytes = WORD * HALF
     pass_bytes = WORD * PACK * H
 
@@ -71,202 +70,263 @@ def tile_list_matting_patch_weave_kernel(
         def bank(name, number):
             return psum.tile([P, HALF], F32, name=name, tag=f"bank{number}")
 
-        def clear(tile, rows):
-            nc.vector.memset(tile[0:rows, :].bitcast(I32), 0)
-
-        def clear_plane(tile):
-            nc.gpsimd.memset(tile[:].bitcast(I32), 0)
-
         def load_list(src, name):
             tile = lists.tile([P, S // GROUP], U16, name=name)
             nc.sync.dma_start(tile[:], src)
             return tile
 
-        def load_gain(src, t, name):
-            tile = placed([P, S], F32, name, AT_GAIN + ROW * t)
-            rows = src.rearrange("(u t e) j -> t u e j", t=PACK, e=PAIR)[t]
+        def load_gain(src, t, c0, width, name, offset):
+            tile = placed([P, width], F32, name, offset)
+            rows = src.rearrange("(u t e) j -> t u e j", t=PACK, e=PAIR)[t][:, :, c0 : c0 + width]
             for q in (0, 2, 1, 3):
                 nc.sync.dma_start(tile[QUAD * q : QUAD * (q + 1), :], rows)
             return tile
 
         def load_pass(src, a, name, offset):
-            tile = placed([P, PACK, src.shape[1]], F32, name, offset)
+            tile = placed([P, PACK, H], F32, name, offset)
             nc.sync.dma_start(
                 tile[:].rearrange("p i c -> p (i c)"),
                 src[a * PASS : (a + 1) * PASS, :].rearrange("(p i) c -> p (i c)", i=PACK),
             )
             return tile
 
-        wi_plane_tile = placed([P, H], U8, "wi_plane_raw", AT_ROWS + 2 * half_bytes)
-        clear_plane(wi_plane_tile)
-        tab2_rows = placed([P, T], U8, "tab2_rows", AT_CODES + 8 * KIB)
-        clear(tab2_rows, P - GROUP)
-        tab_rows = placed([P, T], U8, "tab_rows", AT_RAW)
-        clear(tab_rows, P - 2 * GROUP)
-        v2_plane = keep.tile([P, S], U8, name="v2_plane", align_bytes=64)
-        v_planes = keep.tile([P, 2 * S], U8, name="v_planes", align_bytes=64)
+        def load_words(src, name, offset):
+            tile = placed([P, T], U32, name, offset)
+            nc.sync.dma_start(tile[:].bitcast(I32), src.rearrange("p t i -> p (t i)").bitcast(I32))
+            return tile
+
+        def entries(lst, c0, width):
+            return lst[:] if width == S else lst[:, c0 // GROUP : (c0 + width) // GROUP]
+
+        tab2_rows = placed([P, T], U8, "tab2_rows", AT_RAW)
+        nc.vector.memset(tab2_rows[0 : P - GROUP, :].bitcast(I32), 0)
+        tab_rows = placed([P, T], U8, "tab_rows", AT_RAW + 2 * pass_bytes - T // 2)
+        nc.vector.memset(tab_rows[0 : P - 2 * GROUP, :].bitcast(I32), 0)
+        wi_plane_raw = placed([P, H], U8, "wi_plane_raw", AT_SMALL + 8 * KIB)
+        nc.gpsimd.memset(wi_plane_raw[:].bitcast(I32), 0)
         identity = keep.tile([P, P], F32, name="identity")
         make_identity(nc, identity[:])
-        clear_plane(v2_plane)
-        for q in range(P // QUAD):
-            nc.gpsimd.dma_start(
-                wi_plane_tile[QUAD * q : QUAD * q + LIVE, :].bitcast(I32),
-                wi_scales[0, LIVE * q : LIVE * (q + 1), :].bitcast(I32),
-            )
-        clear_plane(v_planes)
-        slopes = keep.tile([P, PAIR * PACK - 1], F32, name="slopes")
+        v2_plane = keep.tile([P, S], U8, name="v2_plane", align_bytes=64)
+        nc.gpsimd.memset(v2_plane[:].bitcast(I32), 0)
+        wi_rows = placed([LIVE, P // QUAD, H], U8, "wi_rows", AT_SMALL + 9 * KIB)
+        nc.gpsimd.dma_start(wi_rows[:].bitcast(I32), wi_scales[0].bitcast(I32).rearrange("(q r) c -> r q c", r=LIVE))
+        v_planes = keep.tile([P, 2 * S], U8, name="v_planes", align_bytes=64)
+        nc.gpsimd.memset(v_planes[:].bitcast(I32), 0)
+
         list2 = load_list(offs2, "list2")
         nc.sync.dma_start(tab2_rows[P - GROUP : P, :].bitcast(I32), tab2_scales[0].bitcast(I32))
-        first_rows = placed([P, HALF], F32, "first_rows", AT_ROWS + ROW + KIB)
+        list1 = load_list(offs, "list1")
+        nc.sync.dma_start(
+            tab_rows[P - 2 * GROUP : P, :].bitcast(I32), tab_scales.bitcast(I32).rearrange("a r t -> r a t")
+        )
+        first_rows = placed([P, HALF], F32, "first_rows", AT_SMALL + 6 * KIB)
         nc.sync.dma_start(
             first_rows[:],
             wg2.rearrange("(u f) j -> u (f j)", f=PACK * PAIR)[:, 0 : 2 * PAIR * S].rearrange(
                 "u (x j) -> u x j", j=HALF
             ),
         )
-        list1 = load_list(offs, "list1")
-        for e in range(PAIR):
+        wi_raw = placed([P, H], I32, "wi_raw", AT_RAW + 3 * pass_bytes + 2 * KIB)
+        nc.sync.dma_start(wi_raw[:], wi_words[0].rearrange("p c i -> p (c i)").bitcast(I32))
+        slopes = keep.tile([P, PAIR * PACK - 1], F32, name="slopes")
+
+        def load_slopes(e):
             nc.sync.dma_start(
                 slopes[e:P:PAIR, :], slope.rearrange("(u x) -> u x", x=PACK * PAIR)[:, e : e + PAIR * PACK - 1]
             )
-        nc.sync.dma_start(
-            tab_rows[P - 2 * GROUP : P, :].bitcast(I32), tab_scales.bitcast(I32).rearrange("a r t -> r a t")
-        )
-        tab2_window = placed([P, T], U32, "tab2_window", AT_TAB2)
-        nc.sync.dma_start(tab2_window[:].bitcast(I32), tab2_words[0].rearrange("p t i -> p (t i)").bitcast(I32))
-        wi_raw = placed([P, H], I32, "wi_raw", AT_ROWS + half_bytes)
-        nc.sync.dma_start(wi_raw[:], wi_words[0].rearrange("p c i -> p (c i)").bitcast(I32))
+
+        load_slopes(0)
+        tab2_window = load_words(tab2_words[0], "tab2_window", AT_TAB2)
+        load_slopes(1)
         list4 = load_list(offs4, "list4")
         list3 = load_list(offs3, "list3")
 
-        slope_less_one = keep.tile([P, PACK], F32, name="slope_less_one")
-        nc.scalar.activation(slope_less_one[:], slopes[:, 0 : PAIR * PACK - 1 : PAIR], ACT.Identity, bias=-1.0)
-
-        v2_rows = placed([P, S], U8, "v2_rows", AT_TAB)
+        v2_rows = placed([P, S], U8, "v2_rows", AT_SMALL + 4 * KIB)
         nc.vector.tensor_copy(v2_rows[:], tab2_rows[:].indirect(list2[:]))
         for q in range(P // QUAD):
             nc.sync.dma_start(
                 v2_plane[QUAD * q : QUAD * q + LIVE, :].bitcast(I32),
                 v2_rows[P - GROUP + LIVE * q : P - GROUP + LIVE * (q + 1), :].bitcast(I32),
             )
-
-        turned = bank("turned", 2)
-        for c in range(PACK):
-            nc.tensor.transpose(turned[:, c * P : (c + 1) * P], first_rows[:, c * P : (c + 1) * P], identity[:])
-        v_rows = placed([P, S], U8, "v_rows", AT_RAW + 3 * pass_bytes - S // 2)
+        v_rows = placed([P, S], U8, "v_rows", AT_SMALL + 5 * KIB)
         nc.vector.tensor_copy(v_rows[:], tab_rows[:].indirect(list1[:]))
-        wf_raw = [load_pass(wf, 0, "wf_raw0", AT_RAW)]
+        wf_raw = [load_pass(wf, a, f"wf_raw{a}", AT_RAW + pass_bytes * a) for a in range(2)]
+        wm_raw = [load_pass(wm, 0, "wm_raw0", AT_RAW + 2 * pass_bytes)]
         for q in range(P // QUAD):
             nc.sync.dma_start(
                 v_planes[QUAD * q : QUAD * q + LIVE, :].bitcast(I32).rearrange("p (a c) -> p a c", a=2),
                 v_rows[P - 2 * GROUP + 2 * LIVE * q : P - 2 * GROUP + 2 * LIVE * (q + 1), :].bitcast(I32),
             )
-        gains2 = [placed([P, S], F32, f"gain2_{t}", AT_GAIN + ROW * t) for t in range(2)]
-        for k in range(PACK):
-            repeated = placed([P, PACK, P], F32, f"repeated{k}", AT_CODES + half_bytes * k if k else AT_RAW + pass_bytes)
-            nc.scalar.copy(
-                repeated[:].rearrange("p c (q u e) -> p c q u e", e=PAIR, u=QUAD // PAIR),
-                turned[:].rearrange("p (c u t e h) -> p t h c u e", c=PACK, t=2, e=PAIR, h=halves)[:, k // 2, k % 2]
-                .unsqueeze(2).to_broadcast([P, PACK, P // QUAD, QUAD // PAIR, PAIR]),
-            )
-            back_turned = bank(f"back_turned{k}", (3, 5, 6, 7)[k])
-            for c in range(PACK):
-                nc.tensor.transpose(back_turned[:, c * P : (c + 1) * P], repeated[:, c, :], identity[:])
-            nc.scalar.copy(gains2[k // 2][:, HALF * (k % 2) : HALF * (k % 2 + 1)], back_turned[:])
-
-        wf_raw.append(load_pass(wf, 1, "wf_raw1", AT_RAW + pass_bytes))
-        wb_raw = placed([P, 2, 2 * H], U8, "wb_raw", AT_CODES + half_bytes)
-        nc.sync.dma_start(wb_raw[:].bitcast(I32), wb_words.bitcast(I32).rearrange("a p c -> p a c"))
-        wb_plane_raw = placed([P, 2 * H], U8, "wb_plane_raw", AT_CODES + half_bytes * 2)
-        clear_plane(wb_plane_raw)
-        for q in range(P // QUAD):
-            nc.sync.dma_start(
-                wb_plane_raw[QUAD * q : QUAD * q + LIVE, :].bitcast(I32).rearrange("p (a c) -> p a c", a=2),
-                wb_scales[:, LIVE * q : LIVE * (q + 1), :].bitcast(I32).rearrange("a r c -> r a c"),
-            )
-        tab_window = placed([P, 2, T], U32, "tab_window", AT_TAB)
-        nc.sync.dma_start(tab_window[:].bitcast(I32), tab_words.rearrange("a p t i -> p a (t i)").bitcast(I32))
-        wm_raw = [load_pass(wm, a, f"wm_raw{a}", AT_RAW + pass_bytes * (2 + a)) for a in range(2)]
 
         wi_codes = keep.tile([P, H], I32, name="wi_codes", align_bytes=64)
         nc.vector.tensor_copy(
             wi_codes[:].rearrange("p (t u e) -> p u t e", t=PACK, e=PAIR),
             wi_raw[:].rearrange("p (u t e) -> p u t e", t=PACK, e=PAIR),
         )
+        for q in range(P // QUAD):
+            nc.vector.tensor_copy(
+                wi_plane_raw[QUAD * q : QUAD * q + LIVE, :].bitcast(I32), wi_rows[:, q, :].bitcast(I32)
+            )
         wi_plane = keep.tile([P, H], U8, name="wi_plane", align_bytes=64)
         nc.vector.tensor_copy(
             wi_plane[:].bitcast(U16).rearrange("p (t u) -> p t u", t=PACK),
-            wi_plane_tile[:].bitcast(U16).rearrange("p (u t) -> p t u", t=PACK),
+            wi_plane_raw[:].bitcast(U16).rearrange("p (u t) -> p t u", t=PACK),
         )
+        wm_raw.append(load_pass(wm, 1, "wm_raw1", AT_RAW + 3 * pass_bytes))
 
-        def entries(lst, c0, width):
-            return lst[:] if width == S else lst[:, c0 // GROUP : (c0 + width) // GROUP]
+        turned = bank("turned", 4)
+        for c in range(PACK):
+            nc.tensor.transpose(turned[:, c * P : (c + 1) * P], first_rows[:, c * P : (c + 1) * P], identity[:])
+        first_gains = [placed([P, S], F32, f"gain2_{t}", AT_GAIN + ROW * t) for t in range(2)]
+        at_gain2a = AT_GAIN + 2 * ROW
+        at_wb_raw = at_gain2a + half_bytes
+        at_repeated = (AT_TAB, at_wb_raw + KIB, AT_TAB + WORD * T, at_gain2a)
+        for k in range(PACK):
+            repeated = placed([P, PACK, P], F32, f"repeated{k}", at_repeated[k])
+            nc.scalar.copy(
+                repeated[:].rearrange("p c (q u e) -> p c q u e", e=PAIR, u=QUAD // PAIR),
+                turned[:].rearrange("p (c u t e h) -> p t h c u e", c=PACK, t=2, e=PAIR, h=2)[:, k % 2, k // 2]
+                .unsqueeze(2).to_broadcast([P, PACK, P // QUAD, QUAD // PAIR, PAIR]),
+            )
+            back_turned = bank(f"back_turned{k}", 5 + k % 3)
+            for c in range(PACK):
+                nc.tensor.transpose(back_turned[:, c * P : (c + 1) * P], repeated[:, c, :], identity[:])
+            nc.scalar.copy(first_gains[k % 2][:, HALF * (k // 2) : HALF * (k // 2 + 1)], back_turned[:])
 
-        v2_codes = [placed([P, HALF], U32, f"v2_codes{h}", AT_ROWS + (half_bytes + H) * h) for h in range(halves)]
-        for h in range(halves):
-            nc.vector.tensor_copy(v2_codes[h][:], tab2_window[:].indirect(entries(list2, h * HALF, HALF)))
-        after_wb_codes = AT_TAB2 + 4 * H
+        slope_less_one = keep.tile([P, PACK], F32, name="slope_less_one")
+        nc.scalar.activation(slope_less_one[:], slopes[:, 0 : PAIR * PACK - 1 : PAIR], ACT.Identity, bias=-1.0)
+        tab_windows = [load_words(tab_words[0], "tab_window0", AT_TAB)]
+        wb_raw = placed([P, 2, 2 * H], U8, "wb_raw", at_wb_raw)
+        nc.sync.dma_start(wb_raw[:].bitcast(I32), wb_words.bitcast(I32).rearrange("a p c -> p a c"))
+        wb_plane_raw = placed([P, 2 * H], U8, "wb_plane_raw", at_wb_raw + half_bytes)
+        nc.gpsimd.memset(wb_plane_raw[:].bitcast(I32), 0)
+        for q in range(P // QUAD):
+            nc.sync.dma_start(
+                wb_plane_raw[QUAD * q : QUAD * q + LIVE, :].bitcast(I32).rearrange("p (a c) -> p a c", a=2),
+                wb_scales[:, LIVE * q : LIVE * (q + 1), :].bitcast(I32).rearrange("a r c -> r a c"),
+            )
+        tab_windows.append(load_words(tab_words[1], "tab_window1", AT_TAB + WORD * T))
 
-        page2_overlap = 2 * KIB
         pages = [
-            placed([P, T2], F32, f"page{t}", AT_GROUPED + page2_overlap + WORD * T2 * (t - 3))
-            if t >= 2
-            else keep.tile([P, T2], F32, name=f"page{t}")
-            for t in range(PACK)
+            placed([P, T2], F32, "page0", AT_PAGE0),
+            keep.tile([P, T2], F32, name="page1"),
+            keep.tile([P, T2], F32, name="page2"),
         ]
 
         def scatter(t, lst, value, c0, width):
-            nc.vector.tensor_copy(pages[t][:].indirect(entries(lst, c0, width)), value[:, c0 : c0 + width])
+            nc.vector.tensor_copy(pages[t][:].indirect(entries(lst, c0, width)), value)
 
-        def interior_product(number, t, c0, width):
-            h = c0 // HALF
+        v2_codes = {}
+
+        def gather_v2(c0, width):
+            tile = placed([P, width], U32, f"v2_codes{c0}", AT_SMALL + WORD * c0)
+            nc.vector.tensor_copy(tile[:], tab2_window[:].indirect(entries(list2, c0, width)))
+            for x in range(0, width, QUARTER):
+                v2_codes[c0 + x] = tile[:, x : x + QUARTER]
+
+        interior_banks = []
+
+        def interior_product(t, c0, width):
             cols_w = slice(t * P, (t + 1) * P)
-            d = bank(f"d{t}_{c0}", INTERIOR_BANKS[number % len(INTERIOR_BANKS)])[:, 0:width]
-            nc.tensor.matmul_mx(
-                d, lhsT=wi_codes[:, cols_w].bitcast(FP8X4), lhsT_scale=wi_plane[:, cols_w],
-                rhs=v2_codes[h][:, c0 - h * HALF : c0 - h * HALF + width].bitcast(FP8X4),
-                rhs_scale=v2_plane[:, c0 : c0 + width], start=True, stop=True,
-            )
+            interior_banks.append(t)
+            d = bank(f"d{t}_{c0}", (len(interior_banks) - 1) % PACK)[:, 0:width]
+            for x in range(0, width, QUARTER):
+                nc.tensor.matmul_mx(
+                    d[:, x : x + QUARTER], lhsT=wi_codes[:, cols_w].bitcast(FP8X4), lhsT_scale=wi_plane[:, cols_w],
+                    rhs=v2_codes[c0 + x].bitcast(FP8X4),
+                    rhs_scale=v2_plane[:, c0 + x : c0 + x + QUARTER], start=True, stop=True,
+                )
             return d
 
-        def leak_and_gain(t, value, lift, c0, width):
+        values2 = [placed([P, S], F32, f"value2_{t}", AT_VALUE + ROW * t) for t in range(PACK)]
+        lifts = [placed([P, S], F32, f"lift{t}", AT_LIFT + ROW * t) for t in range(PACK)]
+
+        def interior_terms(t, c0, width):
             cols = slice(c0, c0 + width)
-            leaky = placed([P, width], F32, f"leaky{t}_{c0}", AT_SLOT)
-            nc.gpsimd.tensor_tensor(leaky[:], value[:, cols], lift[:, cols], ALU.add)
-            nc.gpsimd.tensor_tensor(value[:, cols], leaky[:], gains2[t][:, cols], ALU.mult)
+            d = interior_product(t, c0, width)
+            nc.scalar.activation(lifts[t][:, cols], d, ACT.Relu, scale=slope_less_one[:, t : t + 1])
+            nc.scalar.copy(values2[t][:, cols], d)
 
-        def interior_slice(t):
-            early = t < 2
-            value = placed([P, S], F32, f"value2_{t}", AT_VALUE + ROW * t)
-            lift = placed([P, S], F32, f"lift{t}", AT_LIFT + ROW * t if t else AT_GAIN + 3 * ROW - half_bytes)
-            pieces = FIRST_PIECES if t == 0 else ((0, HALF), (HALF, HALF))
-            first = 0 if t == 0 else len(FIRST_PIECES) + halves * (t - 1)
-            for number, (c0, width) in enumerate(pieces):
-                cols = slice(c0, c0 + width)
-                d = interior_product(first + number, t, c0, width)
-                nc.scalar.activation(lift[:, cols], d, ACT.Relu, scale=slope_less_one[:, t : t + 1])
-                if width < HALF:
-                    leaky = placed([P, width], F32, f"leaky{t}_{c0}", AT_SLOT + WORD * c0)
-                    nc.vector.tensor_tensor(leaky[:], d, lift[:, cols], ALU.add)
-                    nc.gpsimd.tensor_tensor(value[:, cols], leaky[:], gains2[t][:, cols], ALU.mult)
-                else:
-                    nc.scalar.copy(value[:, cols], d)
-                    if early:
-                        leak_and_gain(t, value, lift, c0, width)
-                if early:
-                    scatter(t, list4, value, c0, width)
-            return value, lift
+        at_slot = AT_EDGE + ROW - KIB
 
-        interior = [interior_slice(0)]
-        gains2.extend(load_gain(wg2, t, f"gain2_{t}") for t in (2, 3))
-        interior.extend(interior_slice(t) for t in (1, 2, 3))
-        leaky2 = placed([P, S], F32, "leaky2", AT_SLOT)
-        nc.gpsimd.tensor_tensor(leaky2[:], interior[2][0][:], interior[2][1][:], ALU.add)
-        at_edge_slot = AT_LIFT + 2 * ROW
-        leaky3 = placed([P, S], F32, "leaky3", at_edge_slot)
-        nc.gpsimd.tensor_tensor(leaky3[:], interior[3][0][:], interior[3][1][:], ALU.add)
+        def interior_piece(t, c0, width, gain):
+            cols = slice(c0, c0 + width)
+            interior_terms(t, c0, width)
+            leaky = placed([P, width], F32, f"leaky{t}_{c0}", at_slot)
+            nc.gpsimd.tensor_tensor(leaky[:], values2[t][:, cols], lifts[t][:, cols], ALU.add)
+            nc.gpsimd.tensor_tensor(values2[t][:, cols], leaky[:], gain, ALU.mult)
+            scatter(t, list4, values2[t][:, cols], c0, width)
 
-        at_planes = AT_VALUE + ROW + 2 * H
+        def interior_sum(t):
+            for h in range(2):
+                interior_terms(t, h * HALF, HALF)
+            leaky = placed([P, S], F32, f"leaky{t}", AT_EDGE if t == 2 else AT_GROUPED + ROW)
+            nc.gpsimd.tensor_tensor(leaky[:], values2[t][:], lifts[t][:], ALU.add)
+            return leaky
+
+        gather_v2(0, QUARTER)
+        gather_v2(QUARTER, QUARTER)
+        gather_v2(HALF, HALF)
+        first_sums = []
+        for c0 in (0, QUARTER):
+            d = interior_product(0, c0, QUARTER)
+            lift = lifts[0][:, c0 : c0 + QUARTER]
+            nc.scalar.activation(lift, d, ACT.Relu, scale=slope_less_one[:, 0:1])
+            leaky = placed([P, QUARTER], F32, f"first_leaky{c0}", at_slot + WORD * c0)
+            nc.vector.tensor_tensor(leaky[:], d, lift, ALU.add)
+            first_sums.append(leaky)
+        for c0, leaky in zip((0, QUARTER), first_sums):
+            cols = slice(c0, c0 + QUARTER)
+            nc.gpsimd.tensor_tensor(values2[0][:, cols], leaky[:], first_gains[0][:, cols], ALU.mult)
+            scatter(0, list4, values2[0][:, cols], c0, QUARTER)
+        interior_piece(1, 0, HALF, first_gains[1][:, 0:HALF])
+        interior_piece(0, HALF, HALF, first_gains[0][:, HALF:S])
+        gain2 = [load_gain(wg2, 2, h * HALF, HALF, f"gain2_2{h}", AT_TAB2 + half_bytes * h) for h in range(2)]
+        gain3 = load_gain(wg2, 3, 0, S, "gain2_3", AT_TAB2 + ROW)
+
+        grouped = [placed([P, 2, PACK * H], BF16, f"grouped{w}", AT_GROUPED + pass_bytes * w) for w in range(2)]
+
+        def round_wf(a):
+            rounded = grouped[0][:, a, :].rearrange("p (t u e i) -> p t u i e", t=PACK, e=PAIR, i=PACK)
+            loaded = wf_raw[a][:].rearrange("p i (u t e) -> p t u i e", t=PACK, e=PAIR)
+            for t in range(PACK):
+                nc.scalar.activation(rounded[:, t], loaded[:, t], ACT.Copy, scale=-1.0)
+
+        def round_wm(a):
+            nc.scalar.copy(
+                grouped[1][:, a, :].rearrange("p (t u e i) -> p u t i e", t=PACK, e=PAIR, i=PACK),
+                wm_raw[a][:].rearrange("p i (u t e) -> p u t i e", t=PACK, e=PAIR),
+            )
+
+        w_codes = [placed([P, 2 * H], U32, f"w_codes{w}", AT_CODES + ROW * w) for w in range(2)]
+
+        def quantise_weight(w):
+            plane = placed([P, 2 * H], U8, f"w_plane{w}", AT_VALUE + ROW + half_bytes + 2 * H * w)
+            nc.vector.quantize_mx(
+                w_codes[w][:].bitcast(FP8X4), plane[:], grouped[w][:].rearrange("p a x -> p (a x)")
+            )
+            return plane
+
+        def gather_v(a):
+            tiles = []
+            for h in range(2):
+                tile = placed([P, HALF], U32, f"v_codes{a}{h}", AT_GROUPED + pass_bytes * a + half_bytes * h)
+                nc.vector.tensor_copy(tile[:], tab_windows[a][:].indirect(entries(list1, h * HALF, HALF)))
+                tiles.append(tile)
+            return tiles
+
+        round_wf(0)
+        interior_piece(1, HALF, HALF, first_gains[1][:, HALF:S])
+        round_wf(1)
+        w_planes = [quantise_weight(0)]
+        leaky2 = interior_sum(2)
+        v_codes = [gather_v(0)]
+        round_wm(0)
+        leaky3 = interior_sum(3)
+        round_wm(1)
+        w_planes.append(quantise_weight(1))
+        v_codes.append(gather_v(1))
+
         wb_codes = keep.tile([P, 2, 2 * H], U8, name="wb_codes", align_bytes=64)
         nc.scalar.copy(
             wb_codes[:].bitcast(U32).rearrange("p a (t u) -> p a u t", t=PACK),
@@ -277,173 +337,128 @@ def tile_list_matting_patch_weave_kernel(
             wb_plane[:].bitcast(U16).rearrange("p (a t u) -> p a t u", a=2, t=PACK),
             wb_plane_raw[:].bitcast(U16).rearrange("p (a u t) -> p a t u", a=2, t=PACK),
         )
-        grouped = [
-            placed([P, 2, PACK * H], BF16, f"grouped{w}", AT_GROUPED + pass_bytes * (1 - w)) for w in range(2)
-        ]
-        for a in range(2):
-            rounded = grouped[0][:, a, :].rearrange("p (t u e i) -> p t u i e", t=PACK, e=PAIR, i=PACK)
-            loaded = wf_raw[a][:].rearrange("p i (u t e) -> p t u i e", t=PACK, e=PAIR)
-            for t in range(PACK):
-                nc.scalar.activation(rounded[:, t], loaded[:, t], ACT.Copy, scale=-1.0)
-        for a in range(2):
-            nc.scalar.copy(
-                grouped[1][:, a, :].rearrange("p (t u e i) -> p u t i e", t=PACK, e=PAIR, i=PACK),
-                wm_raw[a][:].rearrange("p i (u t e) -> p u t i e", t=PACK, e=PAIR),
-            )
-        w_codes = [placed([P, 2 * H], U32, f"w_codes{w}", AT_CODES + half_bytes * (3 + 2 * w)) for w in range(2)]
-        w_plane = [placed([P, 2 * H], U8, f"w_plane{w}", at_planes + 2 * H * w) for w in range(2)]
-        v_places = ((2, 7), (1, 0))
 
-        def quantise_weight(w):
-            nc.vector.quantize_mx(
-                w_codes[w][:].bitcast(FP8X4), w_plane[w][:], grouped[w][:].rearrange("p a x -> p (a x)")
-            )
+        gained2 = placed([P, S], F32, "gained2", AT_GROUPED + pass_bytes + ROW)
+        for h in range(2):
+            cols = slice(h * HALF, (h + 1) * HALF)
+            nc.gpsimd.tensor_tensor(gained2[:, cols], leaky2[:, cols], gain2[h][:], ALU.mult)
+            scatter(2, list4, gained2[:, cols], h * HALF, HALF)
+        pages.append(placed([P, T2], F32, "page3", AT_TAB + 2 * WORD * T - WORD * T2))
+        gained3 = placed([P, S], F32, "gained3", AT_TAB2)
+        nc.gpsimd.tensor_tensor(gained3[:], leaky3[:], gain3[:], ALU.mult)
+        scatter(3, list4, gained3[:], 0, S)
 
-        quantise_weight(0)
-        gained2 = placed([P, S], F32, "gained2", AT_GROUPED + pass_bytes)
-        nc.gpsimd.tensor_tensor(gained2[:], leaky2[:], gains2[2][:], ALU.mult)
-        gained3 = placed([P, S], F32, "gained3", AT_SLOT)
-        nc.gpsimd.tensor_tensor(gained3[:], leaky3[:], gains2[3][:], ALU.mult)
-        v_codes = [
-            [placed([P, HALF], U32, f"v_codes{h}{a}", AT_CODES + half_bytes * v_places[h][a]) for a in range(2)]
-            for h in range(halves)
-        ]
-        for h in range(halves):
-            for a in range(2):
-                nc.vector.tensor_copy(v_codes[h][a][:], tab_window[:, a, :].indirect(entries(list1, h * HALF, HALF)))
-        quantise_weight(1)
-        scatter(2, list4, gained2, 0, S)
-        scatter(3, list4, gained3, 0, S)
-
-        gains1 = [load_gain(wg1, t, f"gain1_{t}") for t in (0, 1)]
-        wo_raw = placed([P, PACK, N], F32, "wo_raw", AT_VALUE + 2 * ROW)
+        gains1 = [load_gain(wg1, t, 0, S, f"gain1_{t}", AT_GAIN + ROW * t) for t in range(2)]
+        wo_raw = placed([P, PACK, N], F32, "wo_raw", AT_LIFT + 2 * KIB)
         for t in range(PACK):
             nc.sync.dma_start(wo_raw[:, PLACE[t], :], wo.rearrange("(u t e) n -> t u e n", t=PACK, e=PAIR)[t])
-        gains1.extend(load_gain(wg1, t, f"gain1_{t}") for t in (2, 3))
+        gains1.extend(load_gain(wg1, t, 0, S, f"gain1_{t}", AT_LIFT + ROW * t) for t in (2, 3))
 
-        def passes(acc, t, h, weights):
-            steps = [(weight, a) for weight in weights for a in range(2)]
+        turns = []
+
+        def next_bank(name):
+            turns.append(name)
+            return bank(name, (len(turns) - 1) % BANKS)
+
+        def product(name, t, h, weights):
+            acc = next_bank(name)
+            steps = [(weight, a) for a in range(2) for weight in weights]
             for number, (weight, a) in enumerate(steps):
                 cols_a = slice(a * H + t * P, a * H + (t + 1) * P)
                 if weight == "b":
                     codes, plane = wb_codes[:, a, 2 * t * P : 2 * (t + 1) * P].bitcast(FP4X4), wb_plane[:, cols_a]
                 else:
                     w = ("f", "m").index(weight)
-                    codes, plane = w_codes[w][:, cols_a].bitcast(FP8X4), w_plane[w][:, cols_a]
+                    codes, plane = w_codes[w][:, cols_a].bitcast(FP8X4), w_planes[w][:, cols_a]
                 nc.tensor.matmul_mx(
-                    acc[:], lhsT=codes, lhsT_scale=plane, rhs=v_codes[h][a][:].bitcast(FP8X4),
+                    acc[:], lhsT=codes, lhsT_scale=plane, rhs=v_codes[a][h][:].bitcast(FP8X4),
                     rhs_scale=v_planes[:, a * S + h * HALF : a * S + (h + 1) * HALF],
                     start=(number == 0), stop=(number == len(steps) - 1),
                 )
-
-        def blend(t, value, matte, back, c0, width):
-            cols = slice(c0, c0 + width)
-            work = placed([P, width], F32, f"blend{t}_{c0}", at_edge_slot + WORD * c0)
-            if t < PACK - 1:
-                nc.gpsimd.tensor_tensor(work[:], value[:, cols], matte[:, cols], ALU.mult)
-                nc.gpsimd.tensor_tensor(work[:], back[:, cols], work[:], ALU.subtract)
-                nc.gpsimd.tensor_tensor(value[:, cols], work[:], gains1[t][:, cols], ALU.mult)
-            else:
-                nc.gpsimd.tensor_tensor(work[:], value[:, cols], back[:, cols], ALU.add)
-                nc.gpsimd.tensor_tensor(work[:], work[:], matte[:, cols], ALU.mult)
-                nc.gpsimd.tensor_tensor(value[:, cols], back[:, cols], work[:], ALU.subtract)
+            return acc
 
         def add_by_turning(value, back, unit):
             blocks = [slice(c * P, (c + 1) * P) for c in range(PACK)]
-            summed = bank(f"summed{unit}", unit)
+            summed = next_bank(f"summed{unit}")
             for block in blocks:
                 for number, term in enumerate((value, back)):
                     nc.tensor.matmul(
                         summed[:, block], lhsT=term[:, block], rhs=identity[:], is_transpose=True,
                         start=(number == 0), stop=(number == 1),
                     )
-            turned_sum = placed([P, HALF], F32, f"turned_sum{unit}", AT_VALUE + half_bytes * (unit % halves))
+            turned_sum = placed([P, HALF], F32, f"turned_sum{unit}", AT_VALUE + half_bytes * (unit % 2))
             nc.scalar.copy(turned_sum[:], summed[:])
-            upright = bank(f"upright{unit}", unit)
+            upright = next_bank(f"upright{unit}")
             for block in blocks:
                 nc.tensor.transpose(upright[:, block], turned_sum[:, block], identity[:])
             nc.scalar.copy(value, upright[:])
 
-        turns = []
-
-        def next_bank(name):
-            turns.append(name)
-            return bank(name, (len(turns) - 1) % TURN_BANKS)
+        def blend(t, values1, mattes, backs, c0, width):
+            cols = slice(c0, c0 + width)
+            value, back, matte = values1[:, cols], backs[:, cols], mattes[:, cols]
+            work = placed([P, width], F32, f"work{t}_{c0}", AT_TAB2 + ROW + WORD * c0)
+            if t < PACK - 1:
+                nc.gpsimd.tensor_tensor(work[:], value, matte, ALU.mult)
+                nc.gpsimd.tensor_tensor(work[:], back, work[:], ALU.subtract)
+                nc.gpsimd.tensor_tensor(value, work[:], gains1[t][:, cols], ALU.mult)
+            else:
+                nc.gpsimd.tensor_tensor(work[:], value, back, ALU.add)
+                nc.gpsimd.tensor_tensor(work[:], work[:], matte, ALU.mult)
+                nc.gpsimd.tensor_tensor(value, back, work[:], ALU.subtract)
 
         for t in range(PACK):
-            region = AT_RAW + pass_bytes * (3 - t) if t < 2 else after_wb_codes + 2 * ROW * (t - 2)
-            value = placed([P, S], F32, f"value1_{t}", region)
-            back = placed([P, S], F32, f"back{t}", region + ROW)
-            matte = placed([P, S], F32, f"matte{t}", AT_RAW + ROW * t)
-            for h in range(halves):
-                unit = halves * t + h
+            region = AT_RAW + 2 * ROW * t if t < 2 else AT_EDGE + 2 * ROW * (t - 2)
+            values1 = placed([P, S], F32, f"value1_{t}", region)
+            backs = placed([P, S], F32, f"back{t}", region + ROW)
+            mattes = placed([P, S], F32, f"matte{t}", AT_RAW + 2 * pass_bytes + ROW * t)
+            for h in range(2):
+                unit = 2 * t + h
                 cols = slice(h * HALF, (h + 1) * HALF)
-                if 1 <= unit <= BANKS - TURN_BANKS:
-                    mt = bank(f"mt{unit}", TURN_BANKS + unit - 1)
-                if unit < SUMMED_UNITS:
-                    diff = next_bank(f"diff{unit}")
-                    if unit == 0:
-                        mt = next_bank(f"mt{unit}")
-                    bg = next_bank(f"bg{unit}")
-                    passes(diff, t, h, "bf")
-                    nc.scalar.copy(value[:, cols], diff[:])
-                    passes(mt, t, h, "m")
-                    nc.scalar.activation(matte[:, cols], mt[:], ACT.Sigmoid)
-                    passes(bg, t, h, "b")
-                    nc.scalar.copy(back[:, cols], bg[:])
+                value, back, matte = values1[:, cols], backs[:, cols], mattes[:, cols]
+                nc.scalar.activation(matte, product(f"mt{unit}", t, h, "m")[:], ACT.Sigmoid)
+                if unit == 3:
+                    nc.scalar.copy(back, product(f"bg{unit}", t, h, "b")[:])
+                    nc.vector.tensor_tensor(value, product(f"diff{unit}", t, h, "f")[:], back, ALU.add)
                 else:
-                    bg = next_bank(f"bg{unit}")
-                    if unit > BANKS - TURN_BANKS:
-                        mt = next_bank(f"mt{unit}")
-                    less_fg = bank(f"diff{unit}", unit)
-                    passes(bg, t, h, "b")
-                    nc.scalar.copy(back[:, cols], bg[:])
-                    passes(mt, t, h, "m")
-                    nc.scalar.activation(matte[:, cols], mt[:], ACT.Sigmoid)
-                    passes(less_fg, t, h, "f")
-                    if t == 1:
-                        nc.vector.tensor_tensor(value[:, cols], less_fg[:], back[:, cols], ALU.add)
-                    else:
-                        nc.scalar.copy(value[:, cols], less_fg[:])
-                    if t == 2:
-                        add_by_turning(value[:, cols], back[:, cols], unit)
-                if t < 2:
-                    blend(t, value, matte, back, h * HALF, HALF)
-            if t >= 2:
-                blend(t, value, matte, back, 0, S)
+                    nc.scalar.copy(value, product(f"diff{unit}", t, h, "fb" if unit in SUMMED_UNITS else "f")[:])
+                    nc.scalar.copy(back, product(f"bg{unit}", t, h, "b")[:])
+                if unit in TURNED_UNITS:
+                    add_by_turning(value, back, unit)
+                if t == 0:
+                    blend(t, values1, mattes, backs, h * HALF, HALF)
+            if t > 0:
+                blend(t, values1, mattes, backs, 0, S)
             if t < PACK - 1:
-                scatter(t, list3, value, 0, S)
+                scatter(t, list3, values1[:], 0, S)
             else:
-                nc.vector.tensor_tensor(pages[t][:].indirect(list3[:]), value[:], gains1[t][:], ALU.mult)
+                nc.vector.tensor_tensor(pages[t][:].indirect(list3[:]), values1[:], gains1[t][:], ALU.mult)
 
-        wo_grouped = placed([P, PACK * N], BF16, "wo_grouped", at_planes)
+        woven = placed([P, T2, PACK], BF16, "woven", AT_GROUPED + pass_bytes)
+        nc.scalar.copy(woven[:, :, PLACE[0]], pages[0][:])
+        wo_grouped = placed([P, PACK * N], BF16, "wo_grouped", AT_PAGE0)
         nc.scalar.copy(
             wo_grouped[:].rearrange("p (c n i) -> p c i n", n=4, i=PACK),
             wo_raw[:].rearrange("p i (c n) -> p c i n", n=4),
         )
-        wo_codes = keep.tile([P, N], U32, name="wo_codes", align_bytes=64)
-        wo_plane = placed([P, N], U8, "wo_plane", after_wb_codes + 2 * ROW)
-
-        starts = [sum(CHUNKS[:i]) for i in range(len(CHUNKS))]
-        woven = placed([P, T2, PACK], BF16, "woven", AT_CODES)
-        nc.scalar.copy(woven[:, :, 0:2], pages[0][:].unsqueeze(2).to_broadcast([P, T2, 2]))
         nc.scalar.copy(woven[:, :, PLACE[1]], pages[1][:])
-        for i, width in enumerate(CHUNKS):
-            cols = slice(starts[i], starts[i] + width)
+        for i, width in enumerate(WEAVE_CHUNKS):
+            cols = slice(sum(WEAVE_CHUNKS[:i]), sum(WEAVE_CHUNKS[: i + 1]))
             nc.scalar.copy(woven[:, cols, PLACE[2]], pages[2][:, cols])
+        wo_codes = keep.tile([P, N], U32, name="wo_codes", align_bytes=64)
+        wo_plane = placed([P, N], U8, "wo_plane", AT_EDGE + 2 * ROW)
+
+        def quantise_wo(n0, n1):
+            nc.vector.quantize_mx(
+                wo_codes[:, n0:n1].bitcast(FP8X4), wo_plane[:, n0:n1], wo_grouped[:, PACK * n0 : PACK * n1]
+            )
+
         out_rows = out.rearrange("(n p) c -> p n c", p=P)
-        pieces = [
-            (i, c0, min(width, PIECE)) for i, width in enumerate(CHUNKS) for c0 in range(0, width, PIECE)
-        ]
-        turns.clear()
-        for k, (i, c0, width) in enumerate(pieces):
-            cols = slice(starts[i] + c0, starts[i] + c0 + width)
+        quantise_wo(0, P)
+        for k, width in enumerate(PIECES):
+            cols = slice(sum(PIECES[:k]), sum(PIECES[: k + 1]))
             nc.vector.tensor_copy(woven[:, cols, PLACE[3]], pages[3][:, cols])
             if k == 0:
-                for n0, n1 in ((0, 2 * P), (2 * P, N)):
-                    nc.vector.quantize_mx(
-                        wo_codes[:, n0:n1].bitcast(FP8X4), wo_plane[:, n0:n1], wo_grouped[:, PACK * n0 : PACK * n1]
-                    )
+                quantise_wo(P, N)
             codes = keep.tile([P, width], U32, name=f"page_codes{k}", align_bytes=64)
             plane = keep.tile([P, width], U8, name=f"page_plane{k}", align_bytes=64)
             nc.vector.quantize_mx(
@@ -452,8 +467,7 @@ def tile_list_matting_patch_weave_kernel(
             result = placed([P, N // P, width], F32, f"result{k}", AT_TAB + WORD * (N // P) * cols.start)
             for n0 in range(0, N // P, HALF // width):
                 n1 = min(N // P, n0 + HALF // width)
-                turns.append(k)
-                acc = bank(f"acc{k}{n0}", (len(turns) - 1) % BANKS)
+                acc = next_bank(f"acc{k}{n0}")
                 for n in range(n0, n1):
                     rows = slice(n * P, (n + 1) * P)
                     nc.tensor.matmul_mx(
@@ -462,7 +476,7 @@ def tile_list_matting_patch_weave_kernel(
                         rhs=codes[:].bitcast(FP8X4), rhs_scale=plane[:], start=True, stop=True,
                     )
                 emptied = result[:, n0:n1, :].rearrange("p n c -> p (n c)")
-                if n0 == 0 and k >= len(pieces) - 2:
+                if n0 == 0 and k >= len(PIECES) - 2:
                     nc.vector.tensor_copy(emptied, acc[:, 0 : (n1 - n0) * width])
                 else:
                     nc.scalar.copy(emptied, acc[:, 0 : (n1 - n0) * width])

@@ -31,8 +31,6 @@ WORD = 4
 KIB = 1024
 ROW = WORD * S
 
-SUMMED_UNITS = (0, 1, 2)
-TURNED_UNITS = (4, 5)
 PIECES = (128, 128, 256, 256, 256, 256, 256, 256, 256)
 WEAVE_CHUNKS = (256, 256, 512, 512, 512)
 PLACE = (0, 2, 3, 1)
@@ -179,8 +177,8 @@ def tile_list_matting_patch_weave_kernel(
             nc.tensor.transpose(turned[:, c * P : (c + 1) * P], first_rows[:, c * P : (c + 1) * P], identity[:])
         first_gains = [placed([P, S], F32, f"gain2_{t}", AT_GAIN + ROW * t) for t in range(2)]
         at_gain2a = AT_GAIN + 2 * ROW
-        at_wb_raw = at_gain2a + half_bytes
-        at_repeated = (AT_TAB, at_wb_raw + KIB, AT_TAB + WORD * T, at_gain2a)
+        at_wb_raw = at_gain2a + ROW
+        at_repeated = (at_wb_raw + KIB, AT_TAB, at_gain2a + KIB, AT_TAB + WORD * T)
         for k in range(PACK):
             repeated = placed([P, PACK, P], F32, f"repeated{k}", at_repeated[k])
             nc.scalar.copy(
@@ -195,7 +193,6 @@ def tile_list_matting_patch_weave_kernel(
 
         slope_less_one = keep.tile([P, PACK], F32, name="slope_less_one")
         nc.scalar.activation(slope_less_one[:], slopes[:, 0 : PAIR * PACK - 1 : PAIR], ACT.Identity, bias=-1.0)
-        tab_windows = [load_words(tab_words[0], "tab_window0", AT_TAB)]
         wb_raw = placed([P, 2, 2 * H], U8, "wb_raw", at_wb_raw)
         nc.sync.dma_start(wb_raw[:].bitcast(I32), wb_words.bitcast(I32).rearrange("a p c -> p a c"))
         wb_plane_raw = placed([P, 2 * H], U8, "wb_plane_raw", at_wb_raw + half_bytes)
@@ -205,12 +202,13 @@ def tile_list_matting_patch_weave_kernel(
                 wb_plane_raw[QUAD * q : QUAD * q + LIVE, :].bitcast(I32).rearrange("p (a c) -> p a c", a=2),
                 wb_scales[:, LIVE * q : LIVE * (q + 1), :].bitcast(I32).rearrange("a r c -> r a c"),
             )
+        tab_windows = [load_words(tab_words[0], "tab_window0", AT_TAB)]
+        gain2 = [load_gain(wg2, 2, h * HALF, HALF, f"gain2_2{h}", at_gain2a + half_bytes * h) for h in range(2)]
         tab_windows.append(load_words(tab_words[1], "tab_window1", AT_TAB + WORD * T))
 
         pages = [
             placed([P, T2], F32, "page0", AT_PAGE0),
             keep.tile([P, T2], F32, name="page1"),
-            keep.tile([P, T2], F32, name="page2"),
         ]
 
         def scatter(t, lst, value, c0, width):
@@ -257,11 +255,12 @@ def tile_list_matting_patch_weave_kernel(
             nc.gpsimd.tensor_tensor(values2[t][:, cols], leaky[:], gain, ALU.mult)
             scatter(t, list4, values2[t][:, cols], c0, width)
 
-        def interior_sum(t):
-            for h in range(2):
-                interior_terms(t, h * HALF, HALF)
-            leaky = placed([P, S], F32, f"leaky{t}", AT_EDGE if t == 2 else AT_GROUPED + ROW)
-            nc.gpsimd.tensor_tensor(leaky[:], values2[t][:], lifts[t][:], ALU.add)
+        def interior_sum(t, c0, width, offset):
+            cols = slice(c0, c0 + width)
+            for x in range(c0, c0 + width, HALF):
+                interior_terms(t, x, HALF)
+            leaky = placed([P, width], F32, f"leaky{t}_{c0}", offset)
+            nc.gpsimd.tensor_tensor(leaky[:], values2[t][:, cols], lifts[t][:, cols], ALU.add)
             return leaky
 
         gather_v2(0, QUARTER)
@@ -281,8 +280,7 @@ def tile_list_matting_patch_weave_kernel(
             scatter(0, list4, values2[0][:, cols], c0, QUARTER)
         interior_piece(1, 0, HALF, first_gains[1][:, 0:HALF])
         interior_piece(0, HALF, HALF, first_gains[0][:, HALF:S])
-        gain2 = [load_gain(wg2, 2, h * HALF, HALF, f"gain2_2{h}", AT_TAB2 + half_bytes * h) for h in range(2)]
-        gain3 = load_gain(wg2, 3, 0, S, "gain2_3", AT_TAB2 + ROW)
+        gain3 = load_gain(wg2, 3, 0, S, "gain2_3", AT_TAB2)
 
         grouped = [placed([P, 2, PACK * H], BF16, f"grouped{w}", AT_GROUPED + pass_bytes * w) for w in range(2)]
 
@@ -319,14 +317,6 @@ def tile_list_matting_patch_weave_kernel(
         interior_piece(1, HALF, HALF, first_gains[1][:, HALF:S])
         round_wf(1)
         w_planes = [quantise_weight(0)]
-        leaky2 = interior_sum(2)
-        v_codes = [gather_v(0)]
-        round_wm(0)
-        leaky3 = interior_sum(3)
-        round_wm(1)
-        w_planes.append(quantise_weight(1))
-        v_codes.append(gather_v(1))
-
         wb_codes = keep.tile([P, 2, 2 * H], U8, name="wb_codes", align_bytes=64)
         nc.scalar.copy(
             wb_codes[:].bitcast(U32).rearrange("p a (t u) -> p a u t", t=PACK),
@@ -338,14 +328,32 @@ def tile_list_matting_patch_weave_kernel(
             wb_plane_raw[:].bitcast(U16).rearrange("p (a u t) -> p a t u", a=2, t=PACK),
         )
 
-        gained2 = placed([P, S], F32, "gained2", AT_GROUPED + pass_bytes + ROW)
+        leaky2 = interior_sum(2, 0, S, AT_EDGE)
+        leaky3 = [interior_sum(3, 0, HALF, AT_EDGE + ROW)]
+        gained2 = [placed([P, HALF], F32, "gained2_0", AT_GROUPED + ROW)]
+        nc.gpsimd.tensor_tensor(gained2[0][:], leaky2[:, 0:HALF], gain2[0][:], ALU.mult)
+        v_codes = [gather_v(0)]
+        round_wm(0)
+        round_wm(1)
+        w_planes.append(quantise_weight(1))
+        v_codes.append(gather_v(1))
+
+        gained2.append(placed([P, HALF], F32, "gained2_1", AT_GROUPED + pass_bytes + ROW))
+        nc.gpsimd.tensor_tensor(gained2[1][:], leaky2[:, HALF:S], gain2[1][:], ALU.mult)
+        pages.extend(placed([P, T2], F32, f"page{t}", AT_TAB + WORD * (T + T2 * (t - 2))) for t in (2, 3))
+        for h in range(2):
+            scatter(2, list4, gained2[h][:], h * HALF, HALF)
+        last_d = interior_product(3, HALF, HALF)
+        last_lift = placed([P, HALF], F32, "last_lift", AT_RAW + 3 * pass_bytes)
+        nc.scalar.activation(last_lift[:], last_d, ACT.Relu, scale=slope_less_one[:, 3:4])
+        last_value = placed([P, HALF], F32, "last_value", AT_RAW + 3 * pass_bytes + half_bytes)
+        nc.scalar.copy(last_value[:], last_d)
+        leaky3.append(placed([P, HALF], F32, "last_leaky", AT_GROUPED + ROW + half_bytes))
+        nc.gpsimd.tensor_tensor(leaky3[1][:], last_value[:], last_lift[:], ALU.add)
+        gained3 = placed([P, S], F32, "gained3", at_gain2a)
         for h in range(2):
             cols = slice(h * HALF, (h + 1) * HALF)
-            nc.gpsimd.tensor_tensor(gained2[:, cols], leaky2[:, cols], gain2[h][:], ALU.mult)
-            scatter(2, list4, gained2[:, cols], h * HALF, HALF)
-        pages.append(placed([P, T2], F32, "page3", AT_TAB + 2 * WORD * T - WORD * T2))
-        gained3 = placed([P, S], F32, "gained3", AT_TAB2)
-        nc.gpsimd.tensor_tensor(gained3[:], leaky3[:], gain3[:], ALU.mult)
+            nc.gpsimd.tensor_tensor(gained3[:, cols], leaky3[h][:], gain3[:, cols], ALU.mult)
         scatter(3, list4, gained3[:], 0, S)
 
         gains1 = [load_gain(wg1, t, 0, S, f"gain1_{t}", AT_GAIN + ROW * t) for t in range(2)]
@@ -377,8 +385,10 @@ def tile_list_matting_patch_weave_kernel(
                 )
             return acc
 
-        def add_by_turning(value, back, unit):
-            blocks = [slice(c * P, (c + 1) * P) for c in range(PACK)]
+        blocks = [slice(c * P, (c + 1) * P) for c in range(PACK)]
+
+        def turn_sum(unit):
+            value, back, matte = unit_tiles(unit)
             summed = next_bank(f"summed{unit}")
             for block in blocks:
                 for number, term in enumerate((value, back)):
@@ -388,15 +398,18 @@ def tile_list_matting_patch_weave_kernel(
                     )
             turned_sum = placed([P, HALF], F32, f"turned_sum{unit}", AT_VALUE + half_bytes * (unit % 2))
             nc.scalar.copy(turned_sum[:], summed[:])
+            return turned_sum
+
+        def turn_back(unit, turned_sum):
             upright = next_bank(f"upright{unit}")
             for block in blocks:
                 nc.tensor.transpose(upright[:, block], turned_sum[:, block], identity[:])
-            nc.scalar.copy(value, upright[:])
+            nc.scalar.copy(unit_tiles(unit)[0], upright[:])
 
         def blend(t, values1, mattes, backs, c0, width):
             cols = slice(c0, c0 + width)
             value, back, matte = values1[:, cols], backs[:, cols], mattes[:, cols]
-            work = placed([P, width], F32, f"work{t}_{c0}", AT_TAB2 + ROW + WORD * c0)
+            work = placed([P, width], F32, f"work{t}_{c0}", AT_TAB2 + WORD * c0)
             if t < PACK - 1:
                 nc.gpsimd.tensor_tensor(work[:], value, matte, ALU.mult)
                 nc.gpsimd.tensor_tensor(work[:], back, work[:], ALU.subtract)
@@ -406,26 +419,29 @@ def tile_list_matting_patch_weave_kernel(
                 nc.gpsimd.tensor_tensor(work[:], work[:], matte, ALU.mult)
                 nc.gpsimd.tensor_tensor(value, back, work[:], ALU.subtract)
 
+        slices = []
         for t in range(PACK):
             region = AT_RAW + 2 * ROW * t if t < 2 else AT_EDGE + 2 * ROW * (t - 2)
-            values1 = placed([P, S], F32, f"value1_{t}", region)
-            backs = placed([P, S], F32, f"back{t}", region + ROW)
-            mattes = placed([P, S], F32, f"matte{t}", AT_RAW + 2 * pass_bytes + ROW * t)
-            for h in range(2):
-                unit = 2 * t + h
-                cols = slice(h * HALF, (h + 1) * HALF)
-                value, back, matte = values1[:, cols], backs[:, cols], mattes[:, cols]
-                nc.scalar.activation(matte, product(f"mt{unit}", t, h, "m")[:], ACT.Sigmoid)
-                if unit == 3:
-                    nc.scalar.copy(back, product(f"bg{unit}", t, h, "b")[:])
-                    nc.vector.tensor_tensor(value, product(f"diff{unit}", t, h, "f")[:], back, ALU.add)
-                else:
-                    nc.scalar.copy(value, product(f"diff{unit}", t, h, "fb" if unit in SUMMED_UNITS else "f")[:])
-                    nc.scalar.copy(back, product(f"bg{unit}", t, h, "b")[:])
-                if unit in TURNED_UNITS:
-                    add_by_turning(value, back, unit)
-                if t == 0:
-                    blend(t, values1, mattes, backs, h * HALF, HALF)
+            slices.append((
+                placed([P, S], F32, f"value1_{t}", region),
+                placed([P, S], F32, f"back{t}", region + ROW),
+                placed([P, S], F32, f"matte{t}", AT_RAW + 2 * pass_bytes + ROW * t),
+            ))
+
+        def unit_tiles(unit):
+            return [tile[:, (unit % 2) * HALF : (unit % 2 + 1) * HALF] for tile in slices[unit // 2]]
+
+        def matte_of(unit):
+            mt = product(f"mt{unit}", unit // 2, unit % 2, "m")
+            nc.scalar.activation(unit_tiles(unit)[2], mt[:], ACT.Sigmoid)
+
+        def terms_of(unit, first):
+            value, back, matte = unit_tiles(unit)
+            nc.scalar.copy(value, product(f"diff{unit}", unit // 2, unit % 2, first)[:])
+            nc.scalar.copy(back, product(f"bg{unit}", unit // 2, unit % 2, "b")[:])
+
+        def finish(t):
+            values1, backs, mattes = slices[t]
             if t > 0:
                 blend(t, values1, mattes, backs, 0, S)
             if t < PACK - 1:
@@ -433,13 +449,47 @@ def tile_list_matting_patch_weave_kernel(
             else:
                 nc.vector.tensor_tensor(pages[t][:].indirect(list3[:]), values1[:], gains1[t][:], ALU.mult)
 
+        for unit in (0, 1):
+            matte_of(unit)
+            terms_of(unit, "fb")
+            blend(0, slices[0][0], slices[0][2], slices[0][1], unit * HALF, HALF)
+        finish(0)
+        terms_of(2, "f")
+        matte_of(3)
+        terms_of(3, "fb")
+        turned2 = turn_sum(2)
+        matte_of(2)
+        turn_back(2, turned2)
+        finish(1)
+        terms_of(4, "f")
+        terms_of(5, "f")
+        turned4 = turn_sum(4)
+        matte_of(4)
+        turned5 = turn_sum(5)
+        turn_back(4, turned4)
+        matte_of(5)
+        turn_back(5, turned5)
+        finish(2)
+        for unit in (6, 7):
+            for back_step in range(3):
+                turns.pop()
+            matte_of(unit)
+            terms_of(unit, "f")
+        finish(3)
+        values1 = slices[3][0]
+
+        def round_wo(n0, n1, offset):
+            tile = placed([P, PACK * (n1 - n0)], BF16, f"wo_grouped{n0}", offset)
+            nc.scalar.copy(
+                tile[:].rearrange("p (c n i) -> p c i n", n=4, i=PACK),
+                wo_raw[:, :, n0:n1].rearrange("p i (c n) -> p c i n", n=4),
+            )
+            return tile
+
+        wo_grouped = [round_wo(0, 2 * P, AT_GROUPED)]
         woven = placed([P, T2, PACK], BF16, "woven", AT_GROUPED + pass_bytes)
         nc.scalar.copy(woven[:, :, PLACE[0]], pages[0][:])
-        wo_grouped = placed([P, PACK * N], BF16, "wo_grouped", AT_PAGE0)
-        nc.scalar.copy(
-            wo_grouped[:].rearrange("p (c n i) -> p c i n", n=4, i=PACK),
-            wo_raw[:].rearrange("p i (c n) -> p c i n", n=4),
-        )
+        wo_grouped.append(round_wo(2 * P, N, AT_PAGE0))
         nc.scalar.copy(woven[:, :, PLACE[1]], pages[1][:])
         for i, width in enumerate(WEAVE_CHUNKS):
             cols = slice(sum(WEAVE_CHUNKS[:i]), sum(WEAVE_CHUNKS[: i + 1]))
@@ -447,24 +497,22 @@ def tile_list_matting_patch_weave_kernel(
         wo_codes = keep.tile([P, N], U32, name="wo_codes", align_bytes=64)
         wo_plane = placed([P, N], U8, "wo_plane", AT_EDGE + 2 * ROW)
 
-        def quantise_wo(n0, n1):
-            nc.vector.quantize_mx(
-                wo_codes[:, n0:n1].bitcast(FP8X4), wo_plane[:, n0:n1], wo_grouped[:, PACK * n0 : PACK * n1]
-            )
+        def quantise_wo(n0, n1, rounded):
+            nc.vector.quantize_mx(wo_codes[:, n0:n1].bitcast(FP8X4), wo_plane[:, n0:n1], rounded[:])
 
         out_rows = out.rearrange("(n p) c -> p n c", p=P)
-        quantise_wo(0, P)
+        quantise_wo(2 * P, N, wo_grouped[1])
         for k, width in enumerate(PIECES):
             cols = slice(sum(PIECES[:k]), sum(PIECES[: k + 1]))
             nc.vector.tensor_copy(woven[:, cols, PLACE[3]], pages[3][:, cols])
             if k == 0:
-                quantise_wo(P, N)
+                quantise_wo(0, 2 * P, wo_grouped[0])
             codes = keep.tile([P, width], U32, name=f"page_codes{k}", align_bytes=64)
             plane = keep.tile([P, width], U8, name=f"page_plane{k}", align_bytes=64)
             nc.vector.quantize_mx(
                 codes[:].bitcast(FP8X4), plane[:], woven[:, cols, :].rearrange("p c t -> p (c t)")
             )
-            result = placed([P, N // P, width], F32, f"result{k}", AT_TAB + WORD * (N // P) * cols.start)
+            result = placed([P, N // P, width], F32, f"result{k}", AT_TAB2 + 2 * ROW + WORD * (N // P) * cols.start)
             for n0 in range(0, N // P, HALF // width):
                 n1 = min(N // P, n0 + HALF // width)
                 acc = next_bank(f"acc{k}{n0}")

@@ -134,9 +134,9 @@ def tile_list_matting_patch_weave_kernel(
             )
 
         load_slopes(0)
+        list4 = load_list(offs4, "list4")
         tab2_window = load_words(tab2_words[0], "tab2_window", AT_TAB2)
         load_slopes(1)
-        list4 = load_list(offs4, "list4")
         list3 = load_list(offs3, "list3")
 
         v2_rows = placed([P, S], U8, "v2_rows", AT_SMALL + 4 * KIB)
@@ -178,7 +178,7 @@ def tile_list_matting_patch_weave_kernel(
         first_gains = [placed([P, S], F32, f"gain2_{t}", AT_GAIN + ROW * t) for t in range(2)]
         at_gain2a = AT_GAIN + 2 * ROW
         at_wb_raw = at_gain2a + ROW
-        at_repeated = (at_wb_raw + KIB, AT_TAB, at_gain2a + KIB, AT_TAB + WORD * T)
+        at_repeated = (AT_TAB, at_wb_raw + KIB, at_gain2a, AT_TAB + WORD * T)
         for k in range(PACK):
             repeated = placed([P, PACK, P], F32, f"repeated{k}", at_repeated[k])
             nc.scalar.copy(
@@ -193,6 +193,7 @@ def tile_list_matting_patch_weave_kernel(
 
         slope_less_one = keep.tile([P, PACK], F32, name="slope_less_one")
         nc.scalar.activation(slope_less_one[:], slopes[:, 0 : PAIR * PACK - 1 : PAIR], ACT.Identity, bias=-1.0)
+        tab_windows = [load_words(tab_words[0], "tab_window0", AT_TAB)]
         wb_raw = placed([P, 2, 2 * H], U8, "wb_raw", at_wb_raw)
         nc.sync.dma_start(wb_raw[:].bitcast(I32), wb_words.bitcast(I32).rearrange("a p c -> p a c"))
         wb_plane_raw = placed([P, 2 * H], U8, "wb_plane_raw", at_wb_raw + half_bytes)
@@ -202,8 +203,7 @@ def tile_list_matting_patch_weave_kernel(
                 wb_plane_raw[QUAD * q : QUAD * q + LIVE, :].bitcast(I32).rearrange("p (a c) -> p a c", a=2),
                 wb_scales[:, LIVE * q : LIVE * (q + 1), :].bitcast(I32).rearrange("a r c -> r a c"),
             )
-        tab_windows = [load_words(tab_words[0], "tab_window0", AT_TAB)]
-        gain2 = [load_gain(wg2, 2, h * HALF, HALF, f"gain2_2{h}", at_gain2a + half_bytes * h) for h in range(2)]
+        gain2 = [load_gain(wg2, 2, 0, HALF, "gain2_20", at_gain2a)]
         tab_windows.append(load_words(tab_words[1], "tab_window1", AT_TAB + WORD * T))
 
         pages = [
@@ -280,6 +280,7 @@ def tile_list_matting_patch_weave_kernel(
             scatter(0, list4, values2[0][:, cols], c0, QUARTER)
         interior_piece(1, 0, HALF, first_gains[1][:, 0:HALF])
         interior_piece(0, HALF, HALF, first_gains[0][:, HALF:S])
+        gain2.append(load_gain(wg2, 2, HALF, HALF, "gain2_21", AT_TAB2 + ROW))
         gain3 = load_gain(wg2, 3, 0, S, "gain2_3", AT_TAB2)
 
         grouped = [placed([P, 2, PACK * H], BF16, f"grouped{w}", AT_GROUPED + pass_bytes * w) for w in range(2)]
@@ -299,7 +300,7 @@ def tile_list_matting_patch_weave_kernel(
         w_codes = [placed([P, 2 * H], U32, f"w_codes{w}", AT_CODES + ROW * w) for w in range(2)]
 
         def quantise_weight(w):
-            plane = placed([P, 2 * H], U8, f"w_plane{w}", AT_VALUE + ROW + half_bytes + 2 * H * w)
+            plane = placed([P, 2 * H], U8, f"w_plane{w}", (AT_VALUE + ROW + half_bytes, AT_TAB)[w])
             nc.vector.quantize_mx(
                 w_codes[w][:].bitcast(FP8X4), plane[:], grouped[w][:].rearrange("p a x -> p (a x)")
             )
@@ -317,6 +318,16 @@ def tile_list_matting_patch_weave_kernel(
         interior_piece(1, HALF, HALF, first_gains[1][:, HALF:S])
         round_wf(1)
         w_planes = [quantise_weight(0)]
+        leaky2 = interior_sum(2, 0, S, AT_EDGE)
+        leaky3 = [interior_sum(3, 0, HALF, AT_EDGE + ROW)]
+        gained2 = [placed([P, HALF], F32, "gained2_0", AT_GROUPED + ROW)]
+        nc.gpsimd.tensor_tensor(gained2[0][:], leaky2[:, 0:HALF], gain2[0][:], ALU.mult)
+        v_codes = [gather_v(0)]
+        round_wm(0)
+        round_wm(1)
+        w_planes.append(quantise_weight(1))
+        v_codes.append(gather_v(1))
+
         wb_codes = keep.tile([P, 2, 2 * H], U8, name="wb_codes", align_bytes=64)
         nc.scalar.copy(
             wb_codes[:].bitcast(U32).rearrange("p a (t u) -> p a u t", t=PACK),
@@ -327,16 +338,6 @@ def tile_list_matting_patch_weave_kernel(
             wb_plane[:].bitcast(U16).rearrange("p (a t u) -> p a t u", a=2, t=PACK),
             wb_plane_raw[:].bitcast(U16).rearrange("p (a u t) -> p a t u", a=2, t=PACK),
         )
-
-        leaky2 = interior_sum(2, 0, S, AT_EDGE)
-        leaky3 = [interior_sum(3, 0, HALF, AT_EDGE + ROW)]
-        gained2 = [placed([P, HALF], F32, "gained2_0", AT_GROUPED + ROW)]
-        nc.gpsimd.tensor_tensor(gained2[0][:], leaky2[:, 0:HALF], gain2[0][:], ALU.mult)
-        v_codes = [gather_v(0)]
-        round_wm(0)
-        round_wm(1)
-        w_planes.append(quantise_weight(1))
-        v_codes.append(gather_v(1))
 
         gained2.append(placed([P, HALF], F32, "gained2_1", AT_GROUPED + pass_bytes + ROW))
         nc.gpsimd.tensor_tensor(gained2[1][:], leaky2[:, HALF:S], gain2[1][:], ALU.mult)
@@ -350,7 +351,7 @@ def tile_list_matting_patch_weave_kernel(
         nc.scalar.copy(last_value[:], last_d)
         leaky3.append(placed([P, HALF], F32, "last_leaky", AT_GROUPED + ROW + half_bytes))
         nc.gpsimd.tensor_tensor(leaky3[1][:], last_value[:], last_lift[:], ALU.add)
-        gained3 = placed([P, S], F32, "gained3", at_gain2a)
+        gained3 = placed([P, S], F32, "gained3", AT_TAB2 + ROW)
         for h in range(2):
             cols = slice(h * HALF, (h + 1) * HALF)
             nc.gpsimd.tensor_tensor(gained3[:, cols], leaky3[h][:], gain3[:, cols], ALU.mult)

@@ -357,10 +357,11 @@ def tile_list_matting_patch_weave_kernel(
             nc.gpsimd.tensor_tensor(gained3[:, cols], leaky3[h][:], gain3[:, cols], ALU.mult)
         scatter(3, list4, gained3[:], 0, S)
 
-        gains1 = [load_gain(wg1, t, 0, S, f"gain1_{t}", AT_GAIN + ROW * t) for t in range(2)]
+        gains1 = [load_gain(wg1, 0, 0, S, "gain1_0", AT_GAIN)]
         wo_raw = placed([P, PACK, N], F32, "wo_raw", AT_LIFT + 2 * KIB)
         for t in range(PACK):
             nc.sync.dma_start(wo_raw[:, PLACE[t], :], wo.rearrange("(u t e) n -> t u e n", t=PACK, e=PAIR)[t])
+        gains1.append(load_gain(wg1, 1, 0, S, "gain1_1", AT_GAIN + ROW))
         gains1.extend(load_gain(wg1, t, 0, S, f"gain1_{t}", AT_LIFT + ROW * t) for t in (2, 3))
 
         turns = []
@@ -487,7 +488,7 @@ def tile_list_matting_patch_weave_kernel(
             )
             return tile
 
-        wo_grouped = [round_wo(0, 2 * P, AT_GROUPED)]
+        wo_grouped = [round_wo(0, 2 * P, AT_VALUE + 2 * ROW)]
         woven = placed([P, T2, PACK], BF16, "woven", AT_GROUPED + pass_bytes)
         nc.scalar.copy(woven[:, :, PLACE[0]], pages[0][:])
         wo_grouped.append(round_wo(2 * P, N, AT_PAGE0))

@@ -526,7 +526,7 @@ def tile_list_matting_patch_weave_kernel(
                         rhs=codes[:].bitcast(FP8X4), rhs_scale=plane[:], start=True, stop=True,
                     )
                 emptied = result[:, n0:n1, :].rearrange("p n c -> p (n c)")
-                if n0 == 0 and k >= len(PIECES) - 2:
+                if n0 == 0 and k == len(PIECES) - 1:
                     nc.vector.tensor_copy(emptied, acc[:, 0 : (n1 - n0) * width])
                 else:
                     nc.scalar.copy(emptied, acc[:, 0 : (n1 - n0) * width])

@@ -99,7 +99,8 @@ def tile_list_matting_patch_weave_kernel(
         tab2_rows = placed([P, T], U8, "tab2_rows", AT_RAW)
         nc.vector.memset(tab2_rows[0 : P - GROUP, :].bitcast(I32), 0)
         tab_rows = placed([P, T], U8, "tab_rows", AT_RAW + 2 * pass_bytes - T // 2)
-        nc.vector.memset(tab_rows[0 : P - 2 * GROUP, :].bitcast(I32), 0)
+        nc.vector.memset(tab_rows[2 * QUAD : P, :].bitcast(I32), 0)
+        nc.vector.memset(tab_rows[QUAD : 2 * QUAD, :].bitcast(I32), 0)
         wi_plane_raw = placed([P, H], U8, "wi_plane_raw", AT_SMALL + 8 * KIB)
         nc.gpsimd.memset(wi_plane_raw[:].bitcast(I32), 0)
         identity = keep.tile([P, P], F32, name="identity")
@@ -115,7 +116,7 @@ def tile_list_matting_patch_weave_kernel(
         nc.sync.dma_start(tab2_rows[P - GROUP : P, :].bitcast(I32), tab2_scales[0].bitcast(I32))
         list1 = load_list(offs, "list1")
         nc.sync.dma_start(
-            tab_rows[P - 2 * GROUP : P, :].bitcast(I32), tab_scales.bitcast(I32).rearrange("a r t -> r a t")
+            tab_rows[0:QUAD, :].bitcast(I32), tab_scales.bitcast(I32).rearrange("a r t -> r a t")
         )
         first_rows = placed([P, HALF], F32, "first_rows", AT_SMALL + 6 * KIB)
         nc.sync.dma_start(
@@ -153,7 +154,7 @@ def tile_list_matting_patch_weave_kernel(
         for q in range(P // QUAD):
             nc.sync.dma_start(
                 v_planes[QUAD * q : QUAD * q + LIVE, :].bitcast(I32).rearrange("p (a c) -> p a c", a=2),
-                v_rows[P - 2 * GROUP + 2 * LIVE * q : P - 2 * GROUP + 2 * LIVE * (q + 1), :].bitcast(I32),
+                v_rows[2 * LIVE * q : 2 * LIVE * (q + 1), :].bitcast(I32),
             )
 
         wi_codes = keep.tile([P, H], I32, name="wi_codes", align_bytes=64)
@@ -280,7 +281,7 @@ def tile_list_matting_patch_weave_kernel(
             scatter(0, list4, values2[0][:, cols], c0, QUARTER)
         interior_piece(1, 0, HALF, first_gains[1][:, 0:HALF])
         interior_piece(0, HALF, HALF, first_gains[0][:, HALF:S])
-        gain2.append(load_gain(wg2, 2, HALF, HALF, "gain2_21", AT_TAB2 + ROW))
+        gain2.append(load_gain(wg2, 2, HALF, HALF, "gain2_21", AT_TAB2 + 2 * ROW))
         gain3 = load_gain(wg2, 3, 0, S, "gain2_3", AT_TAB2)
 
         grouped = [placed([P, 2, PACK * H], BF16, f"grouped{w}", AT_GROUPED + pass_bytes * w) for w in range(2)]
@@ -300,7 +301,7 @@ def tile_list_matting_patch_weave_kernel(
         w_codes = [placed([P, 2 * H], U32, f"w_codes{w}", AT_CODES + ROW * w) for w in range(2)]
 
         def quantise_weight(w):
-            plane = placed([P, 2 * H], U8, f"w_plane{w}", (AT_VALUE + ROW + half_bytes, AT_TAB)[w])
+            plane = placed([P, 2 * H], U8, f"w_plane{w}", (AT_SMALL + 10 * KIB, at_wb_raw)[w])
             nc.vector.quantize_mx(
                 w_codes[w][:].bitcast(FP8X4), plane[:], grouped[w][:].rearrange("p a x -> p (a x)")
             )
@@ -309,7 +310,7 @@ def tile_list_matting_patch_weave_kernel(
         def gather_v(a):
             tiles = []
             for h in range(2):
-                tile = placed([P, HALF], U32, f"v_codes{a}{h}", AT_GROUPED + pass_bytes * a + half_bytes * h)
+                tile = keep.tile([P, HALF], U32, name=f"v_codes{a}{h}", align_bytes=64)
                 nc.vector.tensor_copy(tile[:], tab_windows[a][:].indirect(entries(list1, h * HALF, HALF)))
                 tiles.append(tile)
             return tiles
@@ -325,14 +326,13 @@ def tile_list_matting_patch_weave_kernel(
         v_codes = [gather_v(0)]
         round_wm(0)
         round_wm(1)
-        w_planes.append(quantise_weight(1))
-        v_codes.append(gather_v(1))
-
         wb_codes = keep.tile([P, 2, 2 * H], U8, name="wb_codes", align_bytes=64)
         nc.scalar.copy(
             wb_codes[:].bitcast(U32).rearrange("p a (t u) -> p a u t", t=PACK),
             wb_raw[:].bitcast(U32).rearrange("p a (u t) -> p a u t", t=PACK),
         )
+        w_planes.append(quantise_weight(1))
+        v_codes.append(gather_v(1))
         wb_plane = keep.tile([P, 2 * H], U8, name="wb_plane", align_bytes=64)
         nc.scalar.copy(
             wb_plane[:].bitcast(U16).rearrange("p (a t u) -> p a t u", a=2, t=PACK),
@@ -341,7 +341,7 @@ def tile_list_matting_patch_weave_kernel(
 
         gained2.append(placed([P, HALF], F32, "gained2_1", AT_GROUPED + pass_bytes + ROW))
         nc.gpsimd.tensor_tensor(gained2[1][:], leaky2[:, HALF:S], gain2[1][:], ALU.mult)
-        pages.extend(placed([P, T2], F32, f"page{t}", AT_TAB + WORD * (T + T2 * (t - 2))) for t in (2, 3))
+        pages.extend(placed([P, T2], F32, f"page{t}", AT_TAB2 + 2 * ROW + WORD * T2 * (t - 2)) for t in (2, 3))
         for h in range(2):
             scatter(2, list4, gained2[h][:], h * HALF, HALF)
         last_d = interior_product(3, HALF, HALF)
@@ -514,7 +514,7 @@ def tile_list_matting_patch_weave_kernel(
             nc.vector.quantize_mx(
                 codes[:].bitcast(FP8X4), plane[:], woven[:, cols, :].rearrange("p c t -> p (c t)")
             )
-            result = placed([P, N // P, width], F32, f"result{k}", AT_TAB2 + 2 * ROW + WORD * (N // P) * cols.start)
+            result = placed([P, N // P, width], F32, f"result{k}", AT_TAB + WORD * T + WORD * (N // P) * cols.start)
             for n0 in range(0, N // P, HALF // width):
                 n1 = min(N // P, n0 + HALF // width)
                 acc = next_bank(f"acc{k}{n0}")

@@ -46,6 +46,7 @@ AT_CODES = 144 * KIB
 AT_SMALL = 152 * KIB
 AT_PAGE0 = 164 * KIB
 AT_EDGE = 172 * KIB
+AT_PICKED = 188 * KIB
 
 
 def tile_list_matting_patch_weave_kernel(
@@ -99,8 +100,7 @@ def tile_list_matting_patch_weave_kernel(
         tab2_rows = placed([P, T], U8, "tab2_rows", AT_RAW)
         nc.vector.memset(tab2_rows[0 : P - GROUP, :].bitcast(I32), 0)
         tab_rows = placed([P, T], U8, "tab_rows", AT_RAW + 2 * pass_bytes - T // 2)
-        nc.vector.memset(tab_rows[2 * QUAD : P, :].bitcast(I32), 0)
-        nc.vector.memset(tab_rows[QUAD : 2 * QUAD, :].bitcast(I32), 0)
+        nc.vector.memset(tab_rows[0 : P - 2 * GROUP, :].bitcast(I32), 0)
         wi_plane_raw = placed([P, H], U8, "wi_plane_raw", AT_SMALL + 8 * KIB)
         nc.gpsimd.memset(wi_plane_raw[:].bitcast(I32), 0)
         identity = keep.tile([P, P], F32, name="identity")
@@ -116,7 +116,7 @@ def tile_list_matting_patch_weave_kernel(
         nc.sync.dma_start(tab2_rows[P - GROUP : P, :].bitcast(I32), tab2_scales[0].bitcast(I32))
         list1 = load_list(offs, "list1")
         nc.sync.dma_start(
-            tab_rows[0:QUAD, :].bitcast(I32), tab_scales.bitcast(I32).rearrange("a r t -> r a t")
+            tab_rows[P - 2 * GROUP : P, :].bitcast(I32), tab_scales.bitcast(I32).rearrange("a r t -> r a t")
         )
         first_rows = placed([P, HALF], F32, "first_rows", AT_SMALL + 6 * KIB)
         nc.sync.dma_start(
@@ -154,7 +154,7 @@ def tile_list_matting_patch_weave_kernel(
         for q in range(P // QUAD):
             nc.sync.dma_start(
                 v_planes[QUAD * q : QUAD * q + LIVE, :].bitcast(I32).rearrange("p (a c) -> p a c", a=2),
-                v_rows[2 * LIVE * q : 2 * LIVE * (q + 1), :].bitcast(I32),
+                v_rows[P - 2 * GROUP + 2 * LIVE * q : P - 2 * GROUP + 2 * LIVE * (q + 1), :].bitcast(I32),
             )
 
         wi_codes = keep.tile([P, H], I32, name="wi_codes", align_bytes=64)
@@ -179,7 +179,7 @@ def tile_list_matting_patch_weave_kernel(
         first_gains = [placed([P, S], F32, f"gain2_{t}", AT_GAIN + ROW * t) for t in range(2)]
         at_gain2a = AT_GAIN + 2 * ROW
         at_wb_raw = at_gain2a + ROW
-        at_repeated = (AT_TAB, at_wb_raw + KIB, at_gain2a, AT_TAB + WORD * T)
+        at_repeated = (at_gain2a, AT_TAB, at_wb_raw + KIB, AT_TAB + WORD * T)
         for k in range(PACK):
             repeated = placed([P, PACK, P], F32, f"repeated{k}", at_repeated[k])
             nc.scalar.copy(
@@ -194,6 +194,7 @@ def tile_list_matting_patch_weave_kernel(
 
         slope_less_one = keep.tile([P, PACK], F32, name="slope_less_one")
         nc.scalar.activation(slope_less_one[:], slopes[:, 0 : PAIR * PACK - 1 : PAIR], ACT.Identity, bias=-1.0)
+        gain2 = [load_gain(wg2, 2, 0, HALF, "gain2_20", at_gain2a)]
         tab_windows = [load_words(tab_words[0], "tab_window0", AT_TAB)]
         wb_raw = placed([P, 2, 2 * H], U8, "wb_raw", at_wb_raw)
         nc.sync.dma_start(wb_raw[:].bitcast(I32), wb_words.bitcast(I32).rearrange("a p c -> p a c"))
@@ -204,7 +205,6 @@ def tile_list_matting_patch_weave_kernel(
                 wb_plane_raw[QUAD * q : QUAD * q + LIVE, :].bitcast(I32).rearrange("p (a c) -> p a c", a=2),
                 wb_scales[:, LIVE * q : LIVE * (q + 1), :].bitcast(I32).rearrange("a r c -> r a c"),
             )
-        gain2 = [load_gain(wg2, 2, 0, HALF, "gain2_20", at_gain2a)]
         tab_windows.append(load_words(tab_words[1], "tab_window1", AT_TAB + WORD * T))
 
         pages = [
@@ -301,7 +301,7 @@ def tile_list_matting_patch_weave_kernel(
         w_codes = [placed([P, 2 * H], U32, f"w_codes{w}", AT_CODES + ROW * w) for w in range(2)]
 
         def quantise_weight(w):
-            plane = placed([P, 2 * H], U8, f"w_plane{w}", (AT_SMALL + 10 * KIB, at_wb_raw)[w])
+            plane = placed([P, 2 * H], U8, f"w_plane{w}", (AT_VALUE + ROW + half_bytes, AT_TAB + 2 * ROW)[w])
             nc.vector.quantize_mx(
                 w_codes[w][:].bitcast(FP8X4), plane[:], grouped[w][:].rearrange("p a x -> p (a x)")
             )
@@ -310,7 +310,7 @@ def tile_list_matting_patch_weave_kernel(
         def gather_v(a):
             tiles = []
             for h in range(2):
-                tile = keep.tile([P, HALF], U32, name=f"v_codes{a}{h}", align_bytes=64)
+                tile = placed([P, HALF], U32, f"v_codes{a}{h}", AT_PICKED + ROW * a + half_bytes * h)
                 nc.vector.tensor_copy(tile[:], tab_windows[a][:].indirect(entries(list1, h * HALF, HALF)))
                 tiles.append(tile)
             return tiles

@@ -100,7 +100,6 @@ def tile_list_matting_patch_weave_kernel(
         tab2_rows = placed([P, T], U8, "tab2_rows", AT_RAW)
         nc.vector.memset(tab2_rows[0 : P - GROUP, :].bitcast(I32), 0)
         tab_rows = placed([P, T], U8, "tab_rows", AT_RAW + 2 * pass_bytes - T // 2)
-        nc.vector.memset(tab_rows[0 : P - 2 * GROUP, :].bitcast(I32), 0)
         wi_plane_raw = placed([P, H], U8, "wi_plane_raw", AT_SMALL + 8 * KIB)
         nc.gpsimd.memset(wi_plane_raw[:].bitcast(I32), 0)
         identity = keep.tile([P, P], F32, name="identity")
@@ -109,6 +108,7 @@ def tile_list_matting_patch_weave_kernel(
         nc.gpsimd.memset(v2_plane[:].bitcast(I32), 0)
         wi_rows = placed([LIVE, P // QUAD, H], U8, "wi_rows", AT_SMALL + 9 * KIB)
         nc.gpsimd.dma_start(wi_rows[:].bitcast(I32), wi_scales[0].bitcast(I32).rearrange("(q r) c -> r q c", r=LIVE))
+        nc.gpsimd.memset(tab_rows[0 : P - 2 * GROUP, :].bitcast(I32), 0)
         v_planes = keep.tile([P, 2 * S], U8, name="v_planes", align_bytes=64)
         nc.gpsimd.memset(v_planes[:].bitcast(I32), 0)
 

@@ -97,17 +97,15 @@ def tile_list_matting_patch_weave_kernel(
         def entries(lst, c0, width):
             return lst[:] if width == S else lst[:, c0 // GROUP : (c0 + width) // GROUP]
 
-        tab2_rows = placed([P, T], U8, "tab2_rows", AT_RAW)
+        tab2_rows = placed([P, T], U8, "tab2_rows", AT_RAW + pass_bytes - T // 2)
         nc.vector.memset(tab2_rows[0 : P - GROUP, :].bitcast(I32), 0)
-        tab_rows = placed([P, T], U8, "tab_rows", AT_RAW + 2 * pass_bytes - T // 2)
-        wi_plane_raw = placed([P, H], U8, "wi_plane_raw", AT_SMALL + 8 * KIB)
-        nc.gpsimd.memset(wi_plane_raw[:].bitcast(I32), 0)
+        tab_rows = placed([P, T], U8, "tab_rows", AT_RAW + 3 * pass_bytes - T // 2)
         identity = keep.tile([P, P], F32, name="identity")
         make_identity(nc, identity[:])
+        wi_plane_raw = placed([P, H], U8, "wi_plane_raw", AT_SMALL + 10 * KIB)
+        nc.gpsimd.memset(wi_plane_raw[:].bitcast(I32), 0)
         v2_plane = keep.tile([P, S], U8, name="v2_plane", align_bytes=64)
         nc.gpsimd.memset(v2_plane[:].bitcast(I32), 0)
-        wi_rows = placed([LIVE, P // QUAD, H], U8, "wi_rows", AT_SMALL + 9 * KIB)
-        nc.gpsimd.dma_start(wi_rows[:].bitcast(I32), wi_scales[0].bitcast(I32).rearrange("(q r) c -> r q c", r=LIVE))
         nc.gpsimd.memset(tab_rows[0 : P - 2 * GROUP, :].bitcast(I32), 0)
         v_planes = keep.tile([P, 2 * S], U8, name="v_planes", align_bytes=64)
         nc.gpsimd.memset(v_planes[:].bitcast(I32), 0)
@@ -118,6 +116,8 @@ def tile_list_matting_patch_weave_kernel(
         nc.sync.dma_start(
             tab_rows[P - 2 * GROUP : P, :].bitcast(I32), tab_scales.bitcast(I32).rearrange("a r t -> r a t")
         )
+        wi_rows = placed([LIVE, P // QUAD, H], U8, "wi_rows", AT_SMALL + 8 * KIB)
+        nc.sync.dma_start(wi_rows[:].bitcast(I32), wi_scales[0].bitcast(I32).rearrange("(q r) c -> r q c", r=LIVE))
         first_rows = placed([P, HALF], F32, "first_rows", AT_SMALL + 6 * KIB)
         nc.sync.dma_start(
             first_rows[:],
@@ -125,7 +125,7 @@ def tile_list_matting_patch_weave_kernel(
                 "u (x j) -> u x j", j=HALF
             ),
         )
-        wi_raw = placed([P, H], I32, "wi_raw", AT_RAW + 3 * pass_bytes + 2 * KIB)
+        wi_raw = placed([P, H], I32, "wi_raw", AT_PICKED)
         nc.sync.dma_start(wi_raw[:], wi_words[0].rearrange("p c i -> p (c i)").bitcast(I32))
         slopes = keep.tile([P, PAIR * PACK - 1], F32, name="slopes")
 
@@ -158,9 +158,9 @@ def tile_list_matting_patch_weave_kernel(
             )
 
         wi_codes = keep.tile([P, H], I32, name="wi_codes", align_bytes=64)
-        nc.vector.tensor_copy(
-            wi_codes[:].rearrange("p (t u e) -> p u t e", t=PACK, e=PAIR),
-            wi_raw[:].rearrange("p (u t e) -> p u t e", t=PACK, e=PAIR),
+        nc.scalar.copy(
+            wi_codes[:].bitcast(U32).rearrange("p (t u e) -> p u t e", t=PACK, e=PAIR),
+            wi_raw[:].bitcast(U32).rearrange("p (u t e) -> p u t e", t=PACK, e=PAIR),
         )
         for q in range(P // QUAD):
             nc.vector.tensor_copy(

from contextlib import ExitStack

import concourse.mybir as mybir
from concourse.masks import make_identity

K, K2, H, N, T, S, T2 = 1024, 512, 512, 384, 4096, 1024, 2048
FLOPS = 2 * (3 * K * H * S + K2 * H * S + H * N * T2)

F32 = mybir.dt.float32
BF16 = mybir.dt.bfloat16
I32 = mybir.dt.int32
U32 = mybir.dt.uint32
U16 = mybir.dt.uint16
U8 = mybir.dt.uint8
FP8X4 = mybir.dt.float8_e4m3fn_x4
FP4X4 = mybir.dt.float4_e2m1fn_x4
ALU = mybir.AluOpType
ACT = mybir.ActivationFunctionType

P = 128
PACK = 4
PAIR = 2
QUAD = 32
LIVE = 4
GROUP = 16
PASS = P * PACK
HALF = 512
QUARTER = 256
BANKS = 8
WORD = 4
KIB = 1024
ROW = WORD * S

PIECES = (128, 128, 256, 256, 256, 256, 256, 256, 256)
WEAVE_CHUNKS = (256, 256, 512, 512, 512)
PLACE = (0, 2, 3, 1)

AT_RAW = 0
AT_TAB2 = 32 * KIB
AT_TAB = 48 * KIB
AT_GAIN = 80 * KIB
AT_VALUE = 96 * KIB
AT_LIFT = 112 * KIB
AT_GROUPED = 128 * KIB
AT_CODES = 144 * KIB
AT_SMALL = 152 * KIB
AT_PAGE0 = 164 * KIB
AT_EDGE = 172 * KIB
AT_PICKED = 188 * KIB


def tile_list_matting_patch_weave_kernel(
    tc, tab_words, tab_scales, tab2_words, tab2_scales, offs, offs2, offs3, offs4, wf, wb_words, wb_scales,
    wm, wi_words, wi_scales, slope, wg1, wg2, wo, out,
):
    nc = tc.nc
    half_bytes = WORD * HALF
    pass_bytes = WORD * PACK * H

    with ExitStack() as ctx:
        lists = ctx.enter_context(tc.tile_pool(name="lists", bufs=1))
        keep = ctx.enter_context(tc.tile_pool(name="keep", bufs=1))
        big = ctx.enter_context(tc.tile_pool(name="big", bufs=1))
        psum = ctx.enter_context(tc.psum_pool(name="psum", bufs=1))

        def placed(shape, dtype, name, offset):
            return big.tile(shape, dtype, name=name, offset=offset, align_bytes=64)

        def bank(name, number):
            return psum.tile([P, HALF], F32, name=name, tag=f"bank{number}")

        def load_list(src, name):
            tile = lists.tile([P, S // GROUP], U16, name=name)
            nc.sync.dma_start(tile[:], src)
            return tile

        def load_gain(src, t, c0, width, name, offset):
            tile = placed([P, width], F32, name, offset)
            rows = src.rearrange("(u t e) j -> t u e j", t=PACK, e=PAIR)[t][:, :, c0 : c0 + width]
            for q in (0, 2, 1, 3):
                nc.sync.dma_start(tile[QUAD * q : QUAD * (q + 1), :], rows)
            return tile

        def load_pass(src, a, name, offset):
            tile = placed([P, PACK, H], F32, name, offset)
            nc.sync.dma_start(
                tile[:].rearrange("p i c -> p (i c)"),
                src[a * PASS : (a + 1) * PASS, :].rearrange("(p i) c -> p (i c)", i=PACK),
            )
            return tile

        def load_words(src, name, offset):
            tile = placed([P, T], U32, name, offset)
            nc.sync.dma_start(tile[:].bitcast(I32), src.rearrange("p t i -> p (t i)").bitcast(I32))
            return tile

        def entries(lst, c0, width):
            return lst[:] if width == S else lst[:, c0 // GROUP : (c0 + width) // GROUP]

        tab2_rows = placed([P, T], U8, "tab2_rows", AT_RAW + pass_bytes - T // 2)
        nc.vector.memset(tab2_rows[0 : P - GROUP, :].bitcast(I32), 0)
        tab_rows = placed([P, T], U8, "tab_rows", AT_RAW + 3 * pass_bytes - T // 2)
        identity = keep.tile([P, P], F32, name="identity")
        make_identity(nc, identity[:])
        wi_plane_raw = placed([P, H], U8, "wi_plane_raw", AT_SMALL + 10 * KIB)
        nc.gpsimd.memset(wi_plane_raw[:].bitcast(I32), 0)
        v2_plane = keep.tile([P, S], U8, name="v2_plane", align_bytes=64)
        nc.gpsimd.memset(v2_plane[:].bitcast(I32), 0)
        nc.gpsimd.memset(tab_rows[0 : P - 2 * GROUP, :].bitcast(I32), 0)
        v_planes = keep.tile([P, 2 * S], U8, name="v_planes", align_bytes=64)
        nc.gpsimd.memset(v_planes[:].bitcast(I32), 0)

        list2 = load_list(offs2, "list2")
        nc.sync.dma_start(tab2_rows[P - GROUP : P, :].bitcast(I32), tab2_scales[0].bitcast(I32))
        list1 = load_list(offs, "list1")
        nc.sync.dma_start(
            tab_rows[P - 2 * GROUP : P, :].bitcast(I32), tab_scales.bitcast(I32).rearrange("a r t -> r a t")
        )
        wi_rows = placed([LIVE, P // QUAD, H], U8, "wi_rows", AT_SMALL + 8 * KIB)
        nc.sync.dma_start(wi_rows[:].bitcast(I32), wi_scales[0].bitcast(I32).rearrange("(q r) c -> r q c", r=LIVE))
        first_rows = placed([P, HALF], F32, "first_rows", AT_SMALL + 6 * KIB)
        nc.sync.dma_start(
            first_rows[:],
            wg2.rearrange("(u f) j -> u (f j)", f=PACK * PAIR)[:, 0 : 2 * PAIR * S].rearrange(
                "u (x j) -> u x j", j=HALF
            ),
        )
        wi_raw = placed([P, H], I32, "wi_raw", AT_PICKED)
        nc.sync.dma_start(wi_raw[:], wi_words[0].rearrange("p c i -> p (c i)").bitcast(I32))
        slopes = keep.tile([P, PAIR * PACK - 1], F32, name="slopes")

        def load_slopes(e):
            nc.sync.dma_start(
                slopes[e:P:PAIR, :], slope.rearrange("(u x) -> u x", x=PACK * PAIR)[:, e : e + PAIR * PACK - 1]
            )

        load_slopes(0)
        list4 = load_list(offs4, "list4")
        tab2_window = load_words(tab2_words[0], "tab2_window", AT_TAB2)
        load_slopes(1)
        list3 = load_list(offs3, "list3")

        v2_rows = placed([P, S], U8, "v2_rows", AT_SMALL + 4 * KIB)
        nc.vector.tensor_copy(v2_rows[:], tab2_rows[:].indirect(list2[:]))
        for q in range(P // QUAD):
            nc.sync.dma_start(
                v2_plane[QUAD * q : QUAD * q + LIVE, :].bitcast(I32),
                v2_rows[P - GROUP + LIVE * q : P - GROUP + LIVE * (q + 1), :].bitcast(I32),
            )
        v_rows = placed([P, S], U8, "v_rows", AT_SMALL + 5 * KIB)
        nc.vector.tensor_copy(v_rows[:], tab_rows[:].indirect(list1[:]))
        wf_raw = [load_pass(wf, a, f"wf_raw{a}", AT_RAW + pass_bytes * a) for a in range(2)]
        wm_raw = [load_pass(wm, 0, "wm_raw0", AT_RAW + 2 * pass_bytes)]
        for q in range(P // QUAD):
            nc.sync.dma_start(
                v_planes[QUAD * q : QUAD * q + LIVE, :].bitcast(I32).rearrange("p (a c) -> p a c", a=2),
                v_rows[P - 2 * GROUP + 2 * LIVE * q : P - 2 * GROUP + 2 * LIVE * (q + 1), :].bitcast(I32),
            )

        wi_codes = keep.tile([P, H], I32, name="wi_codes", align_bytes=64)
        nc.scalar.copy(
            wi_codes[:].bitcast(U32).rearrange("p (t u e) -> p u t e", t=PACK, e=PAIR),
            wi_raw[:].bitcast(U32).rearrange("p (u t e) -> p u t e", t=PACK, e=PAIR),
        )
        for q in range(P // QUAD):
            nc.vector.tensor_copy(
                wi_plane_raw[QUAD * q : QUAD * q + LIVE, :].bitcast(I32), wi_rows[:, q, :].bitcast(I32)
            )
        wi_plane = keep.tile([P, H], U8, name="wi_plane", align_bytes=64)
        nc.vector.tensor_copy(
            wi_plane[:].bitcast(U16).rearrange("p (t u) -> p t u", t=PACK),
            wi_plane_raw[:].bitcast(U16).rearrange("p (u t) -> p t u", t=PACK),
        )
        wm_raw.append(load_pass(wm, 1, "wm_raw1", AT_RAW + 3 * pass_bytes))

        turned = bank("turned", 4)
        for c in range(PACK):
            nc.tensor.transpose(turned[:, c * P : (c + 1) * P], first_rows[:, c * P : (c + 1) * P], identity[:])
        first_gains = [placed([P, S], F32, f"gain2_{t}", AT_GAIN + ROW * t) for t in range(2)]
        at_gain2a = AT_GAIN + 2 * ROW
        at_wb_raw = at_gain2a + ROW
        at_repeated = (at_gain2a, AT_TAB, at_wb_raw + KIB, AT_TAB + WORD * T)
        for k in range(PACK):
            repeated = placed([P, PACK, P], F32, f"repeated{k}", at_repeated[k])
            nc.scalar.copy(
                repeated[:].rearrange("p c (q u e) -> p c q u e", e=PAIR, u=QUAD // PAIR),
                turned[:].rearrange("p (c u t e h) -> p t h c u e", c=PACK, t=2, e=PAIR, h=2)[:, k % 2, k // 2]
                .unsqueeze(2).to_broadcast([P, PACK, P // QUAD, QUAD // PAIR, PAIR]),
            )
            back_turned = bank(f"back_turned{k}", 5 + k % 3)
            for c in range(PACK):
                nc.tensor.transpose(back_turned[:, c * P : (c + 1) * P], repeated[:, c, :], identity[:])
            nc.scalar.copy(first_gains[k % 2][:, HALF * (k // 2) : HALF * (k // 2 + 1)], back_turned[:])

        slope_less_one = keep.tile([P, PACK], F32, name="slope_less_one")
        nc.scalar.activation(slope_less_one[:], slopes[:, 0 : PAIR * PACK - 1 : PAIR], ACT.Identity, bias=-1.0)
        gain2 = [load_gain(wg2, 2, 0, HALF, "gain2_20", at_gain2a)]
        tab_windows = [load_words(tab_words[0], "tab_window0", AT_TAB)]
        wb_raw = placed([P, 2, 2 * H], U8, "wb_raw", at_wb_raw)
        nc.sync.dma_start(wb_raw[:].bitcast(I32), wb_words.bitcast(I32).rearrange("a p c -> p a c"))
        wb_plane_raw = placed([P, 2 * H], U8, "wb_plane_raw", at_wb_raw + half_bytes)
        nc.gpsimd.memset(wb_plane_raw[:].bitcast(I32), 0)
        for q in range(P // QUAD):
            nc.sync.dma_start(
                wb_plane_raw[QUAD * q : QUAD * q + LIVE, :].bitcast(I32).rearrange("p (a c) -> p a c", a=2),
                wb_scales[:, LIVE * q : LIVE * (q + 1), :].bitcast(I32).rearrange("a r c -> r a c"),
            )
        tab_windows.append(load_words(tab_words[1], "tab_window1", AT_TAB + WORD * T))

        pages = [
            placed([P, T2], F32, "page0", AT_PAGE0),
            keep.tile([P, T2], F32, name="page1"),
        ]

        def scatter(t, lst, value, c0, width):
            nc.vector.tensor_copy(pages[t][:].indirect(entries(lst, c0, width)), value)

        v2_codes = {}

        def gather_v2(c0, width):
            tile = placed([P, width], U32, f"v2_codes{c0}", AT_SMALL + WORD * c0)
            nc.vector.tensor_copy(tile[:], tab2_window[:].indirect(entries(list2, c0, width)))
            for x in range(0, width, QUARTER):
                v2_codes[c0 + x] = tile[:, x : x + QUARTER]

        interior_banks = []

        def interior_product(t, c0, width):
            cols_w = slice(t * P, (t + 1) * P)
            interior_banks.append(t)
            d = bank(f"d{t}_{c0}", (len(interior_banks) - 1) % PACK)[:, 0:width]
            for x in range(0, width, QUARTER):
                nc.tensor.matmul_mx(
                    d[:, x : x + QUARTER], lhsT=wi_codes[:, cols_w].bitcast(FP8X4), lhsT_scale=wi_plane[:, cols_w],
                    rhs=v2_codes[c0 + x].bitcast(FP8X4),
                    rhs_scale=v2_plane[:, c0 + x : c0 + x + QUARTER], start=True, stop=True,
                )
            return d

        values2 = [placed([P, S], F32, f"value2_{t}", AT_VALUE + ROW * t) for t in range(PACK)]
        lifts = [placed([P, S], F32, f"lift{t}", AT_LIFT + ROW * t) for t in range(PACK)]

        def interior_terms(t, c0, width):
            cols = slice(c0, c0 + width)
            d = interior_product(t, c0, width)
            nc.scalar.activation(lifts[t][:, cols], d, ACT.Relu, scale=slope_less_one[:, t : t + 1])
            nc.scalar.copy(values2[t][:, cols], d)

        at_slot = AT_EDGE + ROW - KIB

        def interior_piece(t, c0, width, gain):
            cols = slice(c0, c0 + width)
            interior_terms(t, c0, width)
            leaky = placed([P, width], F32, f"leaky{t}_{c0}", at_slot)
            nc.gpsimd.tensor_tensor(leaky[:], values2[t][:, cols], lifts[t][:, cols], ALU.add)
            nc.gpsimd.tensor_tensor(values2[t][:, cols], leaky[:], gain, ALU.mult)
            scatter(t, list4, values2[t][:, cols], c0, width)

        def interior_sum(t, c0, width, offset):
            cols = slice(c0, c0 + width)
            for x in range(c0, c0 + width, HALF):
                interior_terms(t, x, HALF)
            leaky = placed([P, width], F32, f"leaky{t}_{c0}", offset)
            nc.gpsimd.tensor_tensor(leaky[:], values2[t][:, cols], lifts[t][:, cols], ALU.add)
            return leaky

        gather_v2(0, QUARTER)
        gather_v2(QUARTER, QUARTER)
        gather_v2(HALF, HALF)
        first_sums = []
        for c0 in (0, QUARTER):
            d = interior_product(0, c0, QUARTER)
            lift = lifts[0][:, c0 : c0 + QUARTER]
            nc.scalar.activation(lift, d, ACT.Relu, scale=slope_less_one[:, 0:1])
            leaky = placed([P, QUARTER], F32, f"first_leaky{c0}", at_slot + WORD * c0)
            nc.vector.tensor_tensor(leaky[:], d, lift, ALU.add)
            first_sums.append(leaky)
        for c0, leaky in zip((0, QUARTER), first_sums):
            cols = slice(c0, c0 + QUARTER)
            nc.gpsimd.tensor_tensor(values2[0][:, cols], leaky[:], first_gains[0][:, cols], ALU.mult)
            scatter(0, list4, values2[0][:, cols], c0, QUARTER)
        interior_piece(1, 0, HALF, first_gains[1][:, 0:HALF])
        interior_piece(0, HALF, HALF, first_gains[0][:, HALF:S])
        gain2.append(load_gain(wg2, 2, HALF, HALF, "gain2_21", AT_TAB2 + 2 * ROW))
        gain3 = load_gain(wg2, 3, 0, S, "gain2_3", AT_TAB2)

        grouped = [placed([P, 2, PACK * H], BF16, f"grouped{w}", AT_GROUPED + pass_bytes * w) for w in range(2)]

        def round_wf(a):
            rounded = grouped[0][:, a, :].rearrange("p (t u e i) -> p t u i e", t=PACK, e=PAIR, i=PACK)
            loaded = wf_raw[a][:].rearrange("p i (u t e) -> p t u i e", t=PACK, e=PAIR)
            for t in range(PACK):
                nc.scalar.activation(rounded[:, t], loaded[:, t], ACT.Copy, scale=-1.0)

        def round_wm(a):
            nc.scalar.copy(
                grouped[1][:, a, :].rearrange("p (t u e i) -> p u t i e", t=PACK, e=PAIR, i=PACK),
                wm_raw[a][:].rearrange("p i (u t e) -> p u t i e", t=PACK, e=PAIR),
            )

        w_codes = [placed([P, 2 * H], U32, f"w_codes{w}", AT_CODES + ROW * w) for w in range(2)]

        def quantise_weight(w):
            plane = placed([P, 2 * H], U8, f"w_plane{w}", (AT_VALUE + ROW + half_bytes, AT_TAB + 2 * ROW)[w])
            nc.vector.quantize_mx(
                w_codes[w][:].bitcast(FP8X4), plane[:], grouped[w][:].rearrange("p a x -> p (a x)")
            )
            return plane

        def gather_v(a):
            tiles = []
            for h in range(2):
                tile = placed([P, HALF], U32, f"v_codes{a}{h}", AT_PICKED + ROW * a + half_bytes * h)
                nc.vector.tensor_copy(tile[:], tab_windows[a][:].indirect(entries(list1, h * HALF, HALF)))
                tiles.append(tile)
            return tiles

        round_wf(0)
        interior_piece(1, HALF, HALF, first_gains[1][:, HALF:S])
        round_wf(1)
        w_planes = [quantise_weight(0)]
        leaky2 = interior_sum(2, 0, S, AT_EDGE)
        leaky3 = [interior_sum(3, 0, HALF, AT_EDGE + ROW)]
        gained2 = [placed([P, HALF], F32, "gained2_0", AT_GROUPED + ROW)]
        nc.gpsimd.tensor_tensor(gained2[0][:], leaky2[:, 0:HALF], gain2[0][:], ALU.mult)
        v_codes = [gather_v(0)]
        round_wm(0)
        round_wm(1)
        wb_codes = keep.tile([P, 2, 2 * H], U8, name="wb_codes", align_bytes=64)
        nc.scalar.copy(
            wb_codes[:].bitcast(U32).rearrange("p a (t u) -> p a u t", t=PACK),
            wb_raw[:].bitcast(U32).rearrange("p a (u t) -> p a u t", t=PACK),
        )
        w_planes.append(quantise_weight(1))
        v_codes.append(gather_v(1))
        wb_plane = keep.tile([P, 2 * H], U8, name="wb_plane", align_bytes=64)
        nc.scalar.copy(
            wb_plane[:].bitcast(U16).rearrange("p (a t u) -> p a t u", a=2, t=PACK),
            wb_plane_raw[:].bitcast(U16).rearrange("p (a u t) -> p a t u", a=2, t=PACK),
        )

        gained2.append(placed([P, HALF], F32, "gained2_1", AT_GROUPED + pass_bytes + ROW))
        nc.gpsimd.tensor_tensor(gained2[1][:], leaky2[:, HALF:S], gain2[1][:], ALU.mult)
        pages.extend(placed([P, T2], F32, f"page{t}", AT_TAB2 + 2 * ROW + WORD * T2 * (t - 2)) for t in (2, 3))
        for h in range(2):
            scatter(2, list4, gained2[h][:], h * HALF, HALF)
        last_d = interior_product(3, HALF, HALF)
        last_lift = placed([P, HALF], F32, "last_lift", AT_RAW + 3 * pass_bytes)
        nc.scalar.activation(last_lift[:], last_d, ACT.Relu, scale=slope_less_one[:, 3:4])
        last_value = placed([P, HALF], F32, "last_value", AT_RAW + 3 * pass_bytes + half_bytes)
        nc.scalar.copy(last_value[:], last_d)
        leaky3.append(placed([P, HALF], F32, "last_leaky", AT_GROUPED + ROW + half_bytes))
        nc.gpsimd.tensor_tensor(leaky3[1][:], last_value[:], last_lift[:], ALU.add)
        gained3 = placed([P, S], F32, "gained3", AT_TAB2 + ROW)
        for h in range(2):
            cols = slice(h * HALF, (h + 1) * HALF)
            nc.gpsimd.tensor_tensor(gained3[:, cols], leaky3[h][:], gain3[:, cols], ALU.mult)
        scatter(3, list4, gained3[:], 0, S)

        gains1 = [load_gain(wg1, 0, 0, S, "gain1_0", AT_GAIN)]
        wo_raw = placed([P, PACK, N], F32, "wo_raw", AT_LIFT + 2 * KIB)
        for t in range(PACK):
            nc.sync.dma_start(wo_raw[:, PLACE[t], :], wo.rearrange("(u t e) n -> t u e n", t=PACK, e=PAIR)[t])
        gains1.append(load_gain(wg1, 1, 0, S, "gain1_1", AT_GAIN + ROW))
        gains1.extend(load_gain(wg1, t, 0, S, f"gain1_{t}", AT_LIFT + ROW * t) for t in (2, 3))

        turns = []

        def next_bank(name):
            turns.append(name)
            return bank(name, (len(turns) - 1) % BANKS)

        def product(name, t, h, weights):
            acc = next_bank(name)
            steps = [(weight, a) for a in range(2) for weight in weights]
            for number, (weight, a) in enumerate(steps):
                cols_a = slice(a * H + t * P, a * H + (t + 1) * P)
                if weight == "b":
                    codes, plane = wb_codes[:, a, 2 * t * P : 2 * (t + 1) * P].bitcast(FP4X4), wb_plane[:, cols_a]
                else:
                    w = ("f", "m").index(weight)
                    codes, plane = w_codes[w][:, cols_a].bitcast(FP8X4), w_planes[w][:, cols_a]
                nc.tensor.matmul_mx(
                    acc[:], lhsT=codes, lhsT_scale=plane, rhs=v_codes[a][h][:].bitcast(FP8X4),
                    rhs_scale=v_planes[:, a * S + h * HALF : a * S + (h + 1) * HALF],
                    start=(number == 0), stop=(number == len(steps) - 1),
                )
            return acc

        blocks = [slice(c * P, (c + 1) * P) for c in range(PACK)]

        def turn_sum(unit):
            value, back, matte = unit_tiles(unit)
            summed = next_bank(f"summed{unit}")
            for block in blocks:
                for number, term in enumerate((value, back)):
                    nc.tensor.matmul(
                        summed[:, block], lhsT=term[:, block], rhs=identity[:], is_transpose=True,
                        start=(number == 0), stop=(number == 1),
                    )
            turned_sum = placed([P, HALF], F32, f"turned_sum{unit}", AT_VALUE + half_bytes * (unit % 2))
            nc.scalar.copy(turned_sum[:], summed[:])
            return turned_sum

        def turn_back(unit, turned_sum):
            upright = next_bank(f"upright{unit}")
            for block in blocks:
                nc.tensor.transpose(upright[:, block], turned_sum[:, block], identity[:])
            nc.scalar.copy(unit_tiles(unit)[0], upright[:])

        def blend(t, values1, mattes, backs, c0, width):
            cols = slice(c0, c0 + width)
            value, back, matte = values1[:, cols], backs[:, cols], mattes[:, cols]
            work = placed([P, width], F32, f"work{t}_{c0}", AT_TAB2 + WORD * c0)
            if t < PACK - 1:
                nc.gpsimd.tensor_tensor(work[:], value, matte, ALU.mult)
                nc.gpsimd.tensor_tensor(work[:], back, work[:], ALU.subtract)
                nc.gpsimd.tensor_tensor(value, work[:], gains1[t][:, cols], ALU.mult)
            else:
                nc.gpsimd.tensor_tensor(work[:], value, back, ALU.add)
                nc.gpsimd.tensor_tensor(work[:], work[:], matte, ALU.mult)
                nc.gpsimd.tensor_tensor(value, back, work[:], ALU.subtract)

        slices = []
        for t in range(PACK):
            region = AT_RAW + 2 * ROW * t if t < 2 else AT_EDGE + 2 * ROW * (t - 2)
            slices.append((
                placed([P, S], F32, f"value1_{t}", region),
                placed([P, S], F32, f"back{t}", region + ROW),
                placed([P, S], F32, f"matte{t}", AT_RAW + 2 * pass_bytes + ROW * t),
            ))

        def unit_tiles(unit):
            return [tile[:, (unit % 2) * HALF : (unit % 2 + 1) * HALF] for tile in slices[unit // 2]]

        def matte_of(unit):
            mt = product(f"mt{unit}", unit // 2, unit % 2, "m")
            nc.scalar.activation(unit_tiles(unit)[2], mt[:], ACT.Sigmoid)

        def terms_of(unit, first):
            value, back, matte = unit_tiles(unit)
            nc.scalar.copy(value, product(f"diff{unit}", unit // 2, unit % 2, first)[:])
            nc.scalar.copy(back, product(f"bg{unit}", unit // 2, unit % 2, "b")[:])

        def finish(t):
            values1, backs, mattes = slices[t]
            if t > 0:
                blend(t, values1, mattes, backs, 0, S)
            if t < PACK - 1:
                scatter(t, list3, values1[:], 0, S)
            else:
                nc.vector.tensor_tensor(pages[t][:].indirect(list3[:]), values1[:], gains1[t][:], ALU.mult)

        for unit in (0, 1):
            matte_of(unit)
            terms_of(unit, "fb")
            blend(0, slices[0][0], slices[0][2], slices[0][1], unit * HALF, HALF)
        finish(0)
        terms_of(2, "f")
        matte_of(3)
        terms_of(3, "fb")
        turned2 = turn_sum(2)
        matte_of(2)
        turn_back(2, turned2)
        finish(1)
        terms_of(4, "f")
        terms_of(5, "f")
        turned4 = turn_sum(4)
        matte_of(4)
        turned5 = turn_sum(5)
        turn_back(4, turned4)
        matte_of(5)
        turn_back(5, turned5)
        finish(2)
        for unit in (6, 7):
            for back_step in range(3):
                turns.pop()
            matte_of(unit)
            terms_of(unit, "f")
        finish(3)
        values1 = slices[3][0]

        def round_wo(n0, n1, offset):
            tile = placed([P, PACK * (n1 - n0)], BF16, f"wo_grouped{n0}", offset)
            nc.scalar.copy(
                tile[:].rearrange("p (c n i) -> p c i n", n=4, i=PACK),
                wo_raw[:, :, n0:n1].rearrange("p i (c n) -> p c i n", n=4),
            )
            return tile

        wo_grouped = [round_wo(0, 2 * P, AT_VALUE + 2 * ROW)]
        woven = placed([P, T2, PACK], BF16, "woven", AT_GROUPED + pass_bytes)
        nc.scalar.copy(woven[:, :, PLACE[0]], pages[0][:])
        wo_grouped.append(round_wo(2 * P, N, AT_PAGE0))
        nc.scalar.copy(woven[:, :, PLACE[1]], pages[1][:])
        for i, width in enumerate(WEAVE_CHUNKS):
            cols = slice(sum(WEAVE_CHUNKS[:i]), sum(WEAVE_CHUNKS[: i + 1]))
            nc.scalar.copy(woven[:, cols, PLACE[2]], pages[2][:, cols])
        wo_codes = keep.tile([P, N], U32, name="wo_codes", align_bytes=64)
        wo_plane = placed([P, N], U8, "wo_plane", AT_EDGE + 2 * ROW)

        def quantise_wo(n0, n1, rounded):
            nc.vector.quantize_mx(wo_codes[:, n0:n1].bitcast(FP8X4), wo_plane[:, n0:n1], rounded[:])

        out_rows = out.rearrange("(n p) c -> p n c", p=P)
        quantise_wo(2 * P, N, wo_grouped[1])
        for k, width in enumerate(PIECES):
            cols = slice(sum(PIECES[:k]), sum(PIECES[: k + 1]))
            nc.vector.tensor_copy(woven[:, cols, PLACE[3]], pages[3][:, cols])
            if k == 0:
                quantise_wo(0, 2 * P, wo_grouped[0])
            codes = keep.tile([P, width], U32, name=f"page_codes{k}", align_bytes=64)
            plane = keep.tile([P, width], U8, name=f"page_plane{k}", align_bytes=64)
            nc.vector.quantize_mx(
                codes[:].bitcast(FP8X4), plane[:], woven[:, cols, :].rearrange("p c t -> p (c t)")
            )
            result = placed([P, N // P, width], F32, f"result{k}", AT_TAB + WORD * T + WORD * (N // P) * cols.start)
            for n0 in range(0, N // P, HALF // width):
                n1 = min(N // P, n0 + HALF // width)
                acc = next_bank(f"acc{k}{n0}")
                for n in range(n0, n1):
                    rows = slice(n * P, (n + 1) * P)
                    nc.tensor.matmul_mx(
                        acc[:, (n - n0) * width : (n - n0 + 1) * width],
                        lhsT=wo_codes[:, rows].bitcast(FP8X4), lhsT_scale=wo_plane[:, rows],
                        rhs=codes[:].bitcast(FP8X4), rhs_scale=plane[:], start=True, stop=True,
                    )
                emptied = result[:, n0:n1, :].rearrange("p n c -> p (n c)")
                if n0 == 0 and k == len(PIECES) - 1:
                    nc.vector.tensor_copy(emptied, acc[:, 0 : (n1 - n0) * width])
                else:
                    nc.scalar.copy(emptied, acc[:, 0 : (n1 - n0) * width])
            nc.sync.dma_start(out_rows[:, :, cols], result[:])
